import numpy as np
import ml_dtypes


def mxq(x, axis, fmt="e4m3"):
    dtype, down = {"e4m3": (ml_dtypes.float8_e4m3fn, 7), "e5m2": (ml_dtypes.float8_e5m2, 14)}[fmt]
    v = np.moveaxis(np.asarray(x, np.float32).astype(ml_dtypes.bfloat16).astype(np.float64), axis, -1)
    blocks = v.reshape(v.shape[:-1] + (-1, 32))
    amax = np.abs(blocks).max(-1, keepdims=True)
    byte = np.maximum(np.where(amax > 0, np.frexp(amax)[1] - 1 + 127, 0) - down, 1)
    scale = np.exp2(byte - 127.0)
    codes = (blocks / scale).astype(np.float32).astype(dtype).astype(np.float64)
    return np.moveaxis((codes * scale).reshape(v.shape), -1, axis)


WIDE = False


def mx_kscale(k):
    if not WIDE:
        return np.ones(k)
    levels = np.array([10, -10, 5, -5, 0])
    if k % 512:
        return np.exp2(np.random.permutation(np.resize(levels, k // 32))).repeat(32)
    a = np.empty((k // 512, 16))
    for p in range(k // 512):
        a[p, :8] = np.random.permutation(np.resize(levels, 8))
        for g in range(8):
            far = levels[np.abs(levels - a[p, g]) >= 10]
            a[p, g + 8] = far[np.random.randint(len(far))]
    return np.exp2(a.ravel()).repeat(32)


def f64(x):
    return np.asarray(x).astype(np.float64)


def striped(idx):
    return np.tile(idx.reshape(-1, 16).T, (8, 1)).astype(np.uint16)


def unstriped(offs):
    return offs[:16].T.reshape(-1).astype(np.int64)


def striped8(idx):
    return np.concatenate([x.reshape(-1, 16).T for x in idx]).astype(np.uint16)


def runs(offs, k):
    lists = np.stack([offs[16 * r : 16 * r + 16].T.reshape(-1) for r in range(8)]).astype(np.int64)
    return lists[np.arange(k) % 512 // 64]


def pack_weight(w):
    k, n = w.shape
    w = f64(np.asarray(w, np.float32).astype(ml_dtypes.bfloat16)).reshape(k // 32, 32, n)
    amax = np.abs(w).max(1)
    byte = np.clip(np.where(amax > 0, np.frexp(amax)[1] - 1 + 127 - 7, 1), 1, 254)
    scaled = (w * np.exp2(127.0 - byte)[:, None, :]).reshape(k, n).astype(np.float32)
    words = np.ascontiguousarray(scaled.reshape(k // 512, 128, 4, n).transpose(0, 1, 3, 2)).astype(ml_dtypes.float8_e4m3fn).view(np.uint8)
    return words, np.ascontiguousarray(byte.astype(np.uint8).reshape(k // 512, 16, n))


def unpack_weight(words, scales):
    g, p, n, _ = words.shape
    vals = np.ascontiguousarray(words).view(ml_dtypes.float8_e4m3fn).astype(np.float64) * np.repeat(np.exp2(scales.astype(np.float64) - 127.0), 8, axis=1)[..., None]
    return vals.transpose(0, 1, 3, 2).reshape(g * 512, n)

def planes(y):
    n, m = y.shape
    v = y.astype(np.float32).astype(ml_dtypes.bfloat16).astype(np.float64).reshape(n // 32, 32, m)
    top = np.abs(v).max(1)
    byte = np.clip(np.where(top > 0, np.frexp(top)[1] - 1 + 127 - 7, 1), 1, 254)
    codes = (v * np.exp2(127.0 - byte)[:, None, :]).reshape(n, m).astype(np.float32).astype(ml_dtypes.float8_e4m3fn).view(np.uint8)
    words = codes.reshape(n // 512, 128, 4, m).transpose(0, 1, 3, 2)
    return np.ascontiguousarray(words), np.ascontiguousarray(byte.astype(np.uint8).reshape(n // 512, 16, m))


K, T, S, N = 512, 2048, 512, 512
P = 2 ** 7


def setup_inputs():
    n = np.random.standard_normal
    s = mx_kscale(K)[:, None]
    packed_xT = pack_weight(n((K, T)) * s)
    return {
        "x_words": packed_xT[0],
        "x_scales": packed_xT[1],
        "w1": (n((K, N)) / np.sqrt(K) / s).astype(np.float32),
        "w2": (n((K, N)) / np.sqrt(K) / s).astype(np.float32),
        "rw": np.tile(np.random.standard_normal(S), (P, 1)).astype(np.float32),
        "offs": striped(np.random.permutation(T)[:S]),
        "nx": striped8(np.random.randint(0, S, (8, S))),
        "cur": striped8(np.random.randint(0, S, (8, S))),
    }


def reference(x_words, x_scales, w1, w2, rw, offs, nx, cur):
    xq = unpack_weight(x_words, x_scales)[:, unstriped(offs)]
    y = mxq(f64(w1), 0, "e4m3").T @ xq
    e = mxq(f64(w2), 0, "e4m3").T @ xq
    out_0 = f64(rw)[:1] + 0.9 * (np.minimum(y[np.arange(N)[:, None], runs(nx, N)], e[np.arange(N)[:, None], runs(nx, N)])) - (y[np.arange(N)[:, None], runs(cur, N)])
    return (out_0,) + planes(out_0)

@@ -1,0 +1,157 @@
+from contextlib import ExitStack
+
+import concourse.mybir as mybir
+
+K, T, S, N = 512, 2048, 512, 512
+P = 128
+PACK = 4
+FLOPS = 2 * 2 * K * N * S
+
+F32 = mybir.dt.float32
+BF16 = mybir.dt.bfloat16
+I32 = mybir.dt.int32
+U32 = mybir.dt.uint32
+U16 = mybir.dt.uint16
+U8 = mybir.dt.uint8
+FP8X4 = mybir.dt.float8_e4m3fn_x4
+ALU = mybir.AluOpType
+COPY = mybir.ActivationFunctionType.Copy
+
+DISCOUNT = 0.9
+W_CHUNK = 128
+HALF = 256
+OUT_CHUNKS = ((0, 256), (256, 128), (384, 128))
+
+
+def tile_picked_redq_none_po_kernel(
+    tc, x_words, x_scales, w1, w2, rw, offs, nx, cur, out_0, out_1, out_2
+):
+    nc = tc.nc
+    with ExitStack() as ctx:
+        keep = ctx.enter_context(tc.tile_pool(name="keep", bufs=1))
+        psum = ctx.enter_context(tc.psum_pool(name="psum", bufs=1))
+
+        offs_sb = keep.tile([P, S // 16], U16, name="offs_sb")
+        cur_sb = keep.tile([P, S // 16], U16, name="cur_sb")
+        nx_sb = keep.tile([P, S // 16], U16, name="nx_sb")
+        xw = keep.tile([P, T], I32, name="xw", align_bytes=64)
+        xs = keep.tile([P, T], U8, name="xs", align_bytes=64)
+        rw_sb = keep.tile([P, S], F32, name="rw_sb")
+
+        nc.vector.memset(xs[:].bitcast(I32), 0)
+        nc.sync.dma_start(offs_sb[:], offs)
+        nc.sync.dma_start(xw[:], x_words[0].rearrange("p n t -> p (n t)").bitcast(I32))
+        for q in range(4):
+            nc.scalar.dma_start(
+                xs[32 * q : 32 * q + 4, :].bitcast(I32), x_scales[0, 4 * q : 4 * q + 4, :].bitcast(I32)
+            )
+
+        def load_weight(w, name):
+            rows = w.rearrange("(p j) c -> p j c", j=PACK)
+            chunks = []
+            for a in range(N // W_CHUNK):
+                raw = keep.tile([P, PACK, W_CHUNK], F32, name=f"{name}_raw{a}")
+                nc.sync.dma_start(raw[:], rows[:, :, a * W_CHUNK : (a + 1) * W_CHUNK])
+                chunks.append(raw)
+            return chunks
+
+        w1_raw = load_weight(w1, "w1")
+        nc.sync.dma_start(cur_sb[:], cur)
+        nc.sync.dma_start(rw_sb[:], rw)
+        w2_raw = load_weight(w2, "w2")
+        nc.sync.dma_start(nx_sb[:], nx)
+
+        xq_s = keep.tile([P, S], U8, name="xq_s", align_bytes=64)
+        xq_w = keep.tile([P, S], U32, name="xq_w", align_bytes=64)
+        nc.vector.tensor_copy(xq_s[:], xs[:].indirect(offs_sb[:]))
+        nc.vector.tensor_copy(xq_w[:], xw[:].bitcast(U32).indirect(offs_sb[:]))
+
+        def round_chunk(grouped, raw, a):
+            m = W_CHUNK // PACK
+            dst = grouped[:].rearrange("p (t m j) -> p m t j", t=PACK, j=PACK)[:, a * m : (a + 1) * m]
+            src = raw[:].rearrange("p j (m t) -> p m t j", t=PACK)
+            nc.scalar.activation(dst, src, COPY)
+
+        def quantize_weight(grouped, name):
+            codes = keep.tile([P, N], U32, name=f"{name}_codes", align_bytes=64)
+            scales = keep.tile([P, N], U8, name=f"{name}_scales", align_bytes=64)
+            nc.vector.quantize_mx(out=codes[:].bitcast(FP8X4), scales=scales[:], in_=grouped[:])
+            return codes, scales
+
+        def product(codes, scales, t, name):
+            acc = psum.tile([P, S], F32, name=f"{name}{t}")
+            cols = slice(t * P, (t + 1) * P)
+            nc.tensor.matmul_mx(
+                out=acc[:],
+                lhsT=codes[:, cols].bitcast(FP8X4),
+                lhsT_scale=scales[:, cols],
+                rhs=xq_w[:].bitcast(FP8X4),
+                rhs_scale=xq_s[:],
+                start=True,
+                stop=True,
+            )
+            return acc
+
+        w1_bf = keep.tile([P, PACK * N], BF16, name="w1_bf", align_bytes=64)
+        w2_bf = keep.tile([P, PACK * N], BF16, name="w2_bf", align_bytes=64)
+        for a in range(N // W_CHUNK):
+            round_chunk(w1_bf, w1_raw[a], a)
+        w1_codes, w1_scales = quantize_weight(w1_bf, "w1")
+        y = [product(w1_codes, w1_scales, t, "y") for t in range(PACK)]
+
+        base = keep.tile([P, PACK, S], F32, name="base")
+        for t in range(PACK):
+            y_neg = keep.tile([P, S], F32, name=f"y_neg{t}")
+            nc.scalar.activation(y_neg[:], y[t][:], COPY, scale=-1.0)
+            round_chunk(w2_bf, w2_raw[t], t)
+            for h in range(S // HALF):
+                cols = slice(h * HALF, (h + 1) * HALF)
+                nc.vector.tensor_tensor(
+                    base[:, t, cols],
+                    y_neg[:].indirect(cur_sb[:, h * HALF // 16 : (h + 1) * HALF // 16]),
+                    rw_sb[:, cols],
+                    ALU.add,
+                )
+
+        w2_codes, w2_scales = quantize_weight(w2_bf, "w2")
+        e = [product(w2_codes, w2_scales, t, "e") for t in range(PACK)]
+
+        low = []
+        for t in range(PACK):
+            y_disc = keep.tile([P, S], F32, name=f"y_disc{t}")
+            nc.scalar.activation(y_disc[:], y[t][:], COPY, scale=DISCOUNT)
+            low_t = keep.tile([P, S], F32, name=f"low{t}")
+            nc.vector.scalar_tensor_tensor(low_t[:], e[t][:], DISCOUNT, y_disc[:], ALU.mult, ALU.min)
+            low.append(low_t)
+
+        out_rows = out_0.rearrange("(p t) j -> p t j", t=PACK)
+        out_words = out_1[0].rearrange("p n t -> p (n t)").bitcast(I32)
+        o_scales = keep.tile([P, S], U8, name="o_scales", align_bytes=64)
+        for c0, width in OUT_CHUNKS:
+            cols = slice(c0, c0 + width)
+            td = keep.tile([P, PACK, width], F32, name=f"td{c0}")
+            for t in range(PACK):
+                nc.vector.tensor_tensor(
+                    td[:, t, :],
+                    low[t][:].indirect(nx_sb[:, c0 // 16 : (c0 + width) // 16]),
+                    base[:, t, cols],
+                    ALU.add,
+                )
+            nc.sync.dma_start(out_rows[:, :, cols], td[:])
+            td_bf = keep.tile([P, width, PACK], BF16, name=f"td_bf{c0}", align_bytes=64)
+            if c0 + width == S:
+                nc.vector.tensor_copy(td_bf[:], td[:].rearrange("p t j -> p j t"))
+            else:
+                nc.scalar.copy(td_bf[:], td[:].rearrange("p t j -> p j t"))
+            o_codes = keep.tile([P, width], I32, name=f"o_codes{c0}", align_bytes=64)
+            nc.vector.quantize_mx(
+                out=o_codes[:].bitcast(FP8X4),
+                scales=o_scales[:, cols],
+                in_=td_bf[:].rearrange("p j t -> p (j t)"),
+            )
+            nc.sync.dma_start(out_words[:, cols], o_codes[:])
+        for q in range(4):
+            queue = nc.scalar if q % 2 else nc.sync
+            queue.dma_start(
+                out_2[0, 4 * q : 4 * q + 4, :].bitcast(I32), o_scales[32 * q : 32 * q + 4, :].bitcast(I32)
+            )

@@ -18,7 +18,7 @@ ALU = mybir.AluOpType
 COPY = mybir.ActivationFunctionType.Copy
 
 DISCOUNT = 0.9
-W_CHUNK = 128
+W1_SPLIT = 52
 HALF = 256
 OUT_CHUNKS = ((0, 256), (256, 128), (384, 128))
 
@@ -38,39 +38,30 @@ def tile_picked_redq_none_po_kernel(
         xs = keep.tile([P, T], U8, name="xs", align_bytes=64)
         rw_sb = keep.tile([P, S], F32, name="rw_sb")
 
+        def load_weight(w, name):
+            raw = keep.tile([P, PACK, N], F32, name=name, tag="w_raw")
+            nc.sync.dma_start(raw[:], w.rearrange("(p j) c -> p j c", j=PACK))
+            return raw
+
         nc.vector.memset(xs[:].bitcast(I32), 0)
+        w1_raw = load_weight(w1, "w1_raw")
         nc.sync.dma_start(offs_sb[:], offs)
-        nc.sync.dma_start(xw[:], x_words[0].rearrange("p n t -> p (n t)").bitcast(I32))
         for q in range(4):
-            nc.scalar.dma_start(
+            nc.sync.dma_start(
                 xs[32 * q : 32 * q + 4, :].bitcast(I32), x_scales[0, 4 * q : 4 * q + 4, :].bitcast(I32)
             )
-
-        def load_weight(w, name):
-            rows = w.rearrange("(p j) c -> p j c", j=PACK)
-            chunks = []
-            for a in range(N // W_CHUNK):
-                raw = keep.tile([P, PACK, W_CHUNK], F32, name=f"{name}_raw{a}")
-                nc.sync.dma_start(raw[:], rows[:, :, a * W_CHUNK : (a + 1) * W_CHUNK])
-                chunks.append(raw)
-            return chunks
-
-        w1_raw = load_weight(w1, "w1")
+        nc.sync.dma_start(xw[:], x_words[0].rearrange("p n t -> p (n t)").bitcast(I32))
         nc.sync.dma_start(cur_sb[:], cur)
         nc.sync.dma_start(rw_sb[:], rw)
-        w2_raw = load_weight(w2, "w2")
         nc.sync.dma_start(nx_sb[:], nx)
 
         xq_s = keep.tile([P, S], U8, name="xq_s", align_bytes=64)
         xq_w = keep.tile([P, S], U32, name="xq_w", align_bytes=64)
-        nc.vector.tensor_copy(xq_s[:], xs[:].indirect(offs_sb[:]))
-        nc.vector.tensor_copy(xq_w[:], xw[:].bitcast(U32).indirect(offs_sb[:]))
 
-        def round_chunk(grouped, raw, a):
-            m = W_CHUNK // PACK
-            dst = grouped[:].rearrange("p (t m j) -> p m t j", t=PACK, j=PACK)[:, a * m : (a + 1) * m]
-            src = raw[:].rearrange("p j (m t) -> p m t j", t=PACK)
-            nc.scalar.activation(dst, src, COPY)
+        def dealt(grouped, raw, rows):
+            dst = grouped[:].rearrange("p (t m j) -> p m t j", t=PACK, j=PACK)[:, rows]
+            src = raw[:].rearrange("p j (m t) -> p m t j", t=PACK)[:, rows]
+            return dst, src
 
         def quantize_weight(grouped, name):
             codes = keep.tile([P, N], U32, name=f"{name}_codes", align_bytes=64)
@@ -78,50 +69,74 @@ def tile_picked_redq_none_po_kernel(
             nc.vector.quantize_mx(out=codes[:].bitcast(FP8X4), scales=scales[:], in_=grouped[:])
             return codes, scales
 
-        def product(codes, scales, t, name):
-            acc = psum.tile([P, S], F32, name=f"{name}{t}")
-            cols = slice(t * P, (t + 1) * P)
+        def product(acc, codes, scales, t, cols):
+            rows = slice(t * P, (t + 1) * P)
             nc.tensor.matmul_mx(
-                out=acc[:],
-                lhsT=codes[:, cols].bitcast(FP8X4),
-                lhsT_scale=scales[:, cols],
-                rhs=xq_w[:].bitcast(FP8X4),
-                rhs_scale=xq_s[:],
+                out=acc,
+                lhsT=codes[:, rows].bitcast(FP8X4),
+                lhsT_scale=scales[:, rows],
+                rhs=xq_w[:, cols].bitcast(FP8X4),
+                rhs_scale=xq_s[:, cols],
                 start=True,
                 stop=True,
             )
-            return acc
+
+        halves = [slice(h * HALF, (h + 1) * HALF) for h in range(S // HALF)]
+
+        def entries(cols):
+            return slice(cols.start // 16, cols.stop // 16)
 
         w1_bf = keep.tile([P, PACK * N], BF16, name="w1_bf", align_bytes=64)
-        w2_bf = keep.tile([P, PACK * N], BF16, name="w2_bf", align_bytes=64)
-        for a in range(N // W_CHUNK):
-            round_chunk(w1_bf, w1_raw[a], a)
+        dst, src = dealt(w1_bf, w1_raw, slice(0, W1_SPLIT))
+        nc.vector.tensor_copy(dst, src)
+        dst, src = dealt(w1_bf, w1_raw, slice(W1_SPLIT, P))
+        nc.scalar.activation(dst, src, COPY)
+        nc.vector.tensor_copy(xq_s[:], xs[:].indirect(offs_sb[:]))
+        w2_raw = load_weight(w2, "w2_raw")
         w1_codes, w1_scales = quantize_weight(w1_bf, "w1")
-        y = [product(w1_codes, w1_scales, t, "y") for t in range(PACK)]
 
         base = keep.tile([P, PACK, S], F32, name="base")
-        for t in range(PACK):
-            y_neg = keep.tile([P, S], F32, name=f"y_neg{t}")
-            nc.scalar.activation(y_neg[:], y[t][:], COPY, scale=-1.0)
-            round_chunk(w2_bf, w2_raw[t], t)
-            for h in range(S // HALF):
-                cols = slice(h * HALF, (h + 1) * HALF)
+        y_neg = []
+
+        def gather_current(t):
+            for cols in halves:
                 nc.vector.tensor_tensor(
-                    base[:, t, cols],
-                    y_neg[:].indirect(cur_sb[:, h * HALF // 16 : (h + 1) * HALF // 16]),
-                    rw_sb[:, cols],
-                    ALU.add,
+                    base[:, t, cols], y_neg[t][:].indirect(cur_sb[:, entries(cols)]), rw_sb[:, cols], ALU.add
                 )
 
-        w2_codes, w2_scales = quantize_weight(w2_bf, "w2")
-        e = [product(w2_codes, w2_scales, t, "e") for t in range(PACK)]
+        y_neg.append(keep.tile([P, S], F32, name="y_neg0"))
+        for h, cols in enumerate(halves):
+            nc.vector.tensor_copy(xq_w[:, cols], xw[:].bitcast(U32).indirect(offs_sb[:, entries(cols)]))
+            acc = psum.tile([P, HALF], F32, name=f"y0_{h}", tag=f"bank{h}")
+            product(acc[:], w1_codes, w1_scales, 0, cols)
+            nc.scalar.activation(y_neg[0][:, cols], acc[:], COPY, scale=-1.0)
+        y_acc = {}
+        for t in range(1, PACK):
+            y_acc[t] = psum.tile([P, S], F32, name=f"y{t}", tag=f"bank{t + 1}")
+            product(y_acc[t][:], w1_codes, w1_scales, t, slice(0, S))
+        gather_current(0)
+        for t in range(1, PACK - 1):
+            y_neg.append(keep.tile([P, S], F32, name=f"y_neg{t}"))
+            nc.scalar.activation(y_neg[t][:], y_acc[t][:], COPY, scale=-1.0)
+            gather_current(t)
 
+        w2_bf = keep.tile([P, PACK * N], BF16, name="w2_bf", tag="w2_bf", align_bytes=64)
+        dst, src = dealt(w2_bf, w2_raw, slice(0, P))
+        nc.scalar.activation(dst, src, COPY)
+        w2_codes, w2_scales = quantize_weight(w2_bf, "w2")
+        t = PACK - 1
+        y_neg.append(keep.tile([P, S], F32, name=f"y_neg{t}", tag="w_raw"))
+        nc.scalar.activation(y_neg[t][:], y_acc[t][:], COPY, scale=-1.0)
+        gather_current(t)
+
+        y_disc = keep.tile([P, PACK, S], F32, name="y_disc", tag="w2_bf", align_bytes=64)
         low = []
         for t in range(PACK):
-            y_disc = keep.tile([P, S], F32, name=f"y_disc{t}")
-            nc.scalar.activation(y_disc[:], y[t][:], COPY, scale=DISCOUNT)
+            e_acc = psum.tile([P, S], F32, name=f"e{t}", tag=f"bank{(t + 5) % 8}")
+            product(e_acc[:], w2_codes, w2_scales, t, slice(0, S))
+            nc.scalar.activation(y_disc[:, t, :], y_neg[t][:], COPY, scale=-DISCOUNT)
             low_t = keep.tile([P, S], F32, name=f"low{t}")
-            nc.vector.scalar_tensor_tensor(low_t[:], e[t][:], DISCOUNT, y_disc[:], ALU.mult, ALU.min)
+            nc.vector.scalar_tensor_tensor(low_t[:], e_acc[:], DISCOUNT, y_disc[:, t, :], ALU.mult, ALU.min)
             low.append(low_t)
 
         out_rows = out_0.rearrange("(p t) j -> p t j", t=PACK)

@@ -20,7 +20,7 @@ COPY = mybir.ActivationFunctionType.Copy
 DISCOUNT = 0.9
 W1_SPLIT = 52
 HALF = 256
-OUT_CHUNKS = ((0, 256), (256, 128), (384, 128))
+QUARTER = 128
 
 
 def tile_picked_redq_none_po_kernel(
@@ -52,16 +52,21 @@ def tile_picked_redq_none_po_kernel(
             )
         nc.sync.dma_start(xw[:], x_words[0].rearrange("p n t -> p (n t)").bitcast(I32))
         nc.sync.dma_start(cur_sb[:], cur)
+        w2_rows = w2.rearrange("(p j) c -> p j c", j=PACK)
+        w2_raw = [keep.tile([P, PACK, N // 2], F32, name=f"w2_raw{h}", tag=f"w2_raw{h}") for h in range(2)]
+        nc.sync.dma_start(w2_raw[0][:], w2_rows[:, :, : N // 2])
         nc.sync.dma_start(rw_sb[:], rw)
+        nc.sync.dma_start(w2_raw[1][:], w2_rows[:, :, N // 2 :])
         nc.sync.dma_start(nx_sb[:], nx)
 
         xq_s = keep.tile([P, S], U8, name="xq_s", align_bytes=64)
         xq_w = keep.tile([P, S], U32, name="xq_w", align_bytes=64)
 
-        def dealt(grouped, raw, rows):
-            dst = grouped[:].rearrange("p (t m j) -> p m t j", t=PACK, j=PACK)[:, rows]
-            src = raw[:].rearrange("p j (m t) -> p m t j", t=PACK)[:, rows]
-            return dst, src
+        def dealt_out(grouped, rows):
+            return grouped[:].rearrange("p (t m j) -> p m j t", t=PACK, j=PACK)[:, rows]
+
+        def dealt_in(raw):
+            return raw[:].rearrange("p j (m t) -> p m j t", t=PACK)
 
         def quantize_weight(grouped, name):
             codes = keep.tile([P, N], U32, name=f"{name}_codes", align_bytes=64)
@@ -87,21 +92,19 @@ def tile_picked_redq_none_po_kernel(
             return slice(cols.start // 16, cols.stop // 16)
 
         w1_bf = keep.tile([P, PACK * N], BF16, name="w1_bf", align_bytes=64)
-        dst, src = dealt(w1_bf, w1_raw, slice(0, W1_SPLIT))
-        nc.vector.tensor_copy(dst, src)
-        dst, src = dealt(w1_bf, w1_raw, slice(W1_SPLIT, P))
-        nc.scalar.activation(dst, src, COPY)
+        nc.vector.tensor_copy(dealt_out(w1_bf, slice(0, W1_SPLIT)), dealt_in(w1_raw)[:, :W1_SPLIT])
+        nc.scalar.activation(dealt_out(w1_bf, slice(W1_SPLIT, P)), dealt_in(w1_raw)[:, W1_SPLIT:], COPY)
         nc.vector.tensor_copy(xq_s[:], xs[:].indirect(offs_sb[:]))
-        w2_raw = load_weight(w2, "w2_raw")
         w1_codes, w1_scales = quantize_weight(w1_bf, "w1")
 
-        base = keep.tile([P, PACK, S], F32, name="base")
+        base = {}
         y_neg = []
 
         def gather_current(t):
-            for cols in halves:
+            for h, cols in enumerate(halves):
+                base[t, h] = keep.tile([P, HALF], F32, name=f"base{t}_{h}", tag=f"base{t}_{h}")
                 nc.vector.tensor_tensor(
-                    base[:, t, cols], y_neg[t][:].indirect(cur_sb[:, entries(cols)]), rw_sb[:, cols], ALU.add
+                    base[t, h][:], y_neg[t][:].indirect(cur_sb[:, entries(cols)]), rw_sb[:, cols], ALU.add
                 )
 
         y_neg.append(keep.tile([P, S], F32, name="y_neg0"))
@@ -114,57 +117,77 @@ def tile_picked_redq_none_po_kernel(
         for t in range(1, PACK):
             y_acc[t] = psum.tile([P, S], F32, name=f"y{t}", tag=f"bank{t + 1}")
             product(y_acc[t][:], w1_codes, w1_scales, t, slice(0, S))
+        w2_bf = keep.tile([P, PACK * N], BF16, name="w2_bf", tag="w2_bf", align_bytes=64)
+        nc.vector.tensor_copy(dealt_out(w2_bf, slice(0, P // 2)), dealt_in(w2_raw[0]))
         gather_current(0)
         for t in range(1, PACK - 1):
             y_neg.append(keep.tile([P, S], F32, name=f"y_neg{t}"))
             nc.scalar.activation(y_neg[t][:], y_acc[t][:], COPY, scale=-1.0)
             gather_current(t)
 
-        w2_bf = keep.tile([P, PACK * N], BF16, name="w2_bf", tag="w2_bf", align_bytes=64)
-        dst, src = dealt(w2_bf, w2_raw, slice(0, P))
-        nc.scalar.activation(dst, src, COPY)
+        nc.scalar.activation(dealt_out(w2_bf, slice(P // 2, P)), dealt_in(w2_raw[1]), COPY)
         w2_codes, w2_scales = quantize_weight(w2_bf, "w2")
         t = PACK - 1
-        y_neg.append(keep.tile([P, S], F32, name=f"y_neg{t}", tag="w_raw"))
+        y_neg.append(keep.tile([P, S], F32, name=f"y_neg{t}", tag="w2_raw1"))
         nc.scalar.activation(y_neg[t][:], y_acc[t][:], COPY, scale=-1.0)
         gather_current(t)
 
-        y_disc = keep.tile([P, PACK, S], F32, name="y_disc", tag="w2_bf", align_bytes=64)
         low = []
-        for t in range(PACK):
+
+        def clip(t):
             e_acc = psum.tile([P, S], F32, name=f"e{t}", tag=f"bank{(t + 5) % 8}")
             product(e_acc[:], w2_codes, w2_scales, t, slice(0, S))
-            nc.scalar.activation(y_disc[:, t, :], y_neg[t][:], COPY, scale=-DISCOUNT)
-            low_t = keep.tile([P, S], F32, name=f"low{t}")
-            nc.vector.scalar_tensor_tensor(low_t[:], e_acc[:], DISCOUNT, y_disc[:, t, :], ALU.mult, ALU.min)
-            low.append(low_t)
+            tag = "w2_bf" if t == 0 else f"y_disc{t}"
+            y_disc = keep.tile([P, S], F32, name=f"y_disc{t}", tag=tag, align_bytes=64)
+            nc.scalar.activation(y_disc[:], y_neg[t][:], COPY, scale=-DISCOUNT)
+            low.append(keep.tile([P, S], F32, name=f"low{t}"))
+            nc.vector.scalar_tensor_tensor(low[t][:], e_acc[:], DISCOUNT, y_disc[:], ALU.mult, ALU.min)
+
+        def gather_next(td, t, cols):
+            h = cols.start // HALF
+            nc.vector.tensor_tensor(
+                td[:, t, :],
+                low[t][:].indirect(nx_sb[:, entries(cols)]),
+                base[t, h][:, cols.start - h * HALF : cols.stop - h * HALF],
+                ALU.add,
+            )
 
         out_rows = out_0.rearrange("(p t) j -> p t j", t=PACK)
         out_words = out_1[0].rearrange("p n t -> p (n t)").bitcast(I32)
         o_scales = keep.tile([P, S], U8, name="o_scales", align_bytes=64)
-        for c0, width in OUT_CHUNKS:
-            cols = slice(c0, c0 + width)
-            td = keep.tile([P, PACK, width], F32, name=f"td{c0}")
-            for t in range(PACK):
-                nc.vector.tensor_tensor(
-                    td[:, t, :],
-                    low[t][:].indirect(nx_sb[:, c0 // 16 : (c0 + width) // 16]),
-                    base[:, t, cols],
-                    ALU.add,
-                )
+        td_bf = [keep.tile([P, HALF, PACK], BF16, name=f"td_bf{h}", align_bytes=64) for h in range(2)]
+
+        def store_and_round(td, cols, copy):
             nc.sync.dma_start(out_rows[:, :, cols], td[:])
-            td_bf = keep.tile([P, width, PACK], BF16, name=f"td_bf{c0}", align_bytes=64)
-            if c0 + width == S:
-                nc.vector.tensor_copy(td_bf[:], td[:].rearrange("p t j -> p j t"))
-            else:
-                nc.scalar.copy(td_bf[:], td[:].rearrange("p t j -> p j t"))
-            o_codes = keep.tile([P, width], I32, name=f"o_codes{c0}", align_bytes=64)
+            h = cols.start // HALF
+            dst = td_bf[h][:, cols.start - h * HALF : cols.stop - h * HALF, :]
+            copy(dst.rearrange("p (c i) t -> p c t i", i=4), td[:].rearrange("p t (c i) -> p c t i", i=4))
+
+        def quantize_result(h):
+            o_codes = keep.tile([P, HALF], I32, name=f"o_codes{h}", align_bytes=64)
             nc.vector.quantize_mx(
                 out=o_codes[:].bitcast(FP8X4),
-                scales=o_scales[:, cols],
-                in_=td_bf[:].rearrange("p j t -> p (j t)"),
+                scales=o_scales[:, halves[h]],
+                in_=td_bf[h][:].rearrange("p j t -> p (j t)"),
             )
-            nc.sync.dma_start(out_words[:, cols], o_codes[:])
+            nc.sync.dma_start(out_words[:, halves[h]], o_codes[:])
+
+        clip(0)
+        clip(1)
+        td = keep.tile([P, PACK, HALF], F32, name="td_first", tag="y_disc1", align_bytes=64)
+        for t in range(PACK):
+            gather_next(td, t, halves[0])
+            if t + 2 < PACK:
+                clip(t + 2)
+        store_and_round(td, halves[0], nc.scalar.copy)
+        quantize_result(0)
+        for i, copy in enumerate((nc.scalar.copy, nc.vector.tensor_copy)):
+            cols = slice(HALF + i * QUARTER, HALF + (i + 1) * QUARTER)
+            td = keep.tile([P, PACK, QUARTER], F32, name=f"td_last{i}", tag=f"base{2 + i}_0")
+            for t in range(PACK):
+                gather_next(td, t, cols)
+            store_and_round(td, cols, copy)
+        quantize_result(1)
         for q in range(4):
             queue = nc.scalar if q % 2 else nc.sync
             queue.dma_start(

@@ -19,6 +19,7 @@ COPY = mybir.ActivationFunctionType.Copy
 
 DISCOUNT = 0.9
 W1_SPLIT = 52
+W2_SPLIT = 32
 HALF = 256
 QUARTER = 128
 
@@ -51,12 +52,16 @@ def tile_picked_redq_none_po_kernel(
                 xs[32 * q : 32 * q + 4, :].bitcast(I32), x_scales[0, 4 * q : 4 * q + 4, :].bitcast(I32)
             )
         nc.sync.dma_start(xw[:], x_words[0].rearrange("p n t -> p (n t)").bitcast(I32))
-        nc.sync.dma_start(cur_sb[:], cur)
-        w2_rows = w2.rearrange("(p j) c -> p j c", j=PACK)
-        w2_raw = [keep.tile([P, PACK, N // 2], F32, name=f"w2_raw{h}", tag=f"w2_raw{h}") for h in range(2)]
-        nc.sync.dma_start(w2_raw[0][:], w2_rows[:, :, : N // 2])
         nc.sync.dma_start(rw_sb[:], rw)
-        nc.sync.dma_start(w2_raw[1][:], w2_rows[:, :, N // 2 :])
+        w2_rows = w2.rearrange("(p j) c -> p j c", j=PACK)
+        w2_cut = PACK * W2_SPLIT
+        w2_raw = [
+            keep.tile([P, PACK, width], F32, name=f"w2_raw{h}", tag=f"w2_raw{h}")
+            for h, width in enumerate((w2_cut, N - w2_cut))
+        ]
+        nc.sync.dma_start(w2_raw[0][:], w2_rows[:, :, :w2_cut])
+        nc.sync.dma_start(cur_sb[:], cur)
+        nc.sync.dma_start(w2_raw[1][:], w2_rows[:, :, w2_cut:])
         nc.sync.dma_start(nx_sb[:], nx)
 
         xq_s = keep.tile([P, S], U8, name="xq_s", align_bytes=64)
@@ -97,71 +102,73 @@ def tile_picked_redq_none_po_kernel(
         nc.vector.tensor_copy(xq_s[:], xs[:].indirect(offs_sb[:]))
         w1_codes, w1_scales = quantize_weight(w1_bf, "w1")
 
-        base = {}
+        base = keep.tile([P, PACK, S], F32, name="base")
         y_neg = []
 
-        def gather_current(t):
-            for h, cols in enumerate(halves):
-                base[t, h] = keep.tile([P, HALF], F32, name=f"base{t}_{h}", tag=f"base{t}_{h}")
+        def gather_current(t, pieces):
+            for cols in pieces:
                 nc.vector.tensor_tensor(
-                    base[t, h][:], y_neg[t][:].indirect(cur_sb[:, entries(cols)]), rw_sb[:, cols], ALU.add
+                    base[:, t, cols], y_neg[t][:].indirect(cur_sb[:, entries(cols)]), rw_sb[:, cols], ALU.add
                 )
 
-        y_neg.append(keep.tile([P, S], F32, name="y_neg0"))
-        for h, cols in enumerate(halves):
+        for t in range(PACK - 1):
+            y_neg.append(keep.tile([P, 2 * S], F32, name=f"y_neg{t}"))
+            nc.gpsimd.memset(y_neg[t][:, S:], 0.0)
+        for cols in halves:
             nc.vector.tensor_copy(xq_w[:, cols], xw[:].bitcast(U32).indirect(offs_sb[:, entries(cols)]))
-            acc = psum.tile([P, HALF], F32, name=f"y0_{h}", tag=f"bank{h}")
+        w2_bf = keep.tile([P, PACK * N], BF16, name="w2_bf", tag="w2_bf", align_bytes=64)
+        nc.vector.tensor_copy(dealt_out(w2_bf, slice(0, W2_SPLIT)), dealt_in(w2_raw[0]))
+        pieces = (halves[0], slice(HALF, HALF + QUARTER), slice(HALF + QUARTER, S))
+        for i, cols in enumerate(pieces):
+            acc = psum.tile([P, cols.stop - cols.start], F32, name=f"y0_{i}", tag=f"bank{i}")
             product(acc[:], w1_codes, w1_scales, 0, cols)
-            nc.scalar.activation(y_neg[0][:, cols], acc[:], COPY, scale=-1.0)
+            if cols.stop < S:
+                nc.scalar.activation(y_neg[0][:, cols], acc[:], COPY, scale=-1.0)
+            else:
+                nc.vector.tensor_scalar_mul(y_neg[0][:, cols], acc[:], -1.0)
         y_acc = {}
         for t in range(1, PACK):
-            y_acc[t] = psum.tile([P, S], F32, name=f"y{t}", tag=f"bank{t + 1}")
+            y_acc[t] = psum.tile([P, S], F32, name=f"y{t}", tag=f"bank{t + 2}")
             product(y_acc[t][:], w1_codes, w1_scales, t, slice(0, S))
-        w2_bf = keep.tile([P, PACK * N], BF16, name="w2_bf", tag="w2_bf", align_bytes=64)
-        nc.vector.tensor_copy(dealt_out(w2_bf, slice(0, P // 2)), dealt_in(w2_raw[0]))
-        gather_current(0)
+        gather_current(0, [slice(0, S)])
         for t in range(1, PACK - 1):
-            y_neg.append(keep.tile([P, S], F32, name=f"y_neg{t}"))
-            nc.scalar.activation(y_neg[t][:], y_acc[t][:], COPY, scale=-1.0)
-            gather_current(t)
+            nc.scalar.activation(y_neg[t][:, :S], y_acc[t][:], COPY, scale=-1.0)
+            gather_current(t, [slice(0, S)])
 
-        nc.scalar.activation(dealt_out(w2_bf, slice(P // 2, P)), dealt_in(w2_raw[1]), COPY)
+        nc.scalar.activation(dealt_out(w2_bf, slice(W2_SPLIT, P)), dealt_in(w2_raw[1]), COPY)
         w2_codes, w2_scales = quantize_weight(w2_bf, "w2")
         t = PACK - 1
         y_neg.append(keep.tile([P, S], F32, name=f"y_neg{t}", tag="w2_raw1"))
         nc.scalar.activation(y_neg[t][:], y_acc[t][:], COPY, scale=-1.0)
-        gather_current(t)
+        gather_current(t, halves)
 
         low = []
+        y_disc = keep.tile([P, PACK, S], F32, name="y_disc", tag="w2_bf", align_bytes=64)
 
         def clip(t):
-            e_acc = psum.tile([P, S], F32, name=f"e{t}", tag=f"bank{(t + 5) % 8}")
+            e_acc = psum.tile([P, S], F32, name=f"e{t}", tag=f"bank{(t + 6) % 8}")
             product(e_acc[:], w2_codes, w2_scales, t, slice(0, S))
-            tag = "w2_bf" if t == 0 else f"y_disc{t}"
-            y_disc = keep.tile([P, S], F32, name=f"y_disc{t}", tag=tag, align_bytes=64)
-            nc.scalar.activation(y_disc[:], y_neg[t][:], COPY, scale=-DISCOUNT)
+            nc.scalar.activation(y_disc[:, t, :], y_neg[t][:, :S], COPY, scale=-DISCOUNT)
             low.append(keep.tile([P, S], F32, name=f"low{t}"))
-            nc.vector.scalar_tensor_tensor(low[t][:], e_acc[:], DISCOUNT, y_disc[:], ALU.mult, ALU.min)
-
-        def gather_next(td, t, cols):
-            h = cols.start // HALF
-            nc.vector.tensor_tensor(
-                td[:, t, :],
-                low[t][:].indirect(nx_sb[:, entries(cols)]),
-                base[t, h][:, cols.start - h * HALF : cols.stop - h * HALF],
-                ALU.add,
-            )
+            nc.vector.scalar_tensor_tensor(low[t][:], e_acc[:], DISCOUNT, y_disc[:, t, :], ALU.mult, ALU.min)
 
         out_rows = out_0.rearrange("(p t) j -> p t j", t=PACK)
         out_words = out_1[0].rearrange("p n t -> p (n t)").bitcast(I32)
         o_scales = keep.tile([P, S], U8, name="o_scales", align_bytes=64)
+        td = [keep.tile([P, PACK, HALF], F32, name=f"td{h}") for h in range(2)]
         td_bf = [keep.tile([P, HALF, PACK], BF16, name=f"td_bf{h}", align_bytes=64) for h in range(2)]
 
-        def store_and_round(td, cols, copy):
-            nc.sync.dma_start(out_rows[:, :, cols], td[:])
-            h = cols.start // HALF
-            dst = td_bf[h][:, cols.start - h * HALF : cols.stop - h * HALF, :]
-            copy(dst.rearrange("p (c i) t -> p c t i", i=4), td[:].rearrange("p t (c i) -> p c t i", i=4))
+        def gather_next(t, h, part):
+            cols = slice(h * HALF + part.start, h * HALF + part.stop)
+            nc.vector.tensor_tensor(
+                td[h][:, t, part], low[t][:].indirect(nx_sb[:, entries(cols)]), base[:, t, cols], ALU.add
+            )
+
+        def round_result(h, part, copy):
+            copy(
+                td_bf[h][:, part, :].rearrange("p (c i) t -> p c t i", i=4),
+                td[h][:, :, part].rearrange("p t (c i) -> p c t i", i=4),
+            )
 
         def quantize_result(h):
             o_codes = keep.tile([P, HALF], I32, name=f"o_codes{h}", align_bytes=64)
@@ -172,21 +179,24 @@ def tile_picked_redq_none_po_kernel(
             )
             nc.sync.dma_start(out_words[:, halves[h]], o_codes[:])
 
+        whole = slice(0, HALF)
         clip(0)
         clip(1)
-        td = keep.tile([P, PACK, HALF], F32, name="td_first", tag="y_disc1", align_bytes=64)
         for t in range(PACK):
-            gather_next(td, t, halves[0])
+            gather_next(t, 0, whole)
             if t + 2 < PACK:
                 clip(t + 2)
-        store_and_round(td, halves[0], nc.scalar.copy)
+        nc.sync.dma_start(out_rows[:, :, halves[0]], td[0][:])
+        round_result(0, whole, nc.scalar.copy)
         quantize_result(0)
-        for i, copy in enumerate((nc.scalar.copy, nc.vector.tensor_copy)):
-            cols = slice(HALF + i * QUARTER, HALF + (i + 1) * QUARTER)
-            td = keep.tile([P, PACK, QUARTER], F32, name=f"td_last{i}", tag=f"base{2 + i}_0")
-            for t in range(PACK):
-                gather_next(td, t, cols)
-            store_and_round(td, cols, copy)
+        last = PACK - 1
+        for t in range(last):
+            gather_next(t, 1, whole)
+        nc.sync.dma_start(out_rows[:, :last, halves[1]], td[1][:, :last, :])
+        for part, copy in ((slice(0, QUARTER), nc.scalar.copy), (slice(QUARTER, HALF), nc.vector.tensor_copy)):
+            gather_next(last, 1, part)
+            round_result(1, part, copy)
+        nc.sync.dma_start(out_rows[:, last, halves[1]], td[1][:, last, :])
         quantize_result(1)
         for q in range(4):
             queue = nc.scalar if q % 2 else nc.sync

@@ -1,6 +1,7 @@
 from contextlib import ExitStack
 
 import concourse.mybir as mybir
+from concourse.masks import make_identity
 
 K, T, S, N = 512, 2048, 512, 512
 P = 128
@@ -16,12 +17,14 @@ U8 = mybir.dt.uint8
 FP8X4 = mybir.dt.float8_e4m3fn_x4
 ALU = mybir.AluOpType
 COPY = mybir.ActivationFunctionType.Copy
+RELU = mybir.ActivationFunctionType.Relu
 
 DISCOUNT = 0.9
 W1_SPLIT = 52
 W2_SPLIT = 32
 HALF = 256
 QUARTER = 128
+END_SPLIT = 64
 
 
 def tile_picked_redq_none_po_kernel(
@@ -30,6 +33,7 @@ def tile_picked_redq_none_po_kernel(
     nc = tc.nc
     with ExitStack() as ctx:
         keep = ctx.enter_context(tc.tile_pool(name="keep", bufs=1))
+        late = ctx.enter_context(tc.tile_pool(name="late", bufs=1))
         psum = ctx.enter_context(tc.psum_pool(name="psum", bufs=1))
 
         offs_sb = keep.tile([P, S // 16], U16, name="offs_sb")
@@ -56,9 +60,11 @@ def tile_picked_redq_none_po_kernel(
         w2_rows = w2.rearrange("(p j) c -> p j c", j=PACK)
         w2_cut = PACK * W2_SPLIT
         w2_raw = [
-            keep.tile([P, PACK, width], F32, name=f"w2_raw{h}", tag=f"w2_raw{h}")
-            for h, width in enumerate((w2_cut, N - w2_cut))
+            keep.tile([P, PACK, w2_cut], F32, name="w2_raw0"),
+            late.tile([P, PACK, N - w2_cut], F32, name="w2_raw1", offset=0),
         ]
+        ident = keep.tile([P, P], F32, name="ident")
+        make_identity(nc, ident[:])
         nc.sync.dma_start(w2_raw[0][:], w2_rows[:, :, :w2_cut])
         nc.sync.dma_start(cur_sb[:], cur)
         nc.sync.dma_start(w2_raw[1][:], w2_rows[:, :, w2_cut:])
@@ -97,18 +103,29 @@ def tile_picked_redq_none_po_kernel(
             return slice(cols.start // 16, cols.stop // 16)
 
         w1_bf = keep.tile([P, PACK * N], BF16, name="w1_bf", align_bytes=64)
-        nc.vector.tensor_copy(dealt_out(w1_bf, slice(0, W1_SPLIT)), dealt_in(w1_raw)[:, :W1_SPLIT])
-        nc.scalar.activation(dealt_out(w1_bf, slice(W1_SPLIT, P)), dealt_in(w1_raw)[:, W1_SPLIT:], COPY)
+        nc.vector.tensor_scalar_mul(dealt_out(w1_bf, slice(0, W1_SPLIT)), dealt_in(w1_raw)[:, :W1_SPLIT], -1.0)
+        nc.scalar.activation(dealt_out(w1_bf, slice(W1_SPLIT, P)), dealt_in(w1_raw)[:, W1_SPLIT:], COPY, scale=-1.0)
         nc.vector.tensor_copy(xq_s[:], xs[:].indirect(offs_sb[:]))
         w1_codes, w1_scales = quantize_weight(w1_bf, "w1")
 
-        base = keep.tile([P, PACK, S], F32, name="base")
+        base = keep.tile([P, PACK - 1, S], F32, name="base")
+        base_last = [late.tile([P, HALF], F32, name=f"base_last{h}", offset=(16 + 4 * h) * S) for h in range(2)]
+        discount = late.tile([P, 1], F32, name="discount", offset=24 * S)
+        nc.gpsimd.memset(discount[:], 1.0)
+        nc.gpsimd.tensor_scalar(discount[:], discount[:], -DISCOUNT, 0.0, ALU.mult, ALU.add)
+
+        def base_cols(t, cols):
+            if t < PACK - 1:
+                return base[:, t, cols]
+            h = cols.start // HALF
+            return base_last[h][:, cols.start - h * HALF : cols.stop - h * HALF]
+
         y_neg = []
 
         def gather_current(t, pieces):
             for cols in pieces:
                 nc.vector.tensor_tensor(
-                    base[:, t, cols], y_neg[t][:].indirect(cur_sb[:, entries(cols)]), rw_sb[:, cols], ALU.add
+                    base_cols(t, cols), y_neg[t][:].indirect(cur_sb[:, entries(cols)]), rw_sb[:, cols], ALU.add
                 )
 
         for t in range(PACK - 1):
@@ -122,46 +139,88 @@ def tile_picked_redq_none_po_kernel(
         for i, cols in enumerate(pieces):
             acc = psum.tile([P, cols.stop - cols.start], F32, name=f"y0_{i}", tag=f"bank{i}")
             product(acc[:], w1_codes, w1_scales, 0, cols)
-            if cols.stop < S:
-                nc.scalar.activation(y_neg[0][:, cols], acc[:], COPY, scale=-1.0)
-            else:
-                nc.vector.tensor_scalar_mul(y_neg[0][:, cols], acc[:], -1.0)
+            nc.scalar.copy(y_neg[0][:, cols], acc[:])
         y_acc = {}
         for t in range(1, PACK):
             y_acc[t] = psum.tile([P, S], F32, name=f"y{t}", tag=f"bank{t + 2}")
             product(y_acc[t][:], w1_codes, w1_scales, t, slice(0, S))
+        last = PACK - 1
+        last_rows = slice(last * P, N)
+
+        def turned_product(acc, codes, scales, b, start, stop):
+            tokens = slice(b * P, (b + 1) * P)
+            nc.tensor.matmul_mx(
+                out=acc[:, tokens],
+                lhsT=xq_w[:, tokens].bitcast(FP8X4),
+                lhsT_scale=xq_s[:, tokens],
+                rhs=codes[:, last_rows].bitcast(FP8X4),
+                rhs_scale=scales[:, last_rows],
+                start=start,
+                stop=stop,
+            )
+
+        blocks = range(S // P)
+        yt_acc = psum.tile([P, S], F32, name="yt_acc", tag="bank1")
+        gap_acc = psum.tile([P, S], F32, name="gap_acc", tag="bank2")
+        for b in blocks:
+            turned_product(yt_acc, w1_codes, w1_scales, b, True, True)
+        for b in blocks:
+            turned_product(gap_acc, w1_codes, w1_scales, b, b == 0, False)
         gather_current(0, [slice(0, S)])
         for t in range(1, PACK - 1):
-            nc.scalar.activation(y_neg[t][:, :S], y_acc[t][:], COPY, scale=-1.0)
+            nc.scalar.copy(y_neg[t][:, :S], y_acc[t][:])
             gather_current(t, [slice(0, S)])
 
         nc.scalar.activation(dealt_out(w2_bf, slice(W2_SPLIT, P)), dealt_in(w2_raw[1]), COPY)
         w2_codes, w2_scales = quantize_weight(w2_bf, "w2")
         t = PACK - 1
-        y_neg.append(keep.tile([P, S], F32, name=f"y_neg{t}", tag="w2_raw1"))
-        nc.scalar.activation(y_neg[t][:], y_acc[t][:], COPY, scale=-1.0)
+        y_neg.append(late.tile([P, S], F32, name=f"y_neg{t}", offset=0))
+        nc.scalar.copy(y_neg[t][:], y_acc[t][:])
         gather_current(t, halves)
 
-        low = []
-        y_disc = keep.tile([P, PACK, S], F32, name="y_disc", tag="w2_bf", align_bytes=64)
+        low = [keep.tile([P, S], F32, name=f"low{t}") for t in range(PACK)]
+        y_disc_late = keep.tile([P, 2, S], F32, name="y_disc", tag="w2_bf", align_bytes=64)
+        y_disc = [late.tile([P, S], F32, name=f"y_disc{t}", offset=4 * S * (t + 1))[:] for t in range(2)]
+        y_disc.append(y_disc_late[:, 0, :])
 
         def clip(t):
             e_acc = psum.tile([P, S], F32, name=f"e{t}", tag=f"bank{(t + 6) % 8}")
             product(e_acc[:], w2_codes, w2_scales, t, slice(0, S))
-            nc.scalar.activation(y_disc[:, t, :], y_neg[t][:, :S], COPY, scale=-DISCOUNT)
-            low.append(keep.tile([P, S], F32, name=f"low{t}"))
-            nc.vector.scalar_tensor_tensor(low[t][:], e_acc[:], DISCOUNT, y_disc[:, t, :], ALU.mult, ALU.min)
+            nc.scalar.activation(y_disc[t], y_neg[t][:, :S], COPY, scale=-DISCOUNT)
+            nc.vector.scalar_tensor_tensor(low[t][:], e_acc[:], DISCOUNT, y_disc[t], ALU.mult, ALU.min)
+
+        yt_neg = y_disc_late[:, 1, :]
+        excess = keep.tile([P, S], F32, name="excess")
+        low_acc = psum.tile([P, S], F32, name="low_acc", tag="bank3")
+
+        def turn_back(src, start, stop):
+            for b in blocks:
+                tokens = slice(b * P, (b + 1) * P)
+                nc.tensor.matmul(
+                    low_acc[:, tokens],
+                    lhsT=src[:, tokens],
+                    rhs=ident[:],
+                    start=start and b == 0,
+                    stop=stop and b == S // P - 1,
+                    is_transpose=True,
+                )
 
         out_rows = out_0.rearrange("(p t) j -> p t j", t=PACK)
         out_words = out_1[0].rearrange("p n t -> p (n t)").bitcast(I32)
         o_scales = keep.tile([P, S], U8, name="o_scales", align_bytes=64)
-        td = [keep.tile([P, PACK, HALF], F32, name=f"td{h}") for h in range(2)]
-        td_bf = [keep.tile([P, HALF, PACK], BF16, name=f"td_bf{h}", align_bytes=64) for h in range(2)]
+        stages = (halves[0], slice(HALF, HALF + QUARTER), slice(HALF + QUARTER, S))
+        widths = [cols.stop - cols.start for cols in stages]
+        td = [
+            keep.tile([P, PACK, HALF], F32, name="td0"),
+            late.tile([P, PACK, QUARTER], F32, name="td1", offset=24 * S),
+            late.tile([P, PACK, QUARTER], F32, name="td2", offset=16 * S),
+        ]
+        td_bf = [keep.tile([P, w, PACK], BF16, name=f"td_bf{h}", align_bytes=64) for h, w in enumerate(widths)]
 
-        def gather_next(t, h, part):
-            cols = slice(h * HALF + part.start, h * HALF + part.stop)
+        def gather_next(t, h):
+            cols = stages[h]
             nc.vector.tensor_tensor(
-                td[h][:, t, part], low[t][:].indirect(nx_sb[:, entries(cols)]), base[:, t, cols], ALU.add
+                td[h][:, t, :], low[t][:].indirect(nx_sb[:, entries(cols)]), base_cols(t, cols), ALU.add
             )
 
         def round_result(h, part, copy):
@@ -171,33 +230,41 @@ def tile_picked_redq_none_po_kernel(
             )
 
         def quantize_result(h):
-            o_codes = keep.tile([P, HALF], I32, name=f"o_codes{h}", align_bytes=64)
+            o_codes = keep.tile([P, widths[h]], I32, name=f"o_codes{h}", align_bytes=64)
             nc.vector.quantize_mx(
                 out=o_codes[:].bitcast(FP8X4),
-                scales=o_scales[:, halves[h]],
+                scales=o_scales[:, stages[h]],
                 in_=td_bf[h][:].rearrange("p j t -> p (j t)"),
             )
-            nc.sync.dma_start(out_words[:, halves[h]], o_codes[:])
+            nc.sync.dma_start(out_words[:, stages[h]], o_codes[:])
 
-        whole = slice(0, HALF)
         clip(0)
         clip(1)
+        gather_next(0, 0)
+        clip(2)
+        nc.scalar.copy(yt_neg, yt_acc[:])
+        for b in blocks:
+            turned_product(gap_acc, w2_codes, w2_scales, b, False, b == S // P - 1)
+        nc.scalar.activation(excess[:], gap_acc[:], RELU, scale=-1.0)
+        turn_back(yt_neg, True, False)
+        turn_back(excess[:], False, True)
+        nc.scalar.activation(low[last][:], low_acc[:], COPY, scale=discount[:])
+        for t in range(1, PACK):
+            gather_next(t, 0)
+        nc.sync.dma_start(out_rows[:, :, stages[0]], td[0][:])
+        round_result(0, slice(0, widths[0]), nc.scalar.copy)
         for t in range(PACK):
-            gather_next(t, 0, whole)
-            if t + 2 < PACK:
-                clip(t + 2)
-        nc.sync.dma_start(out_rows[:, :, halves[0]], td[0][:])
-        round_result(0, whole, nc.scalar.copy)
+            gather_next(t, 1)
+        nc.sync.dma_start(out_rows[:, :, stages[1]], td[1][:])
+        round_result(1, slice(0, widths[1]), nc.scalar.copy)
+        for t in range(PACK):
+            gather_next(t, 2)
+        nc.sync.dma_start(out_rows[:, :, stages[2]], td[2][:])
         quantize_result(0)
-        last = PACK - 1
-        for t in range(last):
-            gather_next(t, 1, whole)
-        nc.sync.dma_start(out_rows[:, :last, halves[1]], td[1][:, :last, :])
-        for part, copy in ((slice(0, QUARTER), nc.scalar.copy), (slice(QUARTER, HALF), nc.vector.tensor_copy)):
-            gather_next(last, 1, part)
-            round_result(1, part, copy)
-        nc.sync.dma_start(out_rows[:, last, halves[1]], td[1][:, last, :])
         quantize_result(1)
+        round_result(2, slice(0, END_SPLIT), nc.vector.tensor_copy)
+        round_result(2, slice(END_SPLIT, widths[2]), nc.scalar.copy)
+        quantize_result(2)
         for q in range(4):
             queue = nc.scalar if q % 2 else nc.sync
             queue.dma_start(

@@ -21,7 +21,7 @@ RELU = mybir.ActivationFunctionType.Relu
 
 DISCOUNT = 0.9
 W1_SPLIT = 52
-W2_SPLIT = 32
+W2_SPLIT = 64
 HALF = 256
 QUARTER = 128
 END_SPLIT = 64
@@ -56,7 +56,6 @@ def tile_picked_redq_none_po_kernel(
                 xs[32 * q : 32 * q + 4, :].bitcast(I32), x_scales[0, 4 * q : 4 * q + 4, :].bitcast(I32)
             )
         nc.sync.dma_start(xw[:], x_words[0].rearrange("p n t -> p (n t)").bitcast(I32))
-        nc.sync.dma_start(rw_sb[:], rw)
         w2_rows = w2.rearrange("(p j) c -> p j c", j=PACK)
         w2_cut = PACK * W2_SPLIT
         w2_raw = [
@@ -66,6 +65,7 @@ def tile_picked_redq_none_po_kernel(
         ident = keep.tile([P, P], F32, name="ident")
         make_identity(nc, ident[:])
         nc.sync.dma_start(w2_raw[0][:], w2_rows[:, :, :w2_cut])
+        nc.sync.dma_start(rw_sb[:], rw)
         nc.sync.dma_start(cur_sb[:], cur)
         nc.sync.dma_start(w2_raw[1][:], w2_rows[:, :, w2_cut:])
         nc.sync.dma_start(nx_sb[:], nx)
@@ -128,7 +128,7 @@ def tile_picked_redq_none_po_kernel(
                     base_cols(t, cols), y_neg[t][:].indirect(cur_sb[:, entries(cols)]), rw_sb[:, cols], ALU.add
                 )
 
-        for t in range(PACK - 1):
+        for t in range(2):
             y_neg.append(keep.tile([P, 2 * S], F32, name=f"y_neg{t}"))
             nc.gpsimd.memset(y_neg[t][:, S:], 0.0)
         for cols in halves:
@@ -167,21 +167,19 @@ def tile_picked_redq_none_po_kernel(
         for b in blocks:
             turned_product(gap_acc, w1_codes, w1_scales, b, b == 0, False)
         gather_current(0, [slice(0, S)])
-        for t in range(1, PACK - 1):
-            nc.scalar.copy(y_neg[t][:, :S], y_acc[t][:])
-            gather_current(t, [slice(0, S)])
+        nc.scalar.copy(y_neg[1][:, :S], y_acc[1][:])
+        gather_current(1, [slice(0, S)])
 
         nc.scalar.activation(dealt_out(w2_bf, slice(W2_SPLIT, P)), dealt_in(w2_raw[1]), COPY)
         w2_codes, w2_scales = quantize_weight(w2_bf, "w2")
-        t = PACK - 1
-        y_neg.append(late.tile([P, S], F32, name=f"y_neg{t}", offset=0))
-        nc.scalar.copy(y_neg[t][:], y_acc[t][:])
-        gather_current(t, halves)
+        for t in range(2, PACK):
+            y_neg.append(late.tile([P, S], F32, name=f"y_neg{t}", offset=4 * S * (t - 2)))
+            nc.scalar.copy(y_neg[t][:], y_acc[t][:])
+            gather_current(t, halves)
 
         low = [keep.tile([P, S], F32, name=f"low{t}") for t in range(PACK)]
-        y_disc_late = keep.tile([P, 2, S], F32, name="y_disc", tag="w2_bf", align_bytes=64)
-        y_disc = [late.tile([P, S], F32, name=f"y_disc{t}", offset=4 * S * (t + 1))[:] for t in range(2)]
-        y_disc.append(y_disc_late[:, 0, :])
+        y_disc_late = keep.tile([P, 4, S], F32, name="y_disc", tag="w2_bf", align_bytes=64)
+        y_disc = [y_disc_late[:, t, :] for t in range(last)]
 
         def clip(t):
             e_acc = psum.tile([P, S], F32, name=f"e{t}", tag=f"bank{(t + 6) % 8}")
@@ -189,7 +187,7 @@ def tile_picked_redq_none_po_kernel(
             nc.scalar.activation(y_disc[t], y_neg[t][:, :S], COPY, scale=-DISCOUNT)
             nc.vector.scalar_tensor_tensor(low[t][:], e_acc[:], DISCOUNT, y_disc[t], ALU.mult, ALU.min)
 
-        yt_neg = y_disc_late[:, 1, :]
+        yt_neg = y_disc_late[:, last, :]
         excess = keep.tile([P, S], F32, name="excess")
         low_acc = psum.tile([P, S], F32, name="low_acc", tag="bank3")
 

@@ -51,6 +51,8 @@ def tile_picked_redq_none_po_kernel(
         nc.vector.memset(xs[:].bitcast(I32), 0)
         w1_raw = load_weight(w1, "w1_raw")
         nc.sync.dma_start(offs_sb[:], offs)
+        rw_col = keep.tile([P, PACK], F32, name="rw_col")
+        nc.scalar.dma_start(rw_col[:], rw[0].rearrange("(p b) -> p b", b=PACK))
         for q in range(4):
             nc.sync.dma_start(
                 xs[32 * q : 32 * q + 4, :].bitcast(I32), x_scales[0, 4 * q : 4 * q + 4, :].bitcast(I32)
@@ -65,10 +67,14 @@ def tile_picked_redq_none_po_kernel(
         ident = keep.tile([P, P], F32, name="ident")
         make_identity(nc, ident[:])
         nc.sync.dma_start(w2_raw[0][:], w2_rows[:, :, :w2_cut])
-        nc.sync.dma_start(rw_sb[:], rw)
         nc.sync.dma_start(cur_sb[:], cur)
         nc.sync.dma_start(w2_raw[1][:], w2_rows[:, :, w2_cut:])
         nc.sync.dma_start(nx_sb[:], nx)
+
+        rw_acc = psum.tile([P, PACK, P], F32, name="rw_acc", tag="bank7")
+        for b in range(PACK):
+            nc.tensor.transpose(rw_acc[:, b, :], rw_col[:, b : b + 1].to_broadcast([P, P]), ident[:])
+        nc.scalar.copy(rw_sb[:].rearrange("p (q b) -> p q b", b=PACK), rw_acc[:].rearrange("p b q -> p q b"))
 
         xq_s = keep.tile([P, S], U8, name="xq_s", align_bytes=64)
         xq_w = keep.tile([P, S], U32, name="xq_w", align_bytes=64)
@@ -103,8 +109,8 @@ def tile_picked_redq_none_po_kernel(
             return slice(cols.start // 16, cols.stop // 16)
 
         w1_bf = keep.tile([P, PACK * N], BF16, name="w1_bf", align_bytes=64)
-        nc.vector.tensor_scalar_mul(dealt_out(w1_bf, slice(0, W1_SPLIT)), dealt_in(w1_raw)[:, :W1_SPLIT], -1.0)
-        nc.scalar.activation(dealt_out(w1_bf, slice(W1_SPLIT, P)), dealt_in(w1_raw)[:, W1_SPLIT:], COPY, scale=-1.0)
+        nc.vector.tensor_copy(dealt_out(w1_bf, slice(0, W1_SPLIT)), dealt_in(w1_raw)[:, :W1_SPLIT])
+        nc.scalar.activation(dealt_out(w1_bf, slice(W1_SPLIT, P)), dealt_in(w1_raw)[:, W1_SPLIT:], COPY)
         nc.vector.tensor_copy(xq_s[:], xs[:].indirect(offs_sb[:]))
         w1_codes, w1_scales = quantize_weight(w1_bf, "w1")
 
@@ -113,6 +119,9 @@ def tile_picked_redq_none_po_kernel(
         discount = late.tile([P, 1], F32, name="discount", offset=24 * S)
         nc.gpsimd.memset(discount[:], 1.0)
         nc.gpsimd.tensor_scalar(discount[:], discount[:], -DISCOUNT, 0.0, ALU.mult, ALU.add)
+
+        minus_one = keep.tile([P, 1], F32, name="minus_one", tag="second")
+        nc.gpsimd.memset(minus_one[:], -1.0)
 
         def base_cols(t, cols):
             if t < PACK - 1:
@@ -133,13 +142,29 @@ def tile_picked_redq_none_po_kernel(
             nc.gpsimd.memset(y_neg[t][:, S:], 0.0)
         for cols in halves:
             nc.vector.tensor_copy(xq_w[:, cols], xw[:].bitcast(U32).indirect(offs_sb[:, entries(cols)]))
-        w2_bf = keep.tile([P, PACK * N], BF16, name="w2_bf", tag="w2_bf", align_bytes=64)
-        nc.vector.tensor_copy(dealt_out(w2_bf, slice(0, W2_SPLIT)), dealt_in(w2_raw[0]))
+        w2_bf = [
+            keep.tile([P, PACK * w2_cut], BF16, name="w2_bf0", align_bytes=64),
+            keep.tile([P, PACK * w2_cut], BF16, name="w2_bf1", align_bytes=64),
+        ]
+        w2_codes = keep.tile([P, N], U32, name="w2_codes", align_bytes=64)
+        w2_scales = keep.tile([P, N], U8, name="w2_scales", align_bytes=64)
+
+        def quantize_w2_half(h):
+            for t in range(PACK):
+                rows = slice(t * P + h * W2_SPLIT, t * P + (h + 1) * W2_SPLIT)
+                nc.vector.quantize_mx(
+                    out=w2_codes[:, rows].bitcast(FP8X4),
+                    scales=w2_scales[:, rows],
+                    in_=w2_bf[h][:, t * w2_cut : (t + 1) * w2_cut],
+                )
+
+        nc.vector.tensor_scalar_mul(dealt_out(w2_bf[0], slice(0, W2_SPLIT)), dealt_in(w2_raw[0]), -1.0)
+        quantize_w2_half(0)
         pieces = (halves[0], slice(HALF, HALF + QUARTER), slice(HALF + QUARTER, S))
         for i, cols in enumerate(pieces):
             acc = psum.tile([P, cols.stop - cols.start], F32, name=f"y0_{i}", tag=f"bank{i}")
             product(acc[:], w1_codes, w1_scales, 0, cols)
-            nc.scalar.copy(y_neg[0][:, cols], acc[:])
+            nc.scalar.activation(y_neg[0][:, cols], acc[:], COPY, scale=-1.0)
         y_acc = {}
         for t in range(1, PACK):
             y_acc[t] = psum.tile([P, S], F32, name=f"y{t}", tag=f"bank{t + 2}")
@@ -167,25 +192,25 @@ def tile_picked_redq_none_po_kernel(
         for b in blocks:
             turned_product(gap_acc, w1_codes, w1_scales, b, b == 0, False)
         gather_current(0, [slice(0, S)])
-        nc.scalar.copy(y_neg[1][:, :S], y_acc[1][:])
+        nc.scalar.activation(y_neg[1][:, :S], y_acc[1][:], COPY, scale=-1.0)
         gather_current(1, [slice(0, S)])
 
-        nc.scalar.activation(dealt_out(w2_bf, slice(W2_SPLIT, P)), dealt_in(w2_raw[1]), COPY)
-        w2_codes, w2_scales = quantize_weight(w2_bf, "w2")
+        nc.scalar.activation(dealt_out(w2_bf[1], slice(0, W2_SPLIT)), dealt_in(w2_raw[1]), COPY, scale=minus_one[:])
+        quantize_w2_half(1)
         for t in range(2, PACK):
             y_neg.append(late.tile([P, S], F32, name=f"y_neg{t}", offset=4 * S * (t - 2)))
-            nc.scalar.copy(y_neg[t][:], y_acc[t][:])
+            nc.scalar.activation(y_neg[t][:], y_acc[t][:], COPY, scale=-1.0)
             gather_current(t, halves)
 
         low = [keep.tile([P, S], F32, name=f"low{t}") for t in range(PACK)]
-        y_disc_late = keep.tile([P, 4, S], F32, name="y_disc", tag="w2_bf", align_bytes=64)
+        y_disc_late = keep.tile([P, 4, S], F32, name="y_disc", tag="second")
         y_disc = [y_disc_late[:, t, :] for t in range(last)]
 
         def clip(t):
             e_acc = psum.tile([P, S], F32, name=f"e{t}", tag=f"bank{(t + 6) % 8}")
             product(e_acc[:], w2_codes, w2_scales, t, slice(0, S))
             nc.scalar.activation(y_disc[t], y_neg[t][:, :S], COPY, scale=-DISCOUNT)
-            nc.vector.scalar_tensor_tensor(low[t][:], e_acc[:], DISCOUNT, y_disc[t], ALU.mult, ALU.min)
+            nc.vector.scalar_tensor_tensor(low[t][:], e_acc[:], -DISCOUNT, y_disc[t], ALU.mult, ALU.min)
 
         yt_neg = y_disc_late[:, last, :]
         excess = keep.tile([P, S], F32, name="excess")
@@ -237,13 +262,13 @@ def tile_picked_redq_none_po_kernel(
             nc.sync.dma_start(out_words[:, stages[h]], o_codes[:])
 
         clip(0)
+        for b in blocks:
+            turned_product(gap_acc, w2_codes, w2_scales, b, False, b == S // P - 1)
         clip(1)
         gather_next(0, 0)
         clip(2)
-        nc.scalar.copy(yt_neg, yt_acc[:])
-        for b in blocks:
-            turned_product(gap_acc, w2_codes, w2_scales, b, False, b == S // P - 1)
-        nc.scalar.activation(excess[:], gap_acc[:], RELU, scale=-1.0)
+        nc.scalar.activation(yt_neg, yt_acc[:], COPY, scale=-1.0)
+        nc.scalar.activation(excess[:], gap_acc[:], RELU)
         turn_back(yt_neg, True, False)
         turn_back(excess[:], False, True)
         nc.scalar.activation(low[last][:], low_acc[:], COPY, scale=discount[:])

@@ -51,8 +51,6 @@ def tile_picked_redq_none_po_kernel(
         nc.vector.memset(xs[:].bitcast(I32), 0)
         w1_raw = load_weight(w1, "w1_raw")
         nc.sync.dma_start(offs_sb[:], offs)
-        rw_col = keep.tile([P, PACK], F32, name="rw_col")
-        nc.scalar.dma_start(rw_col[:], rw[0].rearrange("(p b) -> p b", b=PACK))
         for q in range(4):
             nc.sync.dma_start(
                 xs[32 * q : 32 * q + 4, :].bitcast(I32), x_scales[0, 4 * q : 4 * q + 4, :].bitcast(I32)
@@ -67,14 +65,10 @@ def tile_picked_redq_none_po_kernel(
         ident = keep.tile([P, P], F32, name="ident")
         make_identity(nc, ident[:])
         nc.sync.dma_start(w2_raw[0][:], w2_rows[:, :, :w2_cut])
+        nc.sync.dma_start(rw_sb[:], rw)
         nc.sync.dma_start(cur_sb[:], cur)
         nc.sync.dma_start(w2_raw[1][:], w2_rows[:, :, w2_cut:])
         nc.sync.dma_start(nx_sb[:], nx)
-
-        rw_acc = psum.tile([P, PACK, P], F32, name="rw_acc", tag="bank7")
-        for b in range(PACK):
-            nc.tensor.transpose(rw_acc[:, b, :], rw_col[:, b : b + 1].to_broadcast([P, P]), ident[:])
-        nc.scalar.copy(rw_sb[:].rearrange("p (q b) -> p q b", b=PACK), rw_acc[:].rearrange("p b q -> p q b"))
 
         xq_s = keep.tile([P, S], U8, name="xq_s", align_bytes=64)
         xq_w = keep.tile([P, S], U32, name="xq_w", align_bytes=64)
@@ -142,24 +136,8 @@ def tile_picked_redq_none_po_kernel(
             nc.gpsimd.memset(y_neg[t][:, S:], 0.0)
         for cols in halves:
             nc.vector.tensor_copy(xq_w[:, cols], xw[:].bitcast(U32).indirect(offs_sb[:, entries(cols)]))
-        w2_bf = [
-            keep.tile([P, PACK * w2_cut], BF16, name="w2_bf0", align_bytes=64),
-            keep.tile([P, PACK * w2_cut], BF16, name="w2_bf1", align_bytes=64),
-        ]
-        w2_codes = keep.tile([P, N], U32, name="w2_codes", align_bytes=64)
-        w2_scales = keep.tile([P, N], U8, name="w2_scales", align_bytes=64)
-
-        def quantize_w2_half(h):
-            for t in range(PACK):
-                rows = slice(t * P + h * W2_SPLIT, t * P + (h + 1) * W2_SPLIT)
-                nc.vector.quantize_mx(
-                    out=w2_codes[:, rows].bitcast(FP8X4),
-                    scales=w2_scales[:, rows],
-                    in_=w2_bf[h][:, t * w2_cut : (t + 1) * w2_cut],
-                )
-
-        nc.vector.tensor_scalar_mul(dealt_out(w2_bf[0], slice(0, W2_SPLIT)), dealt_in(w2_raw[0]), -1.0)
-        quantize_w2_half(0)
+        w2_bf = keep.tile([P, PACK * N], BF16, name="w2_bf", align_bytes=64)
+        nc.vector.tensor_scalar_mul(dealt_out(w2_bf, slice(0, W2_SPLIT)), dealt_in(w2_raw[0]), -1.0)
         pieces = (halves[0], slice(HALF, HALF + QUARTER), slice(HALF + QUARTER, S))
         for i, cols in enumerate(pieces):
             acc = psum.tile([P, cols.stop - cols.start], F32, name=f"y0_{i}", tag=f"bank{i}")
@@ -195,8 +173,8 @@ def tile_picked_redq_none_po_kernel(
         nc.scalar.activation(y_neg[1][:, :S], y_acc[1][:], COPY, scale=-1.0)
         gather_current(1, [slice(0, S)])
 
-        nc.scalar.activation(dealt_out(w2_bf[1], slice(0, W2_SPLIT)), dealt_in(w2_raw[1]), COPY, scale=minus_one[:])
-        quantize_w2_half(1)
+        nc.scalar.activation(dealt_out(w2_bf, slice(W2_SPLIT, P)), dealt_in(w2_raw[1]), COPY, scale=minus_one[:])
+        w2_codes, w2_scales = quantize_weight(w2_bf, "w2")
         for t in range(2, PACK):
             y_neg.append(late.tile([P, S], F32, name=f"y_neg{t}", offset=4 * S * (t - 2)))
             nc.scalar.activation(y_neg[t][:], y_acc[t][:], COPY, scale=-1.0)

@@ -51,6 +51,8 @@ def tile_picked_redq_none_po_kernel(
         nc.vector.memset(xs[:].bitcast(I32), 0)
         w1_raw = load_weight(w1, "w1_raw")
         nc.sync.dma_start(offs_sb[:], offs)
+        rw_col = keep.tile([P, PACK], F32, name="rw_col")
+        nc.scalar.dma_start(rw_col[:], rw[0].rearrange("(p b) -> p b", b=PACK))
         for q in range(4):
             nc.sync.dma_start(
                 xs[32 * q : 32 * q + 4, :].bitcast(I32), x_scales[0, 4 * q : 4 * q + 4, :].bitcast(I32)
@@ -65,10 +67,14 @@ def tile_picked_redq_none_po_kernel(
         ident = keep.tile([P, P], F32, name="ident")
         make_identity(nc, ident[:])
         nc.sync.dma_start(w2_raw[0][:], w2_rows[:, :, :w2_cut])
-        nc.sync.dma_start(rw_sb[:], rw)
         nc.sync.dma_start(cur_sb[:], cur)
         nc.sync.dma_start(w2_raw[1][:], w2_rows[:, :, w2_cut:])
         nc.sync.dma_start(nx_sb[:], nx)
+
+        rw_acc = psum.tile([P, PACK, P], F32, name="rw_acc", tag="bank7")
+        for b in range(PACK):
+            nc.tensor.transpose(rw_acc[:, b, :], rw_col[:, b : b + 1].to_broadcast([P, P]), ident[:])
+        nc.scalar.copy(rw_sb[:].rearrange("p (q b) -> p q b", b=PACK), rw_acc[:].rearrange("p b q -> p q b"))
 
         xq_s = keep.tile([P, S], U8, name="xq_s", align_bytes=64)
         xq_w = keep.tile([P, S], U32, name="xq_w", align_bytes=64)

@@ -51,8 +51,9 @@ def tile_picked_redq_none_po_kernel(
         nc.vector.memset(xs[:].bitcast(I32), 0)
         w1_raw = load_weight(w1, "w1_raw")
         nc.sync.dma_start(offs_sb[:], offs)
-        rw_col = keep.tile([P, PACK], F32, name="rw_col")
-        nc.scalar.dma_start(rw_col[:], rw[0].rearrange("(p b) -> p b", b=PACK))
+        rw_quarters = keep.tile([P, P], F32, name="rw_quarters")
+        nc.gpsimd.memset(rw_quarters[:], 0.0)
+        nc.scalar.dma_start(rw_quarters[:PACK, :], rw[0].rearrange("(b c) -> b c", b=PACK))
         for q in range(4):
             nc.sync.dma_start(
                 xs[32 * q : 32 * q + 4, :].bitcast(I32), x_scales[0, 4 * q : 4 * q + 4, :].bitcast(I32)
@@ -71,10 +72,14 @@ def tile_picked_redq_none_po_kernel(
         nc.sync.dma_start(w2_raw[1][:], w2_rows[:, :, w2_cut:])
         nc.sync.dma_start(nx_sb[:], nx)
 
-        rw_acc = psum.tile([P, PACK, P], F32, name="rw_acc", tag="bank7")
+        rw_turned = psum.tile([P, P], F32, name="rw_turned", tag="bank6")
+        nc.tensor.transpose(rw_turned[:], rw_quarters[:], ident[:])
+        rw_col = keep.tile([P, PACK], F32, name="rw_col")
+        nc.scalar.copy(rw_col[:], rw_turned[:, :PACK])
+        rw_acc = psum.tile([P, S], F32, name="rw_acc", tag="bank7")
         for b in range(PACK):
-            nc.tensor.transpose(rw_acc[:, b, :], rw_col[:, b : b + 1].to_broadcast([P, P]), ident[:])
-        nc.scalar.copy(rw_sb[:].rearrange("p (q b) -> p q b", b=PACK), rw_acc[:].rearrange("p b q -> p q b"))
+            nc.tensor.transpose(rw_acc[:, b * P : (b + 1) * P], rw_col[:, b : b + 1].to_broadcast([P, P]), ident[:])
+        nc.scalar.copy(rw_sb[:], rw_acc[:])
 
         xq_s = keep.tile([P, S], U8, name="xq_s", align_bytes=64)
         xq_w = keep.tile([P, S], U32, name="xq_w", align_bytes=64)

@@ -24,7 +24,7 @@ W1_SPLIT = 52
 W2_SPLIT = 64
 HALF = 256
 QUARTER = 128
-END_SPLIT = 64
+END_SPLIT = 80
 
 
 def tile_picked_redq_none_po_kernel(
@@ -119,17 +119,14 @@ def tile_picked_redq_none_po_kernel(
         nc.vector.tensor_copy(xq_s[:], xs[:].indirect(offs_sb[:]))
         w1_codes, w1_scales = quantize_weight(w1_bf, "w1")
 
-        base = keep.tile([P, PACK - 1, S], F32, name="base")
+        base = keep.tile([P, PACK, S], F32, name="base")
         base_last = [late.tile([P, HALF], F32, name=f"base_last{h}", offset=(16 + 4 * h) * S) for h in range(2)]
-        discount = late.tile([P, 1], F32, name="discount", offset=24 * S)
-        nc.gpsimd.memset(discount[:], 1.0)
-        nc.gpsimd.tensor_scalar(discount[:], discount[:], -DISCOUNT, 0.0, ALU.mult, ALU.add)
 
         minus_one = keep.tile([P, 1], F32, name="minus_one", tag="second")
         nc.gpsimd.memset(minus_one[:], -1.0)
 
         def base_cols(t, cols):
-            if t < PACK - 1:
+            if t != 2:
                 return base[:, t, cols]
             h = cols.start // HALF
             return base_last[h][:, cols.start - h * HALF : cols.stop - h * HALF]
@@ -150,39 +147,61 @@ def tile_picked_redq_none_po_kernel(
         w2_bf = keep.tile([P, PACK * N], BF16, name="w2_bf", align_bytes=64)
         nc.vector.tensor_scalar_mul(dealt_out(w2_bf, slice(0, W2_SPLIT)), dealt_in(w2_raw[0]), -1.0)
         pieces = (halves[0], slice(HALF, HALF + QUARTER), slice(HALF + QUARTER, S))
+        y_disc0 = keep.tile([P, S], F32, name="y_disc0")
+        first = []
+        y_acc = {t: psum.tile([P, S], F32, name=f"y{t}", tag=f"bank{t + 2}") for t in range(1, PACK)}
         for i, cols in enumerate(pieces):
-            acc = psum.tile([P, cols.stop - cols.start], F32, name=f"y0_{i}", tag=f"bank{i}")
-            product(acc[:], w1_codes, w1_scales, 0, cols)
-            nc.scalar.activation(y_neg[0][:, cols], acc[:], COPY, scale=-1.0)
-        y_acc = {}
-        for t in range(1, PACK):
-            y_acc[t] = psum.tile([P, S], F32, name=f"y{t}", tag=f"bank{t + 2}")
+            first.append(psum.tile([P, cols.stop - cols.start], F32, name=f"y0_{i}", tag=f"bank{i}"))
+            product(first[i][:], w1_codes, w1_scales, 0, cols)
+            if i == 0:
+                product(y_acc[1][:, cols], w1_codes, w1_scales, 1, cols)
+            nc.scalar.activation(y_neg[0][:, cols], first[i][:], COPY, scale=-1.0)
+        for i, cols in enumerate(pieces):
+            nc.scalar.activation(y_disc0[:, cols], first[i][:], COPY, scale=DISCOUNT)
+        product(y_acc[1][:, halves[1]], w1_codes, w1_scales, 1, halves[1])
+        for t in range(2, PACK):
             product(y_acc[t][:], w1_codes, w1_scales, t, slice(0, S))
-        last = PACK - 1
-        last_rows = slice(last * P, N)
+        turned = range(1, 3)
+        blocks = [slice(b * P, (b + 1) * P) for b in range(S // P)]
 
-        def turned_product(acc, codes, scales, b, start, stop):
-            tokens = slice(b * P, (b + 1) * P)
-            nc.tensor.matmul_mx(
-                out=acc[:, tokens],
-                lhsT=xq_w[:, tokens].bitcast(FP8X4),
-                lhsT_scale=xq_s[:, tokens],
-                rhs=codes[:, last_rows].bitcast(FP8X4),
-                rhs_scale=scales[:, last_rows],
-                start=start,
-                stop=stop,
-            )
+        def turned_product(acc, codes, scales, t, start, stop):
+            rows = slice(t * P, (t + 1) * P)
+            for tokens in blocks:
+                nc.tensor.matmul_mx(
+                    out=acc[:, tokens],
+                    lhsT=xq_w[:, tokens].bitcast(FP8X4),
+                    lhsT_scale=xq_s[:, tokens],
+                    rhs=codes[:, rows].bitcast(FP8X4),
+                    rhs_scale=scales[:, rows],
+                    start=start and tokens.start == 0,
+                    stop=stop and tokens.stop == S,
+                )
 
-        blocks = range(S // P)
-        yt_acc = psum.tile([P, S], F32, name="yt_acc", tag="bank1")
-        gap_acc = psum.tile([P, S], F32, name="gap_acc", tag="bank2")
-        for b in blocks:
-            turned_product(yt_acc, w1_codes, w1_scales, b, True, True)
-        for b in blocks:
-            turned_product(gap_acc, w1_codes, w1_scales, b, b == 0, False)
+        def turn(acc, src, start, stop):
+            for cols in blocks:
+                nc.tensor.matmul(
+                    acc[:, cols],
+                    lhsT=src[:, cols],
+                    rhs=ident[:],
+                    start=start and cols.start == 0,
+                    stop=stop and cols.stop == S,
+                    is_transpose=True,
+                )
+
+        gap_acc = {}
+        for t in turned:
+            gap_acc[t] = psum.tile([P, S], F32, name=f"gap_acc{t}", tag=f"bank{t}")
+            turned_product(gap_acc[t], w1_codes, w1_scales, t, True, False)
         gather_current(0, [slice(0, S)])
         nc.scalar.activation(y_neg[1][:, :S], y_acc[1][:], COPY, scale=-1.0)
         gather_current(1, [slice(0, S)])
+        yt_acc = {}
+
+        def turn_y(t):
+            yt_acc[t] = psum.tile([P, S], F32, name=f"yt_acc{t}", tag=f"bank{t + 5}")
+            turn(yt_acc[t], y_neg[t], True, True)
+
+        turn_y(1)
 
         nc.scalar.activation(dealt_out(w2_bf, slice(W2_SPLIT, P)), dealt_in(w2_raw[1]), COPY, scale=minus_one[:])
         w2_codes, w2_scales = quantize_weight(w2_bf, "w2")
@@ -190,32 +209,27 @@ def tile_picked_redq_none_po_kernel(
             y_neg.append(late.tile([P, S], F32, name=f"y_neg{t}", offset=4 * S * (t - 2)))
             nc.scalar.activation(y_neg[t][:], y_acc[t][:], COPY, scale=-1.0)
             gather_current(t, halves)
+        turn_y(2)
 
         low = [keep.tile([P, S], F32, name=f"low{t}") for t in range(PACK)]
-        y_disc_late = keep.tile([P, 4, S], F32, name="y_disc", tag="second")
-        y_disc = [y_disc_late[:, t, :] for t in range(last)]
+        second = keep.tile([P, PACK, S], F32, name="second", tag="second")
 
-        def clip(t):
-            e_acc = psum.tile([P, S], F32, name=f"e{t}", tag=f"bank{(t + 6) % 8}")
+        def clip(t, y_disc):
+            e_acc = psum.tile([P, S], F32, name=f"e{t}", tag=f"bank{t}")
             product(e_acc[:], w2_codes, w2_scales, t, slice(0, S))
-            nc.scalar.activation(y_disc[t], y_neg[t][:, :S], COPY, scale=-DISCOUNT)
-            nc.vector.scalar_tensor_tensor(low[t][:], e_acc[:], -DISCOUNT, y_disc[t], ALU.mult, ALU.min)
+            nc.vector.scalar_tensor_tensor(low[t][:], e_acc[:], -DISCOUNT, y_disc, ALU.mult, ALU.min)
 
-        yt_neg = y_disc_late[:, last, :]
-        excess = keep.tile([P, S], F32, name="excess")
-        low_acc = psum.tile([P, S], F32, name="low_acc", tag="bank3")
+        excess = keep.tile([P, PACK, S], F32, name="excess")
 
-        def turn_back(src, start, stop):
-            for b in blocks:
-                tokens = slice(b * P, (b + 1) * P)
-                nc.tensor.matmul(
-                    low_acc[:, tokens],
-                    lhsT=src[:, tokens],
-                    rhs=ident[:],
-                    start=start and b == 0,
-                    stop=stop and b == S // P - 1,
-                    is_transpose=True,
-                )
+        def exceed(t):
+            turned_product(gap_acc[t], w2_codes, w2_scales, t, False, True)
+            nc.scalar.activation(excess[:, t, :], gap_acc[t][:], RELU)
+
+        def clip_turned(t, scale):
+            low_acc = psum.tile([P, S], F32, name=f"low_acc{t}", tag=f"bank{t + 3}")
+            turn(low_acc, second[:, t, :], True, False)
+            turn(low_acc, excess[:, t, :], False, True)
+            nc.scalar.activation(low[t][:], low_acc[:], COPY, scale=scale)
 
         out_rows = out_0.rearrange("(p t) j -> p t j", t=PACK)
         out_words = out_1[0].rearrange("p n t -> p (n t)").bitcast(I32)
@@ -223,8 +237,8 @@ def tile_picked_redq_none_po_kernel(
         stages = (halves[0], slice(HALF, HALF + QUARTER), slice(HALF + QUARTER, S))
         widths = [cols.stop - cols.start for cols in stages]
         td = [
-            keep.tile([P, PACK, HALF], F32, name="td0"),
-            late.tile([P, PACK, QUARTER], F32, name="td1", offset=24 * S),
+            late.tile([P, PACK, HALF], F32, name="td0", offset=4 * S + 64),
+            late.tile([P, PACK, QUARTER], F32, name="td1", offset=64),
             late.tile([P, PACK, QUARTER], F32, name="td2", offset=16 * S),
         ]
         td_bf = [keep.tile([P, w, PACK], BF16, name=f"td_bf{h}", align_bytes=64) for h, w in enumerate(widths)]
@@ -250,26 +264,29 @@ def tile_picked_redq_none_po_kernel(
             )
             nc.sync.dma_start(out_words[:, stages[h]], o_codes[:])
 
-        clip(0)
-        for b in blocks:
-            turned_product(gap_acc, w2_codes, w2_scales, b, False, b == S // P - 1)
-        clip(1)
-        gather_next(0, 0)
-        clip(2)
-        nc.scalar.activation(yt_neg, yt_acc[:], COPY, scale=-1.0)
-        nc.scalar.activation(excess[:], gap_acc[:], RELU)
-        turn_back(yt_neg, True, False)
-        turn_back(excess[:], False, True)
-        nc.scalar.activation(low[last][:], low_acc[:], COPY, scale=discount[:])
-        for t in range(1, PACK):
+        order = (0, 3, 1, 2)
+        clip(0, y_disc0[:])
+        nc.scalar.activation(second[:, 3, :], y_neg[3][:], COPY, scale=-DISCOUNT)
+        clip(3, second[:, 3, :])
+        nc.scalar.copy(second[:, 1, :], yt_acc[1][:])
+        exceed(1)
+        nc.scalar.copy(second[:, 2, :], yt_acc[2][:])
+        exceed(2)
+        clip_turned(1, -DISCOUNT)
+        clip_turned(2, -DISCOUNT)
+        for h in range(2):
+            for t in order[:2]:
+                gather_next(t, h)
+            nc.sync.dma_start(out_rows[:, 0:PACK:3, stages[h]], td[h][:, 0:PACK:3, :])
+        for t in order[2:]:
             gather_next(t, 0)
-        nc.sync.dma_start(out_rows[:, :, stages[0]], td[0][:])
+        nc.sync.dma_start(out_rows[:, 1:3, stages[0]], td[0][:, 1:3, :])
         round_result(0, slice(0, widths[0]), nc.scalar.copy)
-        for t in range(PACK):
+        for t in order[2:]:
             gather_next(t, 1)
-        nc.sync.dma_start(out_rows[:, :, stages[1]], td[1][:])
+        nc.sync.dma_start(out_rows[:, 1:3, stages[1]], td[1][:, 1:3, :])
         round_result(1, slice(0, widths[1]), nc.scalar.copy)
-        for t in range(PACK):
+        for t in order:
             gather_next(t, 2)
         nc.sync.dma_start(out_rows[:, :, stages[2]], td[2][:])
         quantize_result(0)

@@ -24,7 +24,11 @@ W1_SPLIT = 52
 W2_SPLIT = 64
 HALF = 256
 QUARTER = 128
-END_SPLIT = 80
+END_SPLIT = 64
+FIRST, SECOND, THIRD, FOURTH = 0, 2, 3, 1
+PLAIN = (FIRST, FOURTH)
+TURNED = (SECOND, THIRD)
+ROW = 4 * S
 
 
 def tile_picked_redq_none_po_kernel(
@@ -36,6 +40,9 @@ def tile_picked_redq_none_po_kernel(
         late = ctx.enter_context(tc.tile_pool(name="late", bufs=1))
         psum = ctx.enter_context(tc.psum_pool(name="psum", bufs=1))
 
+        def bank(name, number, width=S):
+            return psum.tile([P, width], F32, name=name, tag=f"bank{number}")
+
         offs_sb = keep.tile([P, S // 16], U16, name="offs_sb")
         cur_sb = keep.tile([P, S // 16], U16, name="cur_sb")
         nx_sb = keep.tile([P, S // 16], U16, name="nx_sb")
@@ -43,13 +50,9 @@ def tile_picked_redq_none_po_kernel(
         xs = keep.tile([P, T], U8, name="xs", align_bytes=64)
         rw_sb = keep.tile([P, S], F32, name="rw_sb")
 
-        def load_weight(w, name):
-            raw = keep.tile([P, PACK, N], F32, name=name, tag="w_raw")
-            nc.sync.dma_start(raw[:], w.rearrange("(p j) c -> p j c", j=PACK))
-            return raw
-
         nc.vector.memset(xs[:].bitcast(I32), 0)
-        w1_raw = load_weight(w1, "w1_raw")
+        w1_raw = keep.tile([P, PACK, N], F32, name="w1_raw")
+        nc.sync.dma_start(w1_raw[:], w1.rearrange("(p j) c -> p j c", j=PACK))
         nc.sync.dma_start(offs_sb[:], offs)
         rw_quarters = keep.tile([P, P], F32, name="rw_quarters")
         nc.gpsimd.memset(rw_quarters[:], 0.0)
@@ -61,24 +64,26 @@ def tile_picked_redq_none_po_kernel(
         nc.sync.dma_start(xw[:], x_words[0].rearrange("p n t -> p (n t)").bitcast(I32))
         w2_rows = w2.rearrange("(p j) c -> p j c", j=PACK)
         w2_cut = PACK * W2_SPLIT
-        w2_raw = [
-            keep.tile([P, PACK, w2_cut], F32, name="w2_raw0"),
-            late.tile([P, PACK, N - w2_cut], F32, name="w2_raw1", offset=0),
-        ]
+        w2_left = keep.tile([P, PACK, w2_cut], F32, name="w2_left")
+        w2_right = late.tile([P, PACK, N - w2_cut], F32, name="w2_right", offset=0)
         ident = keep.tile([P, P], F32, name="ident")
         make_identity(nc, ident[:])
-        nc.sync.dma_start(w2_raw[0][:], w2_rows[:, :, :w2_cut])
+        nc.sync.dma_start(w2_left[:], w2_rows[:, :, :w2_cut])
         nc.sync.dma_start(cur_sb[:], cur)
-        nc.sync.dma_start(w2_raw[1][:], w2_rows[:, :, w2_cut:])
+        nc.sync.dma_start(w2_right[:], w2_rows[:, :, w2_cut:])
         nc.sync.dma_start(nx_sb[:], nx)
 
-        rw_turned = psum.tile([P, P], F32, name="rw_turned", tag="bank6")
+        halves = [slice(h * HALF, (h + 1) * HALF) for h in range(S // HALF)]
+        blocks = [slice(b * P, (b + 1) * P) for b in range(S // P)]
+        stages = (halves[0], slice(HALF, HALF + QUARTER), slice(HALF + QUARTER, S))
+
+        rw_turned = bank("rw_turned", 6, P)
         nc.tensor.transpose(rw_turned[:], rw_quarters[:], ident[:])
         rw_col = keep.tile([P, PACK], F32, name="rw_col")
         nc.scalar.copy(rw_col[:], rw_turned[:, :PACK])
-        rw_acc = psum.tile([P, S], F32, name="rw_acc", tag="bank7")
-        for b in range(PACK):
-            nc.tensor.transpose(rw_acc[:, b * P : (b + 1) * P], rw_col[:, b : b + 1].to_broadcast([P, P]), ident[:])
+        rw_acc = bank("rw_acc", 7)
+        for b, cols in enumerate(blocks):
+            nc.tensor.transpose(rw_acc[:, cols], rw_col[:, b : b + 1].to_broadcast([P, P]), ident[:])
         nc.scalar.copy(rw_sb[:], rw_acc[:])
 
         xq_s = keep.tile([P, S], U8, name="xq_s", align_bytes=64)
@@ -96,83 +101,27 @@ def tile_picked_redq_none_po_kernel(
             nc.vector.quantize_mx(out=codes[:].bitcast(FP8X4), scales=scales[:], in_=grouped[:])
             return codes, scales
 
-        def product(acc, codes, scales, t, cols):
-            rows = slice(t * P, (t + 1) * P)
+        def product(acc, weight, t, cols):
+            codes, scales = weight
             nc.tensor.matmul_mx(
                 out=acc,
-                lhsT=codes[:, rows].bitcast(FP8X4),
-                lhsT_scale=scales[:, rows],
+                lhsT=codes[:, blocks[t]].bitcast(FP8X4),
+                lhsT_scale=scales[:, blocks[t]],
                 rhs=xq_w[:, cols].bitcast(FP8X4),
                 rhs_scale=xq_s[:, cols],
                 start=True,
                 stop=True,
             )
 
-        halves = [slice(h * HALF, (h + 1) * HALF) for h in range(S // HALF)]
-
-        def entries(cols):
-            return slice(cols.start // 16, cols.stop // 16)
-
-        w1_bf = keep.tile([P, PACK * N], BF16, name="w1_bf", align_bytes=64)
-        nc.vector.tensor_copy(dealt_out(w1_bf, slice(0, W1_SPLIT)), dealt_in(w1_raw)[:, :W1_SPLIT])
-        nc.scalar.activation(dealt_out(w1_bf, slice(W1_SPLIT, P)), dealt_in(w1_raw)[:, W1_SPLIT:], COPY)
-        nc.vector.tensor_copy(xq_s[:], xs[:].indirect(offs_sb[:]))
-        w1_codes, w1_scales = quantize_weight(w1_bf, "w1")
-
-        base = keep.tile([P, PACK, S], F32, name="base")
-        base_last = [late.tile([P, HALF], F32, name=f"base_last{h}", offset=(16 + 4 * h) * S) for h in range(2)]
-
-        minus_one = keep.tile([P, 1], F32, name="minus_one", tag="second")
-        nc.gpsimd.memset(minus_one[:], -1.0)
-
-        def base_cols(t, cols):
-            if t != 2:
-                return base[:, t, cols]
-            h = cols.start // HALF
-            return base_last[h][:, cols.start - h * HALF : cols.stop - h * HALF]
-
-        y_neg = []
-
-        def gather_current(t, pieces):
-            for cols in pieces:
-                nc.vector.tensor_tensor(
-                    base_cols(t, cols), y_neg[t][:].indirect(cur_sb[:, entries(cols)]), rw_sb[:, cols], ALU.add
-                )
-
-        for t in range(2):
-            y_neg.append(keep.tile([P, 2 * S], F32, name=f"y_neg{t}"))
-            nc.gpsimd.memset(y_neg[t][:, S:], 0.0)
-        for cols in halves:
-            nc.vector.tensor_copy(xq_w[:, cols], xw[:].bitcast(U32).indirect(offs_sb[:, entries(cols)]))
-        w2_bf = keep.tile([P, PACK * N], BF16, name="w2_bf", align_bytes=64)
-        nc.vector.tensor_scalar_mul(dealt_out(w2_bf, slice(0, W2_SPLIT)), dealt_in(w2_raw[0]), -1.0)
-        pieces = (halves[0], slice(HALF, HALF + QUARTER), slice(HALF + QUARTER, S))
-        y_disc0 = keep.tile([P, S], F32, name="y_disc0")
-        first = []
-        y_acc = {t: psum.tile([P, S], F32, name=f"y{t}", tag=f"bank{t + 2}") for t in range(1, PACK)}
-        for i, cols in enumerate(pieces):
-            first.append(psum.tile([P, cols.stop - cols.start], F32, name=f"y0_{i}", tag=f"bank{i}"))
-            product(first[i][:], w1_codes, w1_scales, 0, cols)
-            if i == 0:
-                product(y_acc[1][:, cols], w1_codes, w1_scales, 1, cols)
-            nc.scalar.activation(y_neg[0][:, cols], first[i][:], COPY, scale=-1.0)
-        for i, cols in enumerate(pieces):
-            nc.scalar.activation(y_disc0[:, cols], first[i][:], COPY, scale=DISCOUNT)
-        product(y_acc[1][:, halves[1]], w1_codes, w1_scales, 1, halves[1])
-        for t in range(2, PACK):
-            product(y_acc[t][:], w1_codes, w1_scales, t, slice(0, S))
-        turned = range(1, 3)
-        blocks = [slice(b * P, (b + 1) * P) for b in range(S // P)]
-
-        def turned_product(acc, codes, scales, t, start, stop):
-            rows = slice(t * P, (t + 1) * P)
+        def turned_product(acc, weight, t, start, stop):
+            codes, scales = weight
             for tokens in blocks:
                 nc.tensor.matmul_mx(
                     out=acc[:, tokens],
                     lhsT=xq_w[:, tokens].bitcast(FP8X4),
                     lhsT_scale=xq_s[:, tokens],
-                    rhs=codes[:, rows].bitcast(FP8X4),
-                    rhs_scale=scales[:, rows],
+                    rhs=codes[:, blocks[t]].bitcast(FP8X4),
+                    rhs_scale=scales[:, blocks[t]],
                     start=start and tokens.start == 0,
                     stop=stop and tokens.stop == S,
                 )
@@ -188,111 +137,149 @@ def tile_picked_redq_none_po_kernel(
                     is_transpose=True,
                 )
 
-        gap_acc = {}
-        for t in turned:
-            gap_acc[t] = psum.tile([P, S], F32, name=f"gap_acc{t}", tag=f"bank{t}")
-            turned_product(gap_acc[t], w1_codes, w1_scales, t, True, False)
-        gather_current(0, [slice(0, S)])
-        nc.scalar.activation(y_neg[1][:, :S], y_acc[1][:], COPY, scale=-1.0)
-        gather_current(1, [slice(0, S)])
-        yt_acc = {}
+        def entries(cols):
+            return slice(cols.start // 16, cols.stop // 16)
 
-        def turn_y(t):
-            yt_acc[t] = psum.tile([P, S], F32, name=f"yt_acc{t}", tag=f"bank{t + 5}")
-            turn(yt_acc[t], y_neg[t], True, True)
+        w1_bf = keep.tile([P, PACK * N], BF16, name="w1_bf", align_bytes=64)
+        nc.vector.tensor_copy(dealt_out(w1_bf, slice(0, W1_SPLIT)), dealt_in(w1_raw)[:, :W1_SPLIT])
+        nc.scalar.activation(dealt_out(w1_bf, slice(W1_SPLIT, P)), dealt_in(w1_raw)[:, W1_SPLIT:], COPY)
+        nc.vector.tensor_copy(xq_s[:], xs[:].indirect(offs_sb[:]))
+        w1_q = quantize_weight(w1_bf, "w1")
 
-        turn_y(1)
+        base = keep.tile([P, PACK, S], F32, name="base")
+        base_third = [late.tile([P, HALF], F32, name=f"base_third{h}", offset=(4 + h) * ROW) for h in range(2)]
+        discount = late.tile([P, 32], F32, name="discount", offset=6 * ROW)
+        nc.gpsimd.memset(discount[:], 1.0)
+        nc.gpsimd.tensor_scalar(discount[:], discount[:], -DISCOUNT, 0.0, ALU.mult, ALU.add)
+        minus_one = keep.tile([P, 1], F32, name="minus_one", tag="second")
+        nc.gpsimd.memset(minus_one[:], -1.0)
 
-        nc.scalar.activation(dealt_out(w2_bf, slice(W2_SPLIT, P)), dealt_in(w2_raw[1]), COPY, scale=minus_one[:])
-        w2_codes, w2_scales = quantize_weight(w2_bf, "w2")
-        for t in range(2, PACK):
-            y_neg.append(late.tile([P, S], F32, name=f"y_neg{t}", offset=4 * S * (t - 2)))
+        def base_cols(t, cols):
+            if t != THIRD:
+                return base[:, t, cols]
+            h = cols.start // HALF
+            return base_third[h][:, cols.start - h * HALF : cols.stop - h * HALF]
+
+        y_neg = {}
+
+        def gather_current(t, pieces):
+            for cols in pieces:
+                nc.vector.tensor_tensor(
+                    base_cols(t, cols), y_neg[t][:].indirect(cur_sb[:, entries(cols)]), rw_sb[:, cols], ALU.add
+                )
+
+        for t in (FIRST, SECOND):
+            y_neg[t] = keep.tile([P, 2 * S], F32, name=f"y_neg{t}")
+            nc.gpsimd.memset(y_neg[t][:, S:], 0.0)
+        for cols in halves:
+            nc.vector.tensor_copy(xq_w[:, cols], xw[:].bitcast(U32).indirect(offs_sb[:, entries(cols)]))
+        w2_bf = keep.tile([P, PACK * N], BF16, name="w2_bf", align_bytes=64)
+        nc.vector.tensor_scalar_mul(dealt_out(w2_bf, slice(0, W2_SPLIT)), dealt_in(w2_left), -1.0)
+
+        y_acc = {t: bank(f"y{t}", number) for t, number in ((SECOND, 3), (THIRD, 4), (FOURTH, 5))}
+        y_first = []
+        for i, cols in enumerate(stages):
+            y_first.append(bank(f"y_first{i}", i, cols.stop - cols.start))
+            product(y_first[i][:], w1_q, FIRST, cols)
+            if cols == halves[0]:
+                product(y_acc[SECOND][:, cols], w1_q, SECOND, cols)
+            nc.scalar.activation(y_neg[FIRST][:, cols], y_first[i][:], COPY, scale=-1.0)
+        product(y_acc[SECOND][:, halves[1]], w1_q, SECOND, halves[1])
+        for t in (THIRD, FOURTH):
+            product(y_acc[t][:], w1_q, t, slice(0, S))
+        gap_acc = {t: bank(f"gap{t}", number) for t, number in ((SECOND, 1), (THIRD, 2))}
+        for t in TURNED:
+            turned_product(gap_acc[t], w1_q, t, True, False)
+        gather_current(FIRST, [slice(0, S)])
+        nc.scalar.activation(y_neg[SECOND][:, :S], y_acc[SECOND][:], COPY, scale=-1.0)
+        gather_current(SECOND, [slice(0, S)])
+        yt_acc = {t: bank(f"yt{t}", number) for t, number in ((SECOND, 6), (THIRD, 7))}
+        turn(yt_acc[SECOND], y_neg[SECOND], True, True)
+
+        nc.scalar.activation(dealt_out(w2_bf, slice(W2_SPLIT, P)), dealt_in(w2_right), COPY, scale=minus_one[:])
+        w2_q = quantize_weight(w2_bf, "w2")
+        for i, t in enumerate((THIRD, FOURTH)):
+            y_neg[t] = late.tile([P, S], F32, name=f"y_neg{t}", offset=i * ROW)
             nc.scalar.activation(y_neg[t][:], y_acc[t][:], COPY, scale=-1.0)
             gather_current(t, halves)
-        turn_y(2)
+        turn(yt_acc[THIRD], y_neg[THIRD], True, True)
 
         low = [keep.tile([P, S], F32, name=f"low{t}") for t in range(PACK)]
         second = keep.tile([P, PACK, S], F32, name="second", tag="second")
-
-        def clip(t, y_disc):
-            e_acc = psum.tile([P, S], F32, name=f"e{t}", tag=f"bank{t}")
-            product(e_acc[:], w2_codes, w2_scales, t, slice(0, S))
-            nc.vector.scalar_tensor_tensor(low[t][:], e_acc[:], -DISCOUNT, y_disc, ALU.mult, ALU.min)
-
         excess = keep.tile([P, PACK, S], F32, name="excess")
 
-        def exceed(t):
-            turned_product(gap_acc[t], w2_codes, w2_scales, t, False, True)
-            nc.scalar.activation(excess[:, t, :], gap_acc[t][:], RELU)
+        def clip(t, number, y_disc):
+            e_acc = bank(f"e{t}", number)
+            product(e_acc[:], w2_q, t, slice(0, S))
+            nc.vector.scalar_tensor_tensor(low[t][:], e_acc[:], -DISCOUNT, y_disc, ALU.mult, ALU.min)
 
-        def clip_turned(t, scale):
-            low_acc = psum.tile([P, S], F32, name=f"low_acc{t}", tag=f"bank{t + 3}")
+        def clip_turned(t, number, scale):
+            low_acc = bank(f"low_acc{t}", number)
             turn(low_acc, second[:, t, :], True, False)
             turn(low_acc, excess[:, t, :], False, True)
             nc.scalar.activation(low[t][:], low_acc[:], COPY, scale=scale)
 
-        out_rows = out_0.rearrange("(p t) j -> p t j", t=PACK)
+        for t, number in ((FIRST, 0), (FOURTH, 3)):
+            nc.scalar.activation(second[:, t, :], y_neg[t][:, :S], COPY, scale=-DISCOUNT)
+            clip(t, number, second[:, t, :])
+        for t in TURNED:
+            nc.scalar.copy(second[:, t, :], yt_acc[t][:])
+            turned_product(gap_acc[t], w2_q, t, False, True)
+            nc.scalar.activation(excess[:, t, :], gap_acc[t][:], RELU)
+        clip_turned(SECOND, 4, -DISCOUNT)
+        clip_turned(THIRD, 5, discount[:, :1])
+
+        out_rows = out_0.rearrange("(p u t) j -> p u t j", u=2, t=2)
         out_words = out_1[0].rearrange("p n t -> p (n t)").bitcast(I32)
         o_scales = keep.tile([P, S], U8, name="o_scales", align_bytes=64)
-        stages = (halves[0], slice(HALF, HALF + QUARTER), slice(HALF + QUARTER, S))
         widths = [cols.stop - cols.start for cols in stages]
-        td = [
-            late.tile([P, PACK, HALF], F32, name="td0", offset=4 * S + 64),
-            late.tile([P, PACK, QUARTER], F32, name="td1", offset=64),
-            late.tile([P, PACK, QUARTER], F32, name="td2", offset=16 * S),
-        ]
-        td_bf = [keep.tile([P, w, PACK], BF16, name=f"td_bf{h}", align_bytes=64) for h, w in enumerate(widths)]
+        td_last = late.tile([P, 2, 2, QUARTER], F32, name="td_last", offset=4 * ROW)
+        td = {
+            (0, 0): late.tile([P, 2, HALF], F32, name="td00", offset=ROW + 64)[:],
+            (1, 0): late.tile([P, 2, QUARTER], F32, name="td10", offset=ROW // 2 + 64)[:],
+            (0, 1): keep.tile([P, 2, HALF], F32, name="td01")[:],
+            (1, 1): late.tile([P, 2, QUARTER], F32, name="td11", offset=6 * ROW + 64 - ROW // 2)[:],
+            (2, 0): td_last[:, 0],
+            (2, 1): td_last[:, 1],
+        }
+        bf_early = late.tile([P, HALF + QUARTER, 2, 2], BF16, name="bf_early", offset=6 * ROW + 64, align_bytes=64)
+        bf_last = keep.tile([P, QUARTER, 2, 2], BF16, name="bf_last", align_bytes=64)
+        td_bf = [bf_early[:, :HALF], bf_early[:, HALF:], bf_last[:]]
 
-        def gather_next(t, h):
+        def gather_next(h, u):
             cols = stages[h]
-            nc.vector.tensor_tensor(
-                td[h][:, t, :], low[t][:].indirect(nx_sb[:, entries(cols)]), base_cols(t, cols), ALU.add
-            )
+            for t in (PLAIN, TURNED)[u]:
+                nc.vector.tensor_tensor(
+                    td[h, u][:, t % 2, :], low[t][:].indirect(nx_sb[:, entries(cols)]), base_cols(t, cols), ALU.add
+                )
 
-        def round_result(h, part, copy):
-            copy(
-                td_bf[h][:, part, :].rearrange("p (c i) t -> p c t i", i=4),
-                td[h][:, :, part].rearrange("p t (c i) -> p c t i", i=4),
-            )
+        def round_pair(h, u, part, copy):
+            copy(td_bf[h][:, part, u, :], td[h, u][:, :, part].rearrange("p t j -> p j t"))
 
         def quantize_result(h):
             o_codes = keep.tile([P, widths[h]], I32, name=f"o_codes{h}", align_bytes=64)
             nc.vector.quantize_mx(
                 out=o_codes[:].bitcast(FP8X4),
                 scales=o_scales[:, stages[h]],
-                in_=td_bf[h][:].rearrange("p j t -> p (j t)"),
+                in_=td_bf[h].rearrange("p j u t -> p (j u t)"),
             )
             nc.sync.dma_start(out_words[:, stages[h]], o_codes[:])
 
-        order = (0, 3, 1, 2)
-        clip(0, y_disc0[:])
-        nc.scalar.activation(second[:, 3, :], y_neg[3][:], COPY, scale=-DISCOUNT)
-        clip(3, second[:, 3, :])
-        nc.scalar.copy(second[:, 1, :], yt_acc[1][:])
-        exceed(1)
-        nc.scalar.copy(second[:, 2, :], yt_acc[2][:])
-        exceed(2)
-        clip_turned(1, -DISCOUNT)
-        clip_turned(2, -DISCOUNT)
-        for h in range(2):
-            for t in order[:2]:
-                gather_next(t, h)
-            nc.sync.dma_start(out_rows[:, 0:PACK:3, stages[h]], td[h][:, 0:PACK:3, :])
-        for t in order[2:]:
-            gather_next(t, 0)
-        nc.sync.dma_start(out_rows[:, 1:3, stages[0]], td[0][:, 1:3, :])
-        round_result(0, slice(0, widths[0]), nc.scalar.copy)
-        for t in order[2:]:
-            gather_next(t, 1)
-        nc.sync.dma_start(out_rows[:, 1:3, stages[1]], td[1][:, 1:3, :])
-        round_result(1, slice(0, widths[1]), nc.scalar.copy)
-        for t in order:
-            gather_next(t, 2)
-        nc.sync.dma_start(out_rows[:, :, stages[2]], td[2][:])
+        for u in range(2):
+            for h in range(2):
+                gather_next(h, u)
+                nc.sync.dma_start(out_rows[:, u, :, stages[h]], td[h, u])
+                round_pair(h, u, slice(0, widths[h]), nc.scalar.copy)
+        gather_next(2, 0)
+        round_pair(2, 0, slice(0, QUARTER), nc.scalar.copy)
+        gather_next(2, 1)
+        nc.sync.dma_start(
+            out_rows.rearrange("p u t j -> p (u t) j")[:, :, stages[2]], td_last[:].rearrange("p u t j -> p (u t) j")
+        )
         quantize_result(0)
         quantize_result(1)
-        round_result(2, slice(0, END_SPLIT), nc.vector.tensor_copy)
-        round_result(2, slice(END_SPLIT, widths[2]), nc.scalar.copy)
+        round_pair(2, 1, slice(0, END_SPLIT), nc.vector.tensor_copy)
+        round_pair(2, 1, slice(END_SPLIT, QUARTER), nc.scalar.copy)
         quantize_result(2)
         for q in range(4):
             queue = nc.scalar if q % 2 else nc.sync

@@ -21,7 +21,7 @@ RELU = mybir.ActivationFunctionType.Relu
 
 DISCOUNT = 0.9
 W1_SPLIT = 52
-W2_SPLIT = 64
+W2_SPLIT = 56
 HALF = 256
 QUARTER = 128
 END_SPLIT = 64
@@ -29,6 +29,7 @@ FIRST, SECOND, THIRD, FOURTH = 0, 2, 3, 1
 PLAIN = (FIRST, FOURTH)
 TURNED = (SECOND, THIRD)
 ROW = 4 * S
+LAP = 64
 
 
 def tile_picked_redq_none_po_kernel(
@@ -37,11 +38,11 @@ def tile_picked_redq_none_po_kernel(
     nc = tc.nc
     with ExitStack() as ctx:
         keep = ctx.enter_context(tc.tile_pool(name="keep", bufs=1))
-        late = ctx.enter_context(tc.tile_pool(name="late", bufs=1))
+        placed = ctx.enter_context(tc.tile_pool(name="placed", bufs=1))
         psum = ctx.enter_context(tc.psum_pool(name="psum", bufs=1))
 
         def bank(name, number, width=S):
-            return psum.tile([P, width], F32, name=name, tag=f"bank{number}")
+            return psum.tile([P, width], F32, name=name, offset=number * ROW)
 
         offs_sb = keep.tile([P, S // 16], U16, name="offs_sb")
         cur_sb = keep.tile([P, S // 16], U16, name="cur_sb")
@@ -65,7 +66,7 @@ def tile_picked_redq_none_po_kernel(
         w2_rows = w2.rearrange("(p j) c -> p j c", j=PACK)
         w2_cut = PACK * W2_SPLIT
         w2_left = keep.tile([P, PACK, w2_cut], F32, name="w2_left")
-        w2_right = late.tile([P, PACK, N - w2_cut], F32, name="w2_right", offset=0)
+        w2_right = placed.tile([P, PACK, N - w2_cut], F32, name="w2_right", offset=0)
         ident = keep.tile([P, P], F32, name="ident")
         make_identity(nc, ident[:])
         nc.sync.dma_start(w2_left[:], w2_rows[:, :, :w2_cut])
@@ -77,7 +78,7 @@ def tile_picked_redq_none_po_kernel(
         blocks = [slice(b * P, (b + 1) * P) for b in range(S // P)]
         stages = (halves[0], slice(HALF, HALF + QUARTER), slice(HALF + QUARTER, S))
 
-        rw_turned = bank("rw_turned", 6, P)
+        rw_turned = bank("rw_turned", 4, P)
         nc.tensor.transpose(rw_turned[:], rw_quarters[:], ident[:])
         rw_col = keep.tile([P, PACK], F32, name="rw_col")
         nc.scalar.copy(rw_col[:], rw_turned[:, :PACK])
@@ -89,8 +90,8 @@ def tile_picked_redq_none_po_kernel(
         xq_s = keep.tile([P, S], U8, name="xq_s", align_bytes=64)
         xq_w = keep.tile([P, S], U32, name="xq_w", align_bytes=64)
 
-        def dealt_out(grouped, rows):
-            return grouped[:].rearrange("p (t m j) -> p m j t", t=PACK, j=PACK)[:, rows]
+        def dealt_out(grouped, groups):
+            return grouped[:].rearrange("p (t m j) -> p m j t", t=PACK, j=PACK)[:, groups]
 
         def dealt_in(raw):
             return raw[:].rearrange("p j (m t) -> p m j t", t=PACK)
@@ -146,17 +147,17 @@ def tile_picked_redq_none_po_kernel(
         nc.vector.tensor_copy(xq_s[:], xs[:].indirect(offs_sb[:]))
         w1_q = quantize_weight(w1_bf, "w1")
 
-        base = keep.tile([P, PACK, S], F32, name="base")
-        base_third = [late.tile([P, HALF], F32, name=f"base_third{h}", offset=(4 + h) * ROW) for h in range(2)]
-        discount = late.tile([P, 32], F32, name="discount", offset=6 * ROW)
-        nc.gpsimd.memset(discount[:], 1.0)
-        nc.gpsimd.tensor_scalar(discount[:], discount[:], -DISCOUNT, 0.0, ALU.mult, ALU.add)
-        minus_one = keep.tile([P, 1], F32, name="minus_one", tag="second")
+        base = {t: keep.tile([P, S], F32, name=f"base{t}") for t in (FIRST, SECOND, FOURTH)}
+        base_third = [placed.tile([P, HALF], F32, name=f"base_third{h}", offset=(4 + h) * ROW) for h in range(2)]
+        minus_discount = placed.tile([P, 2 * LAP // 4], F32, name="minus_discount", offset=6 * ROW)
+        nc.gpsimd.memset(minus_discount[:, :1], 1.0)
+        nc.gpsimd.tensor_scalar(minus_discount[:, :1], minus_discount[:, :1], -DISCOUNT, 0.0, ALU.mult, ALU.add)
+        minus_one = keep.tile([P, 1], F32, name="minus_one", tag="partner")
         nc.gpsimd.memset(minus_one[:], -1.0)
 
         def base_cols(t, cols):
             if t != THIRD:
-                return base[:, t, cols]
+                return base[t][:, cols]
             h = cols.start // HALF
             return base_third[h][:, cols.start - h * HALF : cols.stop - h * HALF]
 
@@ -176,73 +177,67 @@ def tile_picked_redq_none_po_kernel(
         w2_bf = keep.tile([P, PACK * N], BF16, name="w2_bf", align_bytes=64)
         nc.vector.tensor_scalar_mul(dealt_out(w2_bf, slice(0, W2_SPLIT)), dealt_in(w2_left), -1.0)
 
-        y_acc = {t: bank(f"y{t}", number) for t, number in ((SECOND, 3), (THIRD, 4), (FOURTH, 5))}
-        y_first = []
+        y_acc = {t: bank(f"y{t}", number) for t, number in ((SECOND, 3), (THIRD, 5), (FOURTH, 6))}
         for i, cols in enumerate(stages):
-            y_first.append(bank(f"y_first{i}", i, cols.stop - cols.start))
-            product(y_first[i][:], w1_q, FIRST, cols)
+            piece = bank(f"y_first{i}", i, cols.stop - cols.start)
+            product(piece[:], w1_q, FIRST, cols)
             if cols == halves[0]:
                 product(y_acc[SECOND][:, cols], w1_q, SECOND, cols)
-            nc.scalar.activation(y_neg[FIRST][:, cols], y_first[i][:], COPY, scale=-1.0)
+            nc.scalar.activation(y_neg[FIRST][:, cols], piece[:], COPY, scale=-1.0)
         product(y_acc[SECOND][:, halves[1]], w1_q, SECOND, halves[1])
         for t in (THIRD, FOURTH):
             product(y_acc[t][:], w1_q, t, slice(0, S))
-        gap_acc = {t: bank(f"gap{t}", number) for t, number in ((SECOND, 1), (THIRD, 2))}
-        for t in TURNED:
-            turned_product(gap_acc[t], w1_q, t, True, False)
         gather_current(FIRST, [slice(0, S)])
         nc.scalar.activation(y_neg[SECOND][:, :S], y_acc[SECOND][:], COPY, scale=-1.0)
         gather_current(SECOND, [slice(0, S)])
-        yt_acc = {t: bank(f"yt{t}", number) for t, number in ((SECOND, 6), (THIRD, 7))}
+        yt_acc = {t: bank(f"yt{t}", number) for t, number in ((SECOND, 7), (THIRD, 1))}
         turn(yt_acc[SECOND], y_neg[SECOND], True, True)
+        gaps = bank("gaps", 3, 2 * S)
+        gap_acc = {t: gaps[:, i * S : (i + 1) * S] for i, t in enumerate(TURNED)}
+        for t in TURNED:
+            turned_product(gap_acc[t], w1_q, t, True, False)
 
         nc.scalar.activation(dealt_out(w2_bf, slice(W2_SPLIT, P)), dealt_in(w2_right), COPY, scale=minus_one[:])
-        w2_q = quantize_weight(w2_bf, "w2")
+        w2_neg_q = quantize_weight(w2_bf, "w2")
         for i, t in enumerate((THIRD, FOURTH)):
-            y_neg[t] = late.tile([P, S], F32, name=f"y_neg{t}", offset=i * ROW)
+            y_neg[t] = placed.tile([P, S], F32, name=f"y_neg{t}", offset=i * ROW)
             nc.scalar.activation(y_neg[t][:], y_acc[t][:], COPY, scale=-1.0)
             gather_current(t, halves)
         turn(yt_acc[THIRD], y_neg[THIRD], True, True)
 
         low = [keep.tile([P, S], F32, name=f"low{t}") for t in range(PACK)]
-        second = keep.tile([P, PACK, S], F32, name="second", tag="second")
-        excess = keep.tile([P, PACK, S], F32, name="excess")
-
-        def clip(t, number, y_disc):
-            e_acc = bank(f"e{t}", number)
-            product(e_acc[:], w2_q, t, slice(0, S))
-            nc.vector.scalar_tensor_tensor(low[t][:], e_acc[:], -DISCOUNT, y_disc, ALU.mult, ALU.min)
-
-        def clip_turned(t, number, scale):
-            low_acc = bank(f"low_acc{t}", number)
-            turn(low_acc, second[:, t, :], True, False)
-            turn(low_acc, excess[:, t, :], False, True)
-            nc.scalar.activation(low[t][:], low_acc[:], COPY, scale=scale)
-
-        for t, number in ((FIRST, 0), (FOURTH, 3)):
-            nc.scalar.activation(second[:, t, :], y_neg[t][:, :S], COPY, scale=-DISCOUNT)
-            clip(t, number, second[:, t, :])
+        partner = keep.tile([P, PACK, S], F32, name="partner", tag="partner")
+        excess = {t: keep.tile([P, S], F32, name=f"excess{t}") for t in TURNED}
+        for t, number in ((FIRST, 0), (FOURTH, 2)):
+            nc.scalar.activation(partner[:, t, :], y_neg[t][:, :S], COPY, scale=-DISCOUNT)
+            e_neg = bank(f"e_neg{t}", number)
+            product(e_neg[:], w2_neg_q, t, slice(0, S))
+            nc.vector.scalar_tensor_tensor(low[t][:], e_neg[:], -DISCOUNT, partner[:, t, :], ALU.mult, ALU.min)
         for t in TURNED:
-            nc.scalar.copy(second[:, t, :], yt_acc[t][:])
-            turned_product(gap_acc[t], w2_q, t, False, True)
-            nc.scalar.activation(excess[:, t, :], gap_acc[t][:], RELU)
-        clip_turned(SECOND, 4, -DISCOUNT)
-        clip_turned(THIRD, 5, discount[:, :1])
+            nc.scalar.copy(partner[:, t, :], yt_acc[t][:])
+            turned_product(gap_acc[t], w2_neg_q, t, False, True)
+        for t in TURNED:
+            nc.scalar.activation(excess[t][:], gap_acc[t], RELU)
+        for t, number, scale in ((SECOND, 5, -DISCOUNT), (THIRD, 6, minus_discount[:, :1])):
+            min_neg = bank(f"min_neg{t}", number)
+            turn(min_neg, partner[:, t, :], True, False)
+            turn(min_neg, excess[t][:], False, True)
+            nc.scalar.activation(low[t][:], min_neg[:], COPY, scale=scale)
 
         out_rows = out_0.rearrange("(p u t) j -> p u t j", u=2, t=2)
         out_words = out_1[0].rearrange("p n t -> p (n t)").bitcast(I32)
         o_scales = keep.tile([P, S], U8, name="o_scales", align_bytes=64)
         widths = [cols.stop - cols.start for cols in stages]
-        td_last = late.tile([P, 2, 2, QUARTER], F32, name="td_last", offset=4 * ROW)
+        td_last = placed.tile([P, 2, 2, QUARTER], F32, name="td_last", offset=4 * ROW)
         td = {
-            (0, 0): late.tile([P, 2, HALF], F32, name="td00", offset=ROW + 64)[:],
-            (1, 0): late.tile([P, 2, QUARTER], F32, name="td10", offset=ROW // 2 + 64)[:],
+            (0, 0): placed.tile([P, 2, HALF], F32, name="td00", offset=ROW + LAP)[:],
+            (1, 0): placed.tile([P, 2, QUARTER], F32, name="td10", offset=ROW // 2 + LAP)[:],
             (0, 1): keep.tile([P, 2, HALF], F32, name="td01")[:],
-            (1, 1): late.tile([P, 2, QUARTER], F32, name="td11", offset=6 * ROW + 64 - ROW // 2)[:],
+            (1, 1): placed.tile([P, 2, QUARTER], F32, name="td11", offset=6 * ROW - ROW // 2 + LAP)[:],
             (2, 0): td_last[:, 0],
             (2, 1): td_last[:, 1],
         }
-        bf_early = late.tile([P, HALF + QUARTER, 2, 2], BF16, name="bf_early", offset=6 * ROW + 64, align_bytes=64)
+        bf_early = placed.tile([P, HALF + QUARTER, 2, 2], BF16, name="bf_early", offset=6 * ROW + LAP, align_bytes=64)
         bf_last = keep.tile([P, QUARTER, 2, 2], BF16, name="bf_last", align_bytes=64)
         td_bf = [bf_early[:, :HALF], bf_early[:, HALF:], bf_last[:]]
 

@@ -20,7 +20,7 @@ COPY = mybir.ActivationFunctionType.Copy
 RELU = mybir.ActivationFunctionType.Relu
 
 DISCOUNT = 0.9
-W1_SPLIT = 52
+W1_SPLIT = 80
 W2_SPLIT = 56
 HALF = 256
 QUARTER = 128
@@ -29,7 +29,9 @@ FIRST, SECOND, THIRD, FOURTH = 0, 2, 3, 1
 PLAIN = (FIRST, FOURTH)
 TURNED = (SECOND, THIRD)
 ROW = 4 * S
+SCALE_ROW0 = 16
 LAP = 64
+XS_AT = 4 * PACK * (N - PACK * W2_SPLIT) - LAP
 
 
 def tile_picked_redq_none_po_kernel(
@@ -48,31 +50,46 @@ def tile_picked_redq_none_po_kernel(
         cur_sb = keep.tile([P, S // 16], U16, name="cur_sb")
         nx_sb = keep.tile([P, S // 16], U16, name="nx_sb")
         xw = keep.tile([P, T], I32, name="xw", align_bytes=64)
-        xs = keep.tile([P, T], U8, name="xs", align_bytes=64)
+        xs = placed.tile([P, T], U8, name="xs", offset=XS_AT, align_bytes=64)
         rw_sb = keep.tile([P, S], F32, name="rw_sb")
 
-        nc.vector.memset(xs[:].bitcast(I32), 0)
+        minus_one = keep.tile([P, 1], F32, name="minus_one", tag="partner")
+        nc.gpsimd.memset(minus_one[:], -1.0)
+        minus_discount = placed.tile([P, 2 * LAP // 4], F32, name="minus_discount", offset=8 * ROW)
+        nc.scalar.activation(minus_discount[:, :1], minus_one[:], COPY, scale=DISCOUNT)
+        nc.vector.memset(xs[:SCALE_ROW0, :].bitcast(I32), 0)
+        nc.vector.memset(xs[32:64, :].bitcast(I32), 0)
+        nc.vector.memset(xs[64:, :].bitcast(I32), 0)
         w1_raw = keep.tile([P, PACK, N], F32, name="w1_raw")
-        nc.sync.dma_start(w1_raw[:], w1.rearrange("(p j) c -> p j c", j=PACK))
+        w1_rows = w1.rearrange("(p j) c -> p j c", j=PACK)
+        nc.sync.dma_start(w1_raw[:, :1], w1_rows[:, :1])
         nc.sync.dma_start(offs_sb[:], offs)
+        nc.sync.dma_start(xs[SCALE_ROW0 : SCALE_ROW0 + 16, :].bitcast(I32), x_scales[0].bitcast(I32))
+        nc.sync.dma_start(w1_raw[:, 1:], w1_rows[:, 1:])
         rw_quarters = keep.tile([P, P], F32, name="rw_quarters")
-        nc.gpsimd.memset(rw_quarters[:], 0.0)
-        nc.scalar.dma_start(rw_quarters[:PACK, :], rw[0].rearrange("(b c) -> b c", b=PACK))
+        nc.scalar.dma_start(rw_quarters[P - PACK :, :], rw[0].rearrange("(b c) -> b c", b=PACK))
+        nc.gpsimd.memset(rw_quarters[:96, :], 0.0)
+        nc.gpsimd.memset(rw_quarters[96 : P - PACK, :], 0.0)
+        nc.sync.dma_start(cur_sb[:], cur)
+        nc.sync.dma_start(xw[:], x_words[0].rearrange("p n t -> p (n t)").bitcast(I32))
+        nc.sync.dma_start(nx_sb[:], nx)
+        xq_s = keep.tile([P, S], U8, name="xq_s", align_bytes=64)
+        nc.gpsimd.memset(xq_s[:].bitcast(I32), 0)
+        picked_s = keep.tile([P, S], U8, name="picked_s", align_bytes=64)
+        nc.vector.tensor_copy(picked_s[:], xs[:].indirect(offs_sb[:]))
         for q in range(4):
             nc.sync.dma_start(
-                xs[32 * q : 32 * q + 4, :].bitcast(I32), x_scales[0, 4 * q : 4 * q + 4, :].bitcast(I32)
+                xq_s[32 * q : 32 * q + 4, :].bitcast(I32),
+                picked_s[SCALE_ROW0 + 4 * q : SCALE_ROW0 + 4 * q + 4, :].bitcast(I32),
             )
-        nc.sync.dma_start(xw[:], x_words[0].rearrange("p n t -> p (n t)").bitcast(I32))
         w2_rows = w2.rearrange("(p j) c -> p j c", j=PACK)
         w2_cut = PACK * W2_SPLIT
-        w2_left = keep.tile([P, PACK, w2_cut], F32, name="w2_left")
+        w2_left = placed.tile([P, PACK, w2_cut], F32, name="w2_left", offset=XS_AT + T - LAP)
         w2_right = placed.tile([P, PACK, N - w2_cut], F32, name="w2_right", offset=0)
         ident = keep.tile([P, P], F32, name="ident")
         make_identity(nc, ident[:])
         nc.sync.dma_start(w2_left[:], w2_rows[:, :, :w2_cut])
-        nc.sync.dma_start(cur_sb[:], cur)
         nc.sync.dma_start(w2_right[:], w2_rows[:, :, w2_cut:])
-        nc.sync.dma_start(nx_sb[:], nx)
 
         halves = [slice(h * HALF, (h + 1) * HALF) for h in range(S // HALF)]
         blocks = [slice(b * P, (b + 1) * P) for b in range(S // P)]
@@ -81,13 +98,12 @@ def tile_picked_redq_none_po_kernel(
         rw_turned = bank("rw_turned", 4, P)
         nc.tensor.transpose(rw_turned[:], rw_quarters[:], ident[:])
         rw_col = keep.tile([P, PACK], F32, name="rw_col")
-        nc.scalar.copy(rw_col[:], rw_turned[:, :PACK])
+        nc.scalar.copy(rw_col[:], rw_turned[:, P - PACK :])
         rw_acc = bank("rw_acc", 7)
         for b, cols in enumerate(blocks):
             nc.tensor.transpose(rw_acc[:, cols], rw_col[:, b : b + 1].to_broadcast([P, P]), ident[:])
         nc.scalar.copy(rw_sb[:], rw_acc[:])
 
-        xq_s = keep.tile([P, S], U8, name="xq_s", align_bytes=64)
         xq_w = keep.tile([P, S], U32, name="xq_w", align_bytes=64)
 
         def dealt_out(grouped, groups):
@@ -144,16 +160,13 @@ def tile_picked_redq_none_po_kernel(
         w1_bf = keep.tile([P, PACK * N], BF16, name="w1_bf", align_bytes=64)
         nc.vector.tensor_copy(dealt_out(w1_bf, slice(0, W1_SPLIT)), dealt_in(w1_raw)[:, :W1_SPLIT])
         nc.scalar.activation(dealt_out(w1_bf, slice(W1_SPLIT, P)), dealt_in(w1_raw)[:, W1_SPLIT:], COPY)
-        nc.vector.tensor_copy(xq_s[:], xs[:].indirect(offs_sb[:]))
         w1_q = quantize_weight(w1_bf, "w1")
 
-        base = {t: keep.tile([P, S], F32, name=f"base{t}") for t in (FIRST, SECOND, FOURTH)}
-        base_third = [placed.tile([P, HALF], F32, name=f"base_third{h}", offset=(4 + h) * ROW) for h in range(2)]
-        minus_discount = placed.tile([P, 2 * LAP // 4], F32, name="minus_discount", offset=6 * ROW)
-        nc.gpsimd.memset(minus_discount[:, :1], 1.0)
-        nc.gpsimd.tensor_scalar(minus_discount[:, :1], minus_discount[:, :1], -DISCOUNT, 0.0, ALU.mult, ALU.add)
-        minus_one = keep.tile([P, 1], F32, name="minus_one", tag="partner")
-        nc.gpsimd.memset(minus_one[:], -1.0)
+        base = {
+            t: placed.tile([P, S], F32, name=f"base{t}", offset=XS_AT + T + i * ROW) for i, t in enumerate((FIRST, SECOND))
+        }
+        base[FOURTH] = keep.tile([P, S], F32, name="base_fourth")
+        base_third = [placed.tile([P, HALF], F32, name=f"base_third{h}", offset=(6 + h) * ROW) for h in range(2)]
 
         def base_cols(t, cols):
             if t != THIRD:
@@ -228,16 +241,16 @@ def tile_picked_redq_none_po_kernel(
         out_words = out_1[0].rearrange("p n t -> p (n t)").bitcast(I32)
         o_scales = keep.tile([P, S], U8, name="o_scales", align_bytes=64)
         widths = [cols.stop - cols.start for cols in stages]
-        td_last = placed.tile([P, 2, 2, QUARTER], F32, name="td_last", offset=4 * ROW)
+        td_last = placed.tile([P, 2, 2, QUARTER], F32, name="td_last", offset=6 * ROW)
         td = {
             (0, 0): placed.tile([P, 2, HALF], F32, name="td00", offset=ROW + LAP)[:],
             (1, 0): placed.tile([P, 2, QUARTER], F32, name="td10", offset=ROW // 2 + LAP)[:],
             (0, 1): keep.tile([P, 2, HALF], F32, name="td01")[:],
-            (1, 1): placed.tile([P, 2, QUARTER], F32, name="td11", offset=6 * ROW - ROW // 2 + LAP)[:],
+            (1, 1): placed.tile([P, 2, QUARTER], F32, name="td11", offset=8 * ROW - ROW // 2 + LAP)[:],
             (2, 0): td_last[:, 0],
             (2, 1): td_last[:, 1],
         }
-        bf_early = placed.tile([P, HALF + QUARTER, 2, 2], BF16, name="bf_early", offset=6 * ROW + LAP, align_bytes=64)
+        bf_early = placed.tile([P, HALF + QUARTER, 2, 2], BF16, name="bf_early", offset=8 * ROW + LAP, align_bytes=64)
         bf_last = keep.tile([P, QUARTER, 2, 2], BF16, name="bf_last", align_bytes=64)
         td_bf = [bf_early[:, :HALF], bf_early[:, HALF:], bf_last[:]]
 

@@ -17,6 +17,7 @@ U8 = mybir.dt.uint8
 FP8X4 = mybir.dt.float8_e4m3fn_x4
 ALU = mybir.AluOpType
 COPY = mybir.ActivationFunctionType.Copy
+IDENTITY = mybir.ActivationFunctionType.Identity
 RELU = mybir.ActivationFunctionType.Relu
 
 DISCOUNT = 0.9
@@ -24,7 +25,7 @@ W1_SPLIT = 80
 W2_SPLIT = 56
 HALF = 256
 QUARTER = 128
-END_SPLIT = 64
+END_SPLIT = 96
 FIRST, SECOND, THIRD, FOURTH = 0, 2, 3, 1
 PLAIN = (FIRST, FOURTH)
 TURNED = (SECOND, THIRD)
@@ -53,10 +54,13 @@ def tile_picked_redq_none_po_kernel(
         xs = placed.tile([P, T], U8, name="xs", offset=XS_AT, align_bytes=64)
         rw_sb = keep.tile([P, S], F32, name="rw_sb")
 
-        minus_one = keep.tile([P, 1], F32, name="minus_one", tag="partner")
-        nc.gpsimd.memset(minus_one[:], -1.0)
+        y_last = placed.tile([P, 2 * S], F32, name="y_last", offset=11 * ROW)
+        minus_one = y_last[:, :1]
+        nc.gpsimd.memset(minus_one, -1.0)
+        zero = keep.tile([P, 1], F32, name="zero", tag="partner")
+        nc.gpsimd.memset(zero[:], 0.0)
         minus_discount = placed.tile([P, 2 * LAP // 4], F32, name="minus_discount", offset=8 * ROW)
-        nc.scalar.activation(minus_discount[:, :1], minus_one[:], COPY, scale=DISCOUNT)
+        nc.scalar.activation(minus_discount[:, :1], minus_one, COPY, scale=DISCOUNT)
         nc.vector.memset(xs[:SCALE_ROW0, :].bitcast(I32), 0)
         nc.vector.memset(xs[32:64, :].bitcast(I32), 0)
         nc.vector.memset(xs[64:, :].bitcast(I32), 0)
@@ -85,11 +89,12 @@ def tile_picked_redq_none_po_kernel(
         w2_rows = w2.rearrange("(p j) c -> p j c", j=PACK)
         w2_cut = PACK * W2_SPLIT
         w2_left = placed.tile([P, PACK, w2_cut], F32, name="w2_left", offset=XS_AT + T - LAP)
-        w2_right = placed.tile([P, PACK, N - w2_cut], F32, name="w2_right", offset=0)
+        w2_right_rows = placed.tile([P, PACK * (N - w2_cut)], F32, name="w2_right", offset=0)
+        w2_right = w2_right_rows[:].rearrange("p (j c) -> p j c", j=PACK)
         ident = keep.tile([P, P], F32, name="ident")
         make_identity(nc, ident[:])
         nc.sync.dma_start(w2_left[:], w2_rows[:, :, :w2_cut])
-        nc.sync.dma_start(w2_right[:], w2_rows[:, :, w2_cut:])
+        nc.sync.dma_start(w2_right, w2_rows[:, :, w2_cut:])
 
         halves = [slice(h * HALF, (h + 1) * HALF) for h in range(S // HALF)]
         blocks = [slice(b * P, (b + 1) * P) for b in range(S // P)]
@@ -110,7 +115,7 @@ def tile_picked_redq_none_po_kernel(
             return grouped[:].rearrange("p (t m j) -> p m j t", t=PACK, j=PACK)[:, groups]
 
         def dealt_in(raw):
-            return raw[:].rearrange("p j (m t) -> p m j t", t=PACK)
+            return raw.rearrange("p j (m t) -> p m j t", t=PACK)
 
         def quantize_weight(grouped, name):
             codes = keep.tile([P, N], U32, name=f"{name}_codes", align_bytes=64)
@@ -157,38 +162,40 @@ def tile_picked_redq_none_po_kernel(
         def entries(cols):
             return slice(cols.start // 16, cols.stop // 16)
 
+        def within(td, cols):
+            first = cols.start // td.shape[2] * td.shape[2]
+            return slice(cols.start - first, cols.stop - first)
+
         w1_bf = keep.tile([P, PACK * N], BF16, name="w1_bf", align_bytes=64)
-        nc.vector.tensor_copy(dealt_out(w1_bf, slice(0, W1_SPLIT)), dealt_in(w1_raw)[:, :W1_SPLIT])
-        nc.scalar.activation(dealt_out(w1_bf, slice(W1_SPLIT, P)), dealt_in(w1_raw)[:, W1_SPLIT:], COPY)
+        nc.vector.tensor_copy(dealt_out(w1_bf, slice(0, W1_SPLIT)), dealt_in(w1_raw[:])[:, :W1_SPLIT])
+        nc.scalar.activation(dealt_out(w1_bf, slice(W1_SPLIT, P)), dealt_in(w1_raw[:])[:, W1_SPLIT:], COPY)
         w1_q = quantize_weight(w1_bf, "w1")
 
         base = {
             t: placed.tile([P, S], F32, name=f"base{t}", offset=XS_AT + T + i * ROW) for i, t in enumerate((FIRST, SECOND))
         }
-        base[FOURTH] = keep.tile([P, S], F32, name="base_fourth")
-        base_third = [placed.tile([P, HALF], F32, name=f"base_third{h}", offset=(6 + h) * ROW) for h in range(2)]
-
-        def base_cols(t, cols):
-            if t != THIRD:
-                return base[t][:, cols]
-            h = cols.start // HALF
-            return base_third[h][:, cols.start - h * HALF : cols.stop - h * HALF]
+        for t in (THIRD, FOURTH):
+            base[t] = keep.tile([P, S], F32, name=f"base{t}")
 
         y_neg = {}
 
         def gather_current(t, pieces):
             for cols in pieces:
                 nc.vector.tensor_tensor(
-                    base_cols(t, cols), y_neg[t][:].indirect(cur_sb[:, entries(cols)]), rw_sb[:, cols], ALU.add
+                    base[t][:, cols], y_neg[t][:].indirect(cur_sb[:, entries(cols)]), rw_sb[:, cols], ALU.add
                 )
 
         for t in (FIRST, SECOND):
             y_neg[t] = keep.tile([P, 2 * S], F32, name=f"y_neg{t}")
             nc.gpsimd.memset(y_neg[t][:, S:], 0.0)
+        nc.gpsimd.memset(y_last[:, S:], 0.0)
+        low = {t: keep.tile([P, S], F32, name=f"low{t}") for t in (SECOND, THIRD, FOURTH)}
+        low[FIRST] = keep.tile([P, 2 * S], F32, name="low_first")
+        nc.gpsimd.memset(low[FIRST][:, S:], 0.0)
         for cols in halves:
             nc.vector.tensor_copy(xq_w[:, cols], xw[:].bitcast(U32).indirect(offs_sb[:, entries(cols)]))
         w2_bf = keep.tile([P, PACK * N], BF16, name="w2_bf", align_bytes=64)
-        nc.vector.tensor_scalar_mul(dealt_out(w2_bf, slice(0, W2_SPLIT)), dealt_in(w2_left), -1.0)
+        nc.vector.tensor_scalar_mul(dealt_out(w2_bf, slice(0, W2_SPLIT)), dealt_in(w2_left[:]), -1.0)
 
         y_acc = {t: bank(f"y{t}", number) for t, number in ((SECOND, 3), (THIRD, 5), (FOURTH, 6))}
         for i, cols in enumerate(stages):
@@ -205,30 +212,29 @@ def tile_picked_redq_none_po_kernel(
         gather_current(SECOND, [slice(0, S)])
         yt_acc = {t: bank(f"yt{t}", number) for t, number in ((SECOND, 7), (THIRD, 1))}
         turn(yt_acc[SECOND], y_neg[SECOND], True, True)
-        gaps = bank("gaps", 3, 2 * S)
-        gap_acc = {t: gaps[:, i * S : (i + 1) * S] for i, t in enumerate(TURNED)}
+        gap_acc = {t: bank(f"gap{t}", number)[:] for t, number in ((SECOND, 3), (THIRD, 2))}
         for t in TURNED:
             turned_product(gap_acc[t], w1_q, t, True, False)
 
-        nc.scalar.activation(dealt_out(w2_bf, slice(W2_SPLIT, P)), dealt_in(w2_right), COPY, scale=minus_one[:])
+        nc.scalar.activation(dealt_out(w2_bf, slice(W2_SPLIT, P)), dealt_in(w2_right), IDENTITY, scale=minus_one, bias=zero[:])
         w2_neg_q = quantize_weight(w2_bf, "w2")
-        for i, t in enumerate((THIRD, FOURTH)):
-            y_neg[t] = placed.tile([P, S], F32, name=f"y_neg{t}", offset=i * ROW)
-            nc.scalar.activation(y_neg[t][:], y_acc[t][:], COPY, scale=-1.0)
-            gather_current(t, halves)
+        y_neg[THIRD], y_neg[FOURTH] = w2_right_rows, y_last
+        for t in (THIRD, FOURTH):
+            nc.scalar.activation(y_neg[t][:, :S], y_acc[t][:], COPY, scale=-1.0)
+            gather_current(t, [slice(0, S)])
         turn(yt_acc[THIRD], y_neg[THIRD], True, True)
 
-        low = [keep.tile([P, S], F32, name=f"low{t}") for t in range(PACK)]
         partner = keep.tile([P, PACK, S], F32, name="partner", tag="partner")
         excess = {t: keep.tile([P, S], F32, name=f"excess{t}") for t in TURNED}
-        for t, number in ((FIRST, 0), (FOURTH, 2)):
+        for t in TURNED:
+            turned_product(gap_acc[t], w2_neg_q, t, False, True)
+        for t, number in ((FIRST, 0), (FOURTH, 4)):
             nc.scalar.activation(partner[:, t, :], y_neg[t][:, :S], COPY, scale=-DISCOUNT)
             e_neg = bank(f"e_neg{t}", number)
             product(e_neg[:], w2_neg_q, t, slice(0, S))
-            nc.vector.scalar_tensor_tensor(low[t][:], e_neg[:], -DISCOUNT, partner[:, t, :], ALU.mult, ALU.min)
+            nc.vector.scalar_tensor_tensor(low[t][:, :S], e_neg[:], -DISCOUNT, partner[:, t, :], ALU.mult, ALU.min)
         for t in TURNED:
             nc.scalar.copy(partner[:, t, :], yt_acc[t][:])
-            turned_product(gap_acc[t], w2_neg_q, t, False, True)
         for t in TURNED:
             nc.scalar.activation(excess[t][:], gap_acc[t], RELU)
         for t, number, scale in ((SECOND, 5, -DISCOUNT), (THIRD, 6, minus_discount[:, :1])):
@@ -240,55 +246,54 @@ def tile_picked_redq_none_po_kernel(
         out_rows = out_0.rearrange("(p u t) j -> p u t j", u=2, t=2)
         out_words = out_1[0].rearrange("p n t -> p (n t)").bitcast(I32)
         o_scales = keep.tile([P, S], U8, name="o_scales", align_bytes=64)
-        widths = [cols.stop - cols.start for cols in stages]
-        td_last = placed.tile([P, 2, 2, QUARTER], F32, name="td_last", offset=6 * ROW)
-        td = {
-            (0, 0): placed.tile([P, 2, HALF], F32, name="td00", offset=ROW + LAP)[:],
-            (1, 0): placed.tile([P, 2, QUARTER], F32, name="td10", offset=ROW // 2 + LAP)[:],
-            (0, 1): keep.tile([P, 2, HALF], F32, name="td01")[:],
-            (1, 1): placed.tile([P, 2, QUARTER], F32, name="td11", offset=8 * ROW - ROW // 2 + LAP)[:],
-            (2, 0): td_last[:, 0],
-            (2, 1): td_last[:, 1],
-        }
-        bf_early = placed.tile([P, HALF + QUARTER, 2, 2], BF16, name="bf_early", offset=8 * ROW + LAP, align_bytes=64)
-        bf_last = keep.tile([P, QUARTER, 2, 2], BF16, name="bf_last", align_bytes=64)
-        td_bf = [bf_early[:, :HALF], bf_early[:, HALF:], bf_last[:]]
+        td_plain = placed.tile([P, 2, S], F32, name="td_plain", offset=13 * ROW - LAP)
+        td_turned = [
+            keep.tile([P, 2, HALF], F32, name="td_turned0"),
+            placed.tile([P, 2, HALF], F32, name="td_turned1", offset=7 * ROW + LAP),
+        ]
+        td_bf = placed.tile([P, S, 2, 2], BF16, name="td_bf", offset=8 * ROW + LAP, align_bytes=64)
 
-        def gather_next(h, u):
-            cols = stages[h]
-            for t in (PLAIN, TURNED)[u]:
-                nc.vector.tensor_tensor(
-                    td[h, u][:, t % 2, :], low[t][:].indirect(nx_sb[:, entries(cols)]), base_cols(t, cols), ALU.add
-                )
+        def gather_next(td, t, cols):
+            nc.vector.tensor_tensor(
+                td[:, t % 2, within(td, cols)], low[t][:].indirect(nx_sb[:, entries(cols)]), base[t][:, cols], ALU.add
+            )
 
-        def round_pair(h, u, part, copy):
-            copy(td_bf[h][:, part, u, :], td[h, u][:, :, part].rearrange("p t j -> p j t"))
+        def round_pair(td, u, cols, copy):
+            copy(td_bf[:, cols, u, :], td[:, :, within(td, cols)].rearrange("p t j -> p j t"))
 
-        def quantize_result(h):
-            o_codes = keep.tile([P, widths[h]], I32, name=f"o_codes{h}", align_bytes=64)
+        def quantize_result(cols):
+            o_codes = keep.tile([P, cols.stop - cols.start], I32, name=f"o_codes{cols.start}", align_bytes=64)
             nc.vector.quantize_mx(
                 out=o_codes[:].bitcast(FP8X4),
-                scales=o_scales[:, stages[h]],
-                in_=td_bf[h].rearrange("p j u t -> p (j u t)"),
+                scales=o_scales[:, cols],
+                in_=td_bf[:, cols].rearrange("p j u t -> p (j u t)"),
             )
-            nc.sync.dma_start(out_words[:, stages[h]], o_codes[:])
+            nc.sync.dma_start(out_words[:, cols], o_codes[:])
 
-        for u in range(2):
-            for h in range(2):
-                gather_next(h, u)
-                nc.sync.dma_start(out_rows[:, u, :, stages[h]], td[h, u])
-                round_pair(h, u, slice(0, widths[h]), nc.scalar.copy)
-        gather_next(2, 0)
-        round_pair(2, 0, slice(0, QUARTER), nc.scalar.copy)
-        gather_next(2, 1)
-        nc.sync.dma_start(
-            out_rows.rearrange("p u t j -> p (u t) j")[:, :, stages[2]], td_last[:].rearrange("p u t j -> p (u t) j")
-        )
-        quantize_result(0)
-        quantize_result(1)
-        round_pair(2, 1, slice(0, END_SPLIT), nc.vector.tensor_copy)
-        round_pair(2, 1, slice(END_SPLIT, QUARTER), nc.scalar.copy)
-        quantize_result(2)
+        gather_next(td_plain, FIRST, slice(0, S))
+        for cols in halves:
+            gather_next(td_plain, FOURTH, cols)
+            round_pair(td_plain, 0, cols, nc.scalar.copy)
+        nc.sync.dma_start(out_rows[:, 0], td_plain[:])
+        td = td_turned[0]
+        for t in TURNED:
+            gather_next(td, t, halves[0])
+        round_pair(td, 1, halves[0], nc.scalar.copy)
+        nc.sync.dma_start(out_rows[:, 1, :, halves[0]], td[:])
+        td = td_turned[1]
+        for t in TURNED:
+            gather_next(td, t, stages[1])
+        round_pair(td, 1, stages[1], nc.scalar.copy)
+        last = stages[2]
+        for t in TURNED:
+            gather_next(td, t, last)
+        nc.sync.dma_start(out_rows[:, 1, :, halves[1]], td[:])
+        quantize_result(stages[0])
+        cut = last.start + END_SPLIT
+        round_pair(td, 1, slice(last.start, cut), nc.vector.tensor_copy)
+        round_pair(td, 1, slice(cut, last.stop), nc.scalar.copy)
+        quantize_result(stages[1])
+        quantize_result(last)
         for q in range(4):
             queue = nc.scalar if q % 2 else nc.sync
             queue.dma_start(

@@ -197,7 +197,8 @@ def tile_picked_redq_none_po_kernel(
         w2_bf = keep.tile([P, PACK * N], BF16, name="w2_bf", align_bytes=64)
         nc.vector.tensor_scalar_mul(dealt_out(w2_bf, slice(0, W2_SPLIT)), dealt_in(w2_left[:]), -1.0)
 
-        y_acc = {t: bank(f"y{t}", number) for t, number in ((SECOND, 3), (THIRD, 5), (FOURTH, 6))}
+        y_acc = {t: bank(f"y{t}", number) for t, number in ((THIRD, 5), (FOURTH, 6))}
+        y_acc[SECOND] = bank("y_second", 3, 2 * S)
         for i, cols in enumerate(stages):
             piece = bank(f"y_first{i}", i, cols.stop - cols.start)
             product(piece[:], w1_q, FIRST, cols)
@@ -208,11 +209,11 @@ def tile_picked_redq_none_po_kernel(
         for t in (THIRD, FOURTH):
             product(y_acc[t][:], w1_q, t, slice(0, S))
         gather_current(FIRST, [slice(0, S)])
-        nc.scalar.activation(y_neg[SECOND][:, :S], y_acc[SECOND][:], COPY, scale=-1.0)
+        nc.scalar.activation(y_neg[SECOND][:, :S], y_acc[SECOND][:, :S], COPY, scale=-1.0)
         gather_current(SECOND, [slice(0, S)])
         yt_acc = {t: bank(f"yt{t}", number) for t, number in ((SECOND, 7), (THIRD, 1))}
         turn(yt_acc[SECOND], y_neg[SECOND], True, True)
-        gap_acc = {t: bank(f"gap{t}", number)[:] for t, number in ((SECOND, 3), (THIRD, 2))}
+        gap_acc = {t: bank(f"gap{t}", number)[:] for t, number in ((SECOND, 3), (THIRD, 4))}
         for t in TURNED:
             turned_product(gap_acc[t], w1_q, t, True, False)
 
@@ -226,13 +227,13 @@ def tile_picked_redq_none_po_kernel(
 
         partner = keep.tile([P, PACK, S], F32, name="partner", tag="partner")
         excess = {t: keep.tile([P, S], F32, name=f"excess{t}") for t in TURNED}
-        for t in TURNED:
-            turned_product(gap_acc[t], w2_neg_q, t, False, True)
-        for t, number in ((FIRST, 0), (FOURTH, 4)):
+        for t, number in ((FIRST, 0), (FOURTH, 2)):
             nc.scalar.activation(partner[:, t, :], y_neg[t][:, :S], COPY, scale=-DISCOUNT)
             e_neg = bank(f"e_neg{t}", number)
             product(e_neg[:], w2_neg_q, t, slice(0, S))
             nc.vector.scalar_tensor_tensor(low[t][:, :S], e_neg[:], -DISCOUNT, partner[:, t, :], ALU.mult, ALU.min)
+        for t in TURNED:
+            turned_product(gap_acc[t], w2_neg_q, t, False, True)
         for t in TURNED:
             nc.scalar.copy(partner[:, t, :], yt_acc[t][:])
         for t in TURNED:

@@ -30,9 +30,12 @@ FIRST, SECOND, THIRD, FOURTH = 0, 2, 3, 1
 PLAIN = (FIRST, FOURTH)
 TURNED = (SECOND, THIRD)
 ROW = 4 * S
+SCALE_ROWS = K // 32
 SCALE_ROW0 = 16
 LAP = 64
 XS_AT = 4 * PACK * (N - PACK * W2_SPLIT) - LAP
+DISCOUNT_AT = 8 * ROW
+Y_LAST_AT = 11 * ROW
 
 
 def tile_picked_redq_none_po_kernel(
@@ -54,13 +57,14 @@ def tile_picked_redq_none_po_kernel(
         xs = placed.tile([P, T], U8, name="xs", offset=XS_AT, align_bytes=64)
         rw_sb = keep.tile([P, S], F32, name="rw_sb")
 
-        y_last = placed.tile([P, 2 * S], F32, name="y_last", offset=11 * ROW)
+        y_last = placed.tile([P, 2 * S], F32, name="y_last", offset=Y_LAST_AT)
         minus_one = y_last[:, :1]
         nc.gpsimd.memset(minus_one, -1.0)
         zero = keep.tile([P, 1], F32, name="zero", tag="partner")
         nc.gpsimd.memset(zero[:], 0.0)
-        minus_discount = placed.tile([P, 2 * LAP // 4], F32, name="minus_discount", offset=8 * ROW)
+        minus_discount = placed.tile([P, 2 * LAP // 4], F32, name="minus_discount", offset=DISCOUNT_AT)
         nc.scalar.activation(minus_discount[:, :1], minus_one, COPY, scale=DISCOUNT)
+
         nc.vector.memset(xs[:SCALE_ROW0, :].bitcast(I32), 0)
         nc.vector.memset(xs[32:64, :].bitcast(I32), 0)
         nc.vector.memset(xs[64:, :].bitcast(I32), 0)
@@ -68,15 +72,16 @@ def tile_picked_redq_none_po_kernel(
         w1_rows = w1.rearrange("(p j) c -> p j c", j=PACK)
         nc.sync.dma_start(w1_raw[:, :1], w1_rows[:, :1])
         nc.sync.dma_start(offs_sb[:], offs)
-        nc.sync.dma_start(xs[SCALE_ROW0 : SCALE_ROW0 + 16, :].bitcast(I32), x_scales[0].bitcast(I32))
+        nc.sync.dma_start(xs[SCALE_ROW0 : SCALE_ROW0 + SCALE_ROWS, :].bitcast(I32), x_scales[0].bitcast(I32))
         nc.sync.dma_start(w1_raw[:, 1:], w1_rows[:, 1:])
         rw_quarters = keep.tile([P, P], F32, name="rw_quarters")
         nc.scalar.dma_start(rw_quarters[P - PACK :, :], rw[0].rearrange("(b c) -> b c", b=PACK))
         nc.gpsimd.memset(rw_quarters[:96, :], 0.0)
         nc.gpsimd.memset(rw_quarters[96 : P - PACK, :], 0.0)
-        nc.sync.dma_start(cur_sb[:], cur)
         nc.sync.dma_start(xw[:], x_words[0].rearrange("p n t -> p (n t)").bitcast(I32))
+        nc.sync.dma_start(cur_sb[:], cur)
         nc.sync.dma_start(nx_sb[:], nx)
+
         xq_s = keep.tile([P, S], U8, name="xq_s", align_bytes=64)
         nc.gpsimd.memset(xq_s[:].bitcast(I32), 0)
         picked_s = keep.tile([P, S], U8, name="picked_s", align_bytes=64)
@@ -172,18 +177,16 @@ def tile_picked_redq_none_po_kernel(
         w1_q = quantize_weight(w1_bf, "w1")
 
         base = {
-            t: placed.tile([P, S], F32, name=f"base{t}", offset=XS_AT + T + i * ROW) for i, t in enumerate((FIRST, SECOND))
+            t: placed.tile([P, S], F32, name=f"base{t}", offset=XS_AT + T + i * ROW)
+            for i, t in enumerate((FIRST, SECOND))
         }
         for t in (THIRD, FOURTH):
             base[t] = keep.tile([P, S], F32, name=f"base{t}")
 
         y_neg = {}
 
-        def gather_current(t, pieces):
-            for cols in pieces:
-                nc.vector.tensor_tensor(
-                    base[t][:, cols], y_neg[t][:].indirect(cur_sb[:, entries(cols)]), rw_sb[:, cols], ALU.add
-                )
+        def gather_current(t):
+            nc.vector.tensor_tensor(base[t][:], y_neg[t][:].indirect(cur_sb[:]), rw_sb[:], ALU.add)
 
         for t in (FIRST, SECOND):
             y_neg[t] = keep.tile([P, 2 * S], F32, name=f"y_neg{t}")
@@ -208,21 +211,23 @@ def tile_picked_redq_none_po_kernel(
         product(y_acc[SECOND][:, halves[1]], w1_q, SECOND, halves[1])
         for t in (THIRD, FOURTH):
             product(y_acc[t][:], w1_q, t, slice(0, S))
-        gather_current(FIRST, [slice(0, S)])
+        gather_current(FIRST)
         nc.scalar.activation(y_neg[SECOND][:, :S], y_acc[SECOND][:, :S], COPY, scale=-1.0)
-        gather_current(SECOND, [slice(0, S)])
+        gather_current(SECOND)
         yt_acc = {t: bank(f"yt{t}", number) for t, number in ((SECOND, 7), (THIRD, 1))}
         turn(yt_acc[SECOND], y_neg[SECOND], True, True)
         gap_acc = {t: bank(f"gap{t}", number)[:] for t, number in ((SECOND, 3), (THIRD, 4))}
         for t in TURNED:
             turned_product(gap_acc[t], w1_q, t, True, False)
 
-        nc.scalar.activation(dealt_out(w2_bf, slice(W2_SPLIT, P)), dealt_in(w2_right), IDENTITY, scale=minus_one, bias=zero[:])
+        nc.scalar.activation(
+            dealt_out(w2_bf, slice(W2_SPLIT, P)), dealt_in(w2_right), IDENTITY, scale=minus_one, bias=zero[:]
+        )
         w2_neg_q = quantize_weight(w2_bf, "w2")
         y_neg[THIRD], y_neg[FOURTH] = w2_right_rows, y_last
         for t in (THIRD, FOURTH):
             nc.scalar.activation(y_neg[t][:, :S], y_acc[t][:], COPY, scale=-1.0)
-            gather_current(t, [slice(0, S)])
+            gather_current(t)
         turn(yt_acc[THIRD], y_neg[THIRD], True, True)
 
         partner = keep.tile([P, PACK, S], F32, name="partner", tag="partner")
@@ -247,12 +252,12 @@ def tile_picked_redq_none_po_kernel(
         out_rows = out_0.rearrange("(p u t) j -> p u t j", u=2, t=2)
         out_words = out_1[0].rearrange("p n t -> p (n t)").bitcast(I32)
         o_scales = keep.tile([P, S], U8, name="o_scales", align_bytes=64)
-        td_plain = placed.tile([P, 2, S], F32, name="td_plain", offset=13 * ROW - LAP)
+        td_plain = placed.tile([P, 2, S], F32, name="td_plain", offset=Y_LAST_AT + 2 * ROW - LAP)
         td_turned = [
             keep.tile([P, 2, HALF], F32, name="td_turned0"),
-            placed.tile([P, 2, HALF], F32, name="td_turned1", offset=7 * ROW + LAP),
+            placed.tile([P, 2, HALF], F32, name="td_turned1", offset=DISCOUNT_AT + LAP - ROW),
         ]
-        td_bf = placed.tile([P, S, 2, 2], BF16, name="td_bf", offset=8 * ROW + LAP, align_bytes=64)
+        td_bf = placed.tile([P, S, 2, 2], BF16, name="td_bf", offset=DISCOUNT_AT + LAP, align_bytes=64)
 
         def gather_next(td, t, cols):
             nc.vector.tensor_tensor(

@@ -17,25 +17,22 @@ U8 = mybir.dt.uint8
 FP8X4 = mybir.dt.float8_e4m3fn_x4
 ALU = mybir.AluOpType
 COPY = mybir.ActivationFunctionType.Copy
-IDENTITY = mybir.ActivationFunctionType.Identity
-RELU = mybir.ActivationFunctionType.Relu
 
 DISCOUNT = 0.9
 W1_SPLIT = 80
-W2_SPLIT = 56
+W2_SPLIT = 72
 HALF = 256
 QUARTER = 128
 END_SPLIT = 96
-FIRST, SECOND, THIRD, FOURTH = 0, 2, 3, 1
-PLAIN = (FIRST, FOURTH)
-TURNED = (SECOND, THIRD)
+EARLY = (0, 1)
+LATE = (2, 3)
 ROW = 4 * S
 SCALE_ROWS = K // 32
 SCALE_ROW0 = 16
 LAP = 64
-XS_AT = 4 * PACK * (N - PACK * W2_SPLIT) - LAP
-DISCOUNT_AT = 8 * ROW
-Y_LAST_AT = 11 * ROW
+XS_AT = 4 * PACK * PACK * W2_SPLIT + 2 * ROW - LAP
+W2R_AT = XS_AT + T - LAP
+W2R_END = W2R_AT + 4 * PACK * (N - PACK * W2_SPLIT)
 
 
 def tile_picked_redq_none_po_kernel(
@@ -57,18 +54,16 @@ def tile_picked_redq_none_po_kernel(
         xs = placed.tile([P, T], U8, name="xs", offset=XS_AT, align_bytes=64)
         rw_sb = keep.tile([P, S], F32, name="rw_sb")
 
-        y_last = placed.tile([P, 2 * S], F32, name="y_last", offset=Y_LAST_AT)
-        minus_one = y_last[:, :1]
-        nc.gpsimd.memset(minus_one, -1.0)
-        zero = keep.tile([P, 1], F32, name="zero", tag="partner")
-        nc.gpsimd.memset(zero[:], 0.0)
-        minus_discount = placed.tile([P, 2 * LAP // 4], F32, name="minus_discount", offset=DISCOUNT_AT)
-        nc.scalar.activation(minus_discount[:, :1], minus_one, COPY, scale=DISCOUNT)
+        one = keep.tile([P, 1], F32, name="one")
+        nc.gpsimd.memset(one[:], 1.0)
+        discount = keep.tile([P, 1], F32, name="discount")
+        nc.scalar.activation(discount[:], one[:], COPY, scale=DISCOUNT)
 
         nc.vector.memset(xs[:SCALE_ROW0, :].bitcast(I32), 0)
         nc.vector.memset(xs[32:64, :].bitcast(I32), 0)
         nc.vector.memset(xs[64:, :].bitcast(I32), 0)
-        w1_raw = keep.tile([P, PACK, N], F32, name="w1_raw")
+        w1_flat = keep.tile([P, PACK * N], F32, name="w1_flat")
+        w1_raw = w1_flat[:].rearrange("p (j c) -> p j c", j=PACK)
         w1_rows = w1.rearrange("(p j) c -> p j c", j=PACK)
         nc.sync.dma_start(w1_raw[:, :1], w1_rows[:, :1])
         nc.sync.dma_start(offs_sb[:], offs)
@@ -78,8 +73,8 @@ def tile_picked_redq_none_po_kernel(
         nc.scalar.dma_start(rw_quarters[P - PACK :, :], rw[0].rearrange("(b c) -> b c", b=PACK))
         nc.gpsimd.memset(rw_quarters[:96, :], 0.0)
         nc.gpsimd.memset(rw_quarters[96 : P - PACK, :], 0.0)
-        nc.sync.dma_start(xw[:], x_words[0].rearrange("p n t -> p (n t)").bitcast(I32))
         nc.sync.dma_start(cur_sb[:], cur)
+        nc.sync.dma_start(xw[:], x_words[0].rearrange("p n t -> p (n t)").bitcast(I32))
         nc.sync.dma_start(nx_sb[:], nx)
 
         xq_s = keep.tile([P, S], U8, name="xq_s", align_bytes=64)
@@ -93,19 +88,20 @@ def tile_picked_redq_none_po_kernel(
             )
         w2_rows = w2.rearrange("(p j) c -> p j c", j=PACK)
         w2_cut = PACK * W2_SPLIT
-        w2_left = placed.tile([P, PACK, w2_cut], F32, name="w2_left", offset=XS_AT + T - LAP)
-        w2_right_rows = placed.tile([P, PACK * (N - w2_cut)], F32, name="w2_right", offset=0)
-        w2_right = w2_right_rows[:].rearrange("p (j c) -> p j c", j=PACK)
+        w2_right = placed.tile([P, PACK, N - w2_cut], F32, name="w2_right", offset=W2R_AT)
+        left_words = PACK * w2_cut
+        work = placed.tile([P, left_words + 2 * S], F32, name="work", offset=0, align_bytes=64)
+        w2_left = work[:, :left_words].rearrange("p (j c) -> p j c", j=PACK)
         ident = keep.tile([P, P], F32, name="ident")
         make_identity(nc, ident[:])
-        nc.sync.dma_start(w2_left[:], w2_rows[:, :, :w2_cut])
-        nc.sync.dma_start(w2_right, w2_rows[:, :, w2_cut:])
+        nc.sync.dma_start(w2_left, w2_rows[:, :, :w2_cut])
+        nc.sync.dma_start(w2_right[:], w2_rows[:, :, w2_cut:])
 
         halves = [slice(h * HALF, (h + 1) * HALF) for h in range(S // HALF)]
         blocks = [slice(b * P, (b + 1) * P) for b in range(S // P)]
         stages = (halves[0], slice(HALF, HALF + QUARTER), slice(HALF + QUARTER, S))
 
-        rw_turned = bank("rw_turned", 4, P)
+        rw_turned = bank("rw_turned", 6, P)
         nc.tensor.transpose(rw_turned[:], rw_quarters[:], ident[:])
         rw_col = keep.tile([P, PACK], F32, name="rw_col")
         nc.scalar.copy(rw_col[:], rw_turned[:, P - PACK :])
@@ -117,7 +113,7 @@ def tile_picked_redq_none_po_kernel(
         xq_w = keep.tile([P, S], U32, name="xq_w", align_bytes=64)
 
         def dealt_out(grouped, groups):
-            return grouped[:].rearrange("p (t m j) -> p m j t", t=PACK, j=PACK)[:, groups]
+            return grouped.rearrange("p (t m j) -> p m j t", t=PACK, j=PACK)[:, groups]
 
         def dealt_in(raw):
             return raw.rearrange("p j (m t) -> p m j t", t=PACK)
@@ -125,7 +121,7 @@ def tile_picked_redq_none_po_kernel(
         def quantize_weight(grouped, name):
             codes = keep.tile([P, N], U32, name=f"{name}_codes", align_bytes=64)
             scales = keep.tile([P, N], U8, name=f"{name}_scales", align_bytes=64)
-            nc.vector.quantize_mx(out=codes[:].bitcast(FP8X4), scales=scales[:], in_=grouped[:])
+            nc.vector.quantize_mx(out=codes[:].bitcast(FP8X4), scales=scales[:], in_=grouped)
             return codes, scales
 
         def product(acc, weight, t, cols):
@@ -140,166 +136,122 @@ def tile_picked_redq_none_po_kernel(
                 stop=True,
             )
 
-        def turned_product(acc, weight, t, start, stop):
-            codes, scales = weight
-            for tokens in blocks:
-                nc.tensor.matmul_mx(
-                    out=acc[:, tokens],
-                    lhsT=xq_w[:, tokens].bitcast(FP8X4),
-                    lhsT_scale=xq_s[:, tokens],
-                    rhs=codes[:, blocks[t]].bitcast(FP8X4),
-                    rhs_scale=scales[:, blocks[t]],
-                    start=start and tokens.start == 0,
-                    stop=stop and tokens.stop == S,
-                )
-
-        def turn(acc, src, start, stop):
-            for cols in blocks:
-                nc.tensor.matmul(
-                    acc[:, cols],
-                    lhsT=src[:, cols],
-                    rhs=ident[:],
-                    start=start and cols.start == 0,
-                    stop=stop and cols.stop == S,
-                    is_transpose=True,
-                )
-
         def entries(cols):
             return slice(cols.start // 16, cols.stop // 16)
 
-        def within(td, cols):
-            first = cols.start // td.shape[2] * td.shape[2]
-            return slice(cols.start - first, cols.stop - first)
-
         w1_bf = keep.tile([P, PACK * N], BF16, name="w1_bf", align_bytes=64)
-        nc.vector.tensor_copy(dealt_out(w1_bf, slice(0, W1_SPLIT)), dealt_in(w1_raw[:])[:, :W1_SPLIT])
-        nc.scalar.activation(dealt_out(w1_bf, slice(W1_SPLIT, P)), dealt_in(w1_raw[:])[:, W1_SPLIT:], COPY)
-        w1_q = quantize_weight(w1_bf, "w1")
+        nc.vector.tensor_copy(dealt_out(w1_bf[:], slice(0, W1_SPLIT)), dealt_in(w1_raw)[:, :W1_SPLIT])
+        nc.scalar.activation(dealt_out(w1_bf[:], slice(W1_SPLIT, P)), dealt_in(w1_raw)[:, W1_SPLIT:], COPY)
+        w1_q = quantize_weight(w1_bf[:], "w1")
 
-        base = {
-            t: placed.tile([P, S], F32, name=f"base{t}", offset=XS_AT + T + i * ROW)
-            for i, t in enumerate((FIRST, SECOND))
-        }
-        for t in (THIRD, FOURTH):
-            base[t] = keep.tile([P, S], F32, name=f"base{t}")
-
-        y_neg = {}
-
-        def gather_current(t):
-            nc.vector.tensor_tensor(base[t][:], y_neg[t][:].indirect(cur_sb[:]), rw_sb[:], ALU.add)
-
-        for t in (FIRST, SECOND):
-            y_neg[t] = keep.tile([P, 2 * S], F32, name=f"y_neg{t}")
-            nc.gpsimd.memset(y_neg[t][:, S:], 0.0)
-        nc.gpsimd.memset(y_last[:, S:], 0.0)
-        low = {t: keep.tile([P, S], F32, name=f"low{t}") for t in (SECOND, THIRD, FOURTH)}
-        low[FIRST] = keep.tile([P, 2 * S], F32, name="low_first")
-        nc.gpsimd.memset(low[FIRST][:, S:], 0.0)
-        for cols in halves:
+        for cols in stages:
             nc.vector.tensor_copy(xq_w[:, cols], xw[:].bitcast(U32).indirect(offs_sb[:, entries(cols)]))
-        w2_bf = keep.tile([P, PACK * N], BF16, name="w2_bf", align_bytes=64)
-        nc.vector.tensor_scalar_mul(dealt_out(w2_bf, slice(0, W2_SPLIT)), dealt_in(w2_left[:]), -1.0)
+        w2_bf = work[:, left_words:].bitcast(BF16)
+        nc.vector.tensor_copy(dealt_out(w2_bf, slice(0, W2_SPLIT)), dealt_in(w2_left))
 
-        y_acc = {t: bank(f"y{t}", number) for t, number in ((THIRD, 5), (FOURTH, 6))}
-        y_acc[SECOND] = bank("y_second", 3, 2 * S)
+        debt = work[:, left_words - S : left_words + S].rearrange("p (t s) -> p t s", t=2)
+        y = {0: w1_flat}
+        spare = placed.tile([P, S], F32, name="spare", offset=W2R_END - LAP + ROW)
+        nc.gpsimd.memset(spare[:], 0.0)
+        y[1] = placed.tile([P, 2 * S], F32, name="y1", offset=W2R_END - LAP)
+        y[2] = placed.tile([P, S], F32, name="y2", offset=XS_AT + LAP + ROW)
+        y[3] = placed.tile([P, S], F32, name="y3", offset=XS_AT + LAP)
         for i, cols in enumerate(stages):
             piece = bank(f"y_first{i}", i, cols.stop - cols.start)
-            product(piece[:], w1_q, FIRST, cols)
-            if cols == halves[0]:
-                product(y_acc[SECOND][:, cols], w1_q, SECOND, cols)
-            nc.scalar.activation(y_neg[FIRST][:, cols], piece[:], COPY, scale=-1.0)
-        product(y_acc[SECOND][:, halves[1]], w1_q, SECOND, halves[1])
-        for t in (THIRD, FOURTH):
+            product(piece[:], w1_q, 0, cols)
+            nc.scalar.copy(y[0][:, cols], piece[:])
+        y_acc = {t: bank(f"y{t}", 2 + t) for t in (1, 2, 3)}
+        for t in (1, 2, 3):
             product(y_acc[t][:], w1_q, t, slice(0, S))
-        gather_current(FIRST)
-        nc.scalar.activation(y_neg[SECOND][:, :S], y_acc[SECOND][:, :S], COPY, scale=-1.0)
-        gather_current(SECOND)
-        yt_acc = {t: bank(f"yt{t}", number) for t, number in ((SECOND, 7), (THIRD, 1))}
-        turn(yt_acc[SECOND], y_neg[SECOND], True, True)
-        gap_acc = {t: bank(f"gap{t}", number)[:] for t, number in ((SECOND, 3), (THIRD, 4))}
-        for t in TURNED:
-            turned_product(gap_acc[t], w1_q, t, True, False)
+        nc.vector.tensor_tensor(debt[:, 0, :], y[0][:].indirect(cur_sb[:]), rw_sb[:], ALU.subtract)
+        nc.scalar.activation(dealt_out(w2_bf, slice(W2_SPLIT, P)), dealt_in(w2_right[:]), COPY)
+        w2_q = quantize_weight(w2_bf, "w2")
+        nc.scalar.copy(y[1][:, :S], y_acc[1][:])
+        nc.vector.tensor_tensor(debt[:, 1, :], y[1][:].indirect(cur_sb[:]), rw_sb[:], ALU.subtract)
 
-        nc.scalar.activation(
-            dealt_out(w2_bf, slice(W2_SPLIT, P)), dealt_in(w2_right), IDENTITY, scale=minus_one, bias=zero[:]
-        )
-        w2_neg_q = quantize_weight(w2_bf, "w2")
-        y_neg[THIRD], y_neg[FOURTH] = w2_right_rows, y_last
-        for t in (THIRD, FOURTH):
-            nc.scalar.activation(y_neg[t][:, :S], y_acc[t][:], COPY, scale=-1.0)
-            gather_current(t)
-        turn(yt_acc[THIRD], y_neg[THIRD], True, True)
+        seen = {}
+        for t in LATE:
+            nc.scalar.activation(y[t][:], y_acc[t][:], COPY, scale=discount[:])
+            seen[t] = keep.tile([P, S], F32, name=f"seen{t}")
+            for cols in halves:
+                nc.scalar.activation(seen[t][:, cols], y[t][:].indirect(cur_sb[:, entries(cols)]), COPY)
 
-        partner = keep.tile([P, PACK, S], F32, name="partner", tag="partner")
-        excess = {t: keep.tile([P, S], F32, name=f"excess{t}") for t in TURNED}
-        for t, number in ((FIRST, 0), (FOURTH, 2)):
-            nc.scalar.activation(partner[:, t, :], y_neg[t][:, :S], COPY, scale=-DISCOUNT)
-            e_neg = bank(f"e_neg{t}", number)
-            product(e_neg[:], w2_neg_q, t, slice(0, S))
-            nc.vector.scalar_tensor_tensor(low[t][:, :S], e_neg[:], -DISCOUNT, partner[:, t, :], ALU.mult, ALU.min)
-        for t in TURNED:
-            turned_product(gap_acc[t], w2_neg_q, t, False, True)
-        for t in TURNED:
-            nc.scalar.copy(partner[:, t, :], yt_acc[t][:])
-        for t in TURNED:
-            nc.scalar.activation(excess[t][:], gap_acc[t], RELU)
-        for t, number, scale in ((SECOND, 5, -DISCOUNT), (THIRD, 6, minus_discount[:, :1])):
-            min_neg = bank(f"min_neg{t}", number)
-            turn(min_neg, partner[:, t, :], True, False)
-            turn(min_neg, excess[t][:], False, True)
-            nc.scalar.activation(low[t][:], min_neg[:], COPY, scale=scale)
+        low = {}
+        for t, number in zip(range(PACK), (6, 7, 0, 1)):
+            e_acc = bank(f"e{t}", number)
+            product(e_acc[:], w2_q, t, slice(0, S))
+            low[t] = keep.tile([P, S], F32, name=f"low{t}")
+            if t in EARLY:
+                nc.vector.tensor_tensor(low[t][:], e_acc[:], y[t][:, :S], ALU.min)
+            else:
+                nc.vector.scalar_tensor_tensor(low[t][:], e_acc[:], DISCOUNT, y[t][:], ALU.mult, ALU.min)
+        base = y
+        for t in LATE:
+            nc.vector.scalar_tensor_tensor(base[t][:], seen[t][:], -1.0 / DISCOUNT, rw_sb[:], ALU.mult, ALU.add)
 
-        out_rows = out_0.rearrange("(p u t) j -> p u t j", u=2, t=2)
+        ahead = keep.tile([P, 2, S], F32, name="ahead")
+        for cols in halves:
+            for t in EARLY:
+                nc.scalar.activation(ahead[:, t, cols], low[t][:].indirect(nx_sb[:, entries(cols)]), COPY)
+
+        out_rows = out_0.rearrange("(p t) j -> p t j", t=PACK)
         out_words = out_1[0].rearrange("p n t -> p (n t)").bitcast(I32)
         o_scales = keep.tile([P, S], U8, name="o_scales", align_bytes=64)
-        td_plain = placed.tile([P, 2, S], F32, name="td_plain", offset=Y_LAST_AT + 2 * ROW - LAP)
-        td_turned = [
-            keep.tile([P, 2, HALF], F32, name="td_turned0"),
-            placed.tile([P, 2, HALF], F32, name="td_turned1", offset=DISCOUNT_AT + LAP - ROW),
-        ]
-        td_bf = placed.tile([P, S, 2, 2], BF16, name="td_bf", offset=DISCOUNT_AT + LAP, align_bytes=64)
+        td = [keep.tile([P, PACK, HALF], F32, name=f"td{h}") for h in range(2)]
+        td_bf = keep.tile([P, S, PACK], BF16, name="td_bf", align_bytes=64)
 
-        def gather_next(td, t, cols):
-            nc.vector.tensor_tensor(
-                td[:, t % 2, within(td, cols)], low[t][:].indirect(nx_sb[:, entries(cols)]), base[t][:, cols], ALU.add
+        def within(cols):
+            return slice(cols.start % HALF, (cols.stop - 1) % HALF + 1)
+
+        def join_early(h):
+            nc.vector.scalar_tensor_tensor(
+                td[h][:, :2, :], ahead[:, :, halves[h]], DISCOUNT, debt[:, :, halves[h]], ALU.mult, ALU.subtract
             )
 
-        def round_pair(td, u, cols, copy):
-            copy(td_bf[:, cols, u, :], td[:, :, within(td, cols)].rearrange("p t j -> p j t"))
+        def gather_late(cols):
+            for t in LATE:
+                nc.vector.tensor_tensor(
+                    td[cols.start // HALF][:, t, within(cols)],
+                    low[t][:].indirect(nx_sb[:, entries(cols)]),
+                    base[t][:, cols],
+                    ALU.add,
+                )
+
+        def round_result(cols, copy):
+            copy(
+                td_bf[:, cols, :].rearrange("p (c i) t -> p c t i", i=4),
+                td[cols.start // HALF][:, :, within(cols)].rearrange("p t (c i) -> p c t i", i=4),
+            )
+
+        o_codes = keep.tile([P, S], I32, name="o_codes", align_bytes=64)
 
         def quantize_result(cols):
-            o_codes = keep.tile([P, cols.stop - cols.start], I32, name=f"o_codes{cols.start}", align_bytes=64)
             nc.vector.quantize_mx(
-                out=o_codes[:].bitcast(FP8X4),
+                out=o_codes[:, cols].bitcast(FP8X4),
                 scales=o_scales[:, cols],
-                in_=td_bf[:, cols].rearrange("p j u t -> p (j u t)"),
+                in_=td_bf[:, cols].rearrange("p j t -> p (j t)"),
             )
-            nc.sync.dma_start(out_words[:, cols], o_codes[:])
 
-        gather_next(td_plain, FIRST, slice(0, S))
-        for cols in halves:
-            gather_next(td_plain, FOURTH, cols)
-            round_pair(td_plain, 0, cols, nc.scalar.copy)
-        nc.sync.dma_start(out_rows[:, 0], td_plain[:])
-        td = td_turned[0]
-        for t in TURNED:
-            gather_next(td, t, halves[0])
-        round_pair(td, 1, halves[0], nc.scalar.copy)
-        nc.sync.dma_start(out_rows[:, 1, :, halves[0]], td[:])
-        td = td_turned[1]
-        for t in TURNED:
-            gather_next(td, t, stages[1])
-        round_pair(td, 1, stages[1], nc.scalar.copy)
+        gather_late(halves[0])
+        nc.sync.dma_start(out_rows[:, 2:, halves[0]], td[0][:, 2:])
+        join_early(0)
+        nc.sync.dma_start(out_rows[:, :2, halves[0]], td[0][:, :2])
+        round_result(halves[0], nc.scalar.copy)
+        gather_late(stages[1])
+        join_early(1)
+        nc.sync.dma_start(out_rows[:, :2, halves[1]], td[1][:, :2])
+        round_result(stages[1], nc.scalar.copy)
         last = stages[2]
-        for t in TURNED:
-            gather_next(td, t, last)
-        nc.sync.dma_start(out_rows[:, 1, :, halves[1]], td[:])
+        gather_late(last)
+        nc.sync.dma_start(out_rows[:, 2:, halves[1]], td[1][:, 2:])
         quantize_result(stages[0])
         cut = last.start + END_SPLIT
-        round_pair(td, 1, slice(last.start, cut), nc.vector.tensor_copy)
-        round_pair(td, 1, slice(cut, last.stop), nc.scalar.copy)
+        round_result(slice(last.start, cut), nc.vector.tensor_copy)
+        round_result(slice(cut, last.stop), nc.scalar.copy)
         quantize_result(stages[1])
+        nc.sync.dma_start(out_words[:, : last.start], o_codes[:, : last.start])
         quantize_result(last)
+        nc.sync.dma_start(out_words[:, last], o_codes[:, last])
         for q in range(4):
             queue = nc.scalar if q % 2 else nc.sync
             queue.dma_start(

@@ -20,7 +20,7 @@ COPY = mybir.ActivationFunctionType.Copy
 
 DISCOUNT = 0.9
 W1_SPLIT = 80
-W2_SPLIT = 72
+W2_SPLIT = 56
 HALF = 256
 QUARTER = 128
 END_SPLIT = 96
@@ -30,9 +30,8 @@ ROW = 4 * S
 SCALE_ROWS = K // 32
 SCALE_ROW0 = 16
 LAP = 64
-XS_AT = 4 * PACK * PACK * W2_SPLIT + 2 * ROW - LAP
+XS_AT = 4 * ROW - LAP
 W2R_AT = XS_AT + T - LAP
-W2R_END = W2R_AT + 4 * PACK * (N - PACK * W2_SPLIT)
 
 
 def tile_picked_redq_none_po_kernel(
@@ -90,8 +89,8 @@ def tile_picked_redq_none_po_kernel(
         w2_cut = PACK * W2_SPLIT
         w2_right = placed.tile([P, PACK, N - w2_cut], F32, name="w2_right", offset=W2R_AT)
         left_words = PACK * w2_cut
-        work = placed.tile([P, left_words + 2 * S], F32, name="work", offset=0, align_bytes=64)
-        w2_left = work[:, :left_words].rearrange("p (j c) -> p j c", j=PACK)
+        work = placed.tile([P, 4 * S], F32, name="work", offset=0, align_bytes=64)
+        w2_left = work[:, 2 * S - left_words : 2 * S].rearrange("p (j c) -> p j c", j=PACK)
         ident = keep.tile([P, P], F32, name="ident")
         make_identity(nc, ident[:])
         nc.sync.dma_start(w2_left, w2_rows[:, :, :w2_cut])
@@ -146,16 +145,15 @@ def tile_picked_redq_none_po_kernel(
 
         for cols in stages:
             nc.vector.tensor_copy(xq_w[:, cols], xw[:].bitcast(U32).indirect(offs_sb[:, entries(cols)]))
-        w2_bf = work[:, left_words:].bitcast(BF16)
+        w2_bf = work[:, 2 * S :].bitcast(BF16)
         nc.vector.tensor_copy(dealt_out(w2_bf, slice(0, W2_SPLIT)), dealt_in(w2_left))
 
-        debt = work[:, left_words - S : left_words + S].rearrange("p (t s) -> p t s", t=2)
+        debt = work[:].rearrange("p (t s) -> p t s", t=PACK)
         y = {0: w1_flat}
-        spare = placed.tile([P, S], F32, name="spare", offset=W2R_END - LAP + ROW)
-        nc.gpsimd.memset(spare[:], 0.0)
-        y[1] = placed.tile([P, 2 * S], F32, name="y1", offset=W2R_END - LAP)
-        y[2] = placed.tile([P, S], F32, name="y2", offset=XS_AT + LAP + ROW)
-        y[3] = placed.tile([P, S], F32, name="y3", offset=XS_AT + LAP)
+        y[1] = keep.tile([P, 2 * S], F32, name="y1")
+        nc.gpsimd.memset(y[1][:, S:], 0.0)
+        y[2] = placed.tile([P, 2 * S], F32, name="y2", offset=W2R_AT + 2 * LAP)
+        y[3] = placed.tile([P, S], F32, name="y3", offset=W2R_AT + 2 * LAP - ROW)
         for i, cols in enumerate(stages):
             piece = bank(f"y_first{i}", i, cols.stop - cols.start)
             product(piece[:], w1_q, 0, cols)
@@ -164,30 +162,31 @@ def tile_picked_redq_none_po_kernel(
         for t in (1, 2, 3):
             product(y_acc[t][:], w1_q, t, slice(0, S))
         nc.vector.tensor_tensor(debt[:, 0, :], y[0][:].indirect(cur_sb[:]), rw_sb[:], ALU.subtract)
-        nc.scalar.activation(dealt_out(w2_bf, slice(W2_SPLIT, P)), dealt_in(w2_right[:]), COPY)
-        w2_q = quantize_weight(w2_bf, "w2")
         nc.scalar.copy(y[1][:, :S], y_acc[1][:])
         nc.vector.tensor_tensor(debt[:, 1, :], y[1][:].indirect(cur_sb[:]), rw_sb[:], ALU.subtract)
+        nc.scalar.activation(dealt_out(w2_bf, slice(W2_SPLIT, P)), dealt_in(w2_right[:]), COPY)
+        w2_q = quantize_weight(w2_bf, "w2")
+        nc.scalar.copy(y[2][:, :S], y_acc[2][:])
+        nc.vector.tensor_tensor(debt[:, 2, :], y[2][:].indirect(cur_sb[:]), rw_sb[:], ALU.subtract)
 
-        seen = {}
-        for t in LATE:
-            nc.scalar.activation(y[t][:], y_acc[t][:], COPY, scale=discount[:])
-            seen[t] = keep.tile([P, S], F32, name=f"seen{t}")
-            for cols in halves:
-                nc.scalar.activation(seen[t][:, cols], y[t][:].indirect(cur_sb[:, entries(cols)]), COPY)
+        seen = keep.tile([P, S], F32, name="seen")
+        nc.scalar.activation(y[3][:], y_acc[3][:], COPY, scale=discount[:])
+        partner = {2: keep.tile([P, S], F32, name="partner"), 3: y[3]}
+        nc.scalar.activation(partner[2][:], y_acc[2][:], COPY, scale=discount[:])
+        for cols in halves:
+            nc.scalar.activation(seen[:, cols], y[3][:].indirect(cur_sb[:, entries(cols)]), COPY)
 
         low = {}
-        for t, number in zip(range(PACK), (6, 7, 0, 1)):
+        for t, number in zip((0, 1, 3, 2), (6, 7, 0, 1)):
             e_acc = bank(f"e{t}", number)
             product(e_acc[:], w2_q, t, slice(0, S))
             low[t] = keep.tile([P, S], F32, name=f"low{t}")
             if t in EARLY:
                 nc.vector.tensor_tensor(low[t][:], e_acc[:], y[t][:, :S], ALU.min)
             else:
-                nc.vector.scalar_tensor_tensor(low[t][:], e_acc[:], DISCOUNT, y[t][:], ALU.mult, ALU.min)
-        base = y
-        for t in LATE:
-            nc.vector.scalar_tensor_tensor(base[t][:], seen[t][:], -1.0 / DISCOUNT, rw_sb[:], ALU.mult, ALU.add)
+                nc.vector.scalar_tensor_tensor(low[t][:], e_acc[:], DISCOUNT, partner[t][:], ALU.mult, ALU.min)
+        debt_late = {2: debt[:, 2, :], 3: y[3][:]}
+        nc.vector.scalar_tensor_tensor(debt_late[3], seen[:], 1.0 / DISCOUNT, rw_sb[:], ALU.mult, ALU.subtract)
 
         ahead = keep.tile([P, 2, S], F32, name="ahead")
         for cols in halves:
@@ -205,7 +204,7 @@ def tile_picked_redq_none_po_kernel(
 
         def join_early(h):
             nc.vector.scalar_tensor_tensor(
-                td[h][:, :2, :], ahead[:, :, halves[h]], DISCOUNT, debt[:, :, halves[h]], ALU.mult, ALU.subtract
+                td[h][:, :2, :], ahead[:, :, halves[h]], DISCOUNT, debt[:, :2, halves[h]], ALU.mult, ALU.subtract
             )
 
         def gather_late(cols):
@@ -213,8 +212,8 @@ def tile_picked_redq_none_po_kernel(
                 nc.vector.tensor_tensor(
                     td[cols.start // HALF][:, t, within(cols)],
                     low[t][:].indirect(nx_sb[:, entries(cols)]),
-                    base[t][:, cols],
-                    ALU.add,
+                    debt_late[t][:, cols],
+                    ALU.subtract,
                 )
 
         def round_result(cols, copy):
@@ -237,21 +236,21 @@ def tile_picked_redq_none_po_kernel(
         join_early(0)
         nc.sync.dma_start(out_rows[:, :2, halves[0]], td[0][:, :2])
         round_result(halves[0], nc.scalar.copy)
-        gather_late(stages[1])
         join_early(1)
         nc.sync.dma_start(out_rows[:, :2, halves[1]], td[1][:, :2])
+        gather_late(stages[1])
         round_result(stages[1], nc.scalar.copy)
         last = stages[2]
         gather_late(last)
         nc.sync.dma_start(out_rows[:, 2:, halves[1]], td[1][:, 2:])
         quantize_result(stages[0])
+        nc.sync.dma_start(out_words[:, halves[0]], o_codes[:, halves[0]])
         cut = last.start + END_SPLIT
         round_result(slice(last.start, cut), nc.vector.tensor_copy)
         round_result(slice(cut, last.stop), nc.scalar.copy)
         quantize_result(stages[1])
-        nc.sync.dma_start(out_words[:, : last.start], o_codes[:, : last.start])
         quantize_result(last)
-        nc.sync.dma_start(out_words[:, last], o_codes[:, last])
+        nc.sync.dma_start(out_words[:, halves[1]], o_codes[:, halves[1]])
         for q in range(4):
             queue = nc.scalar if q % 2 else nc.sync
             queue.dma_start(

@@ -173,11 +173,13 @@ def tile_picked_redq_none_po_kernel(
         nc.scalar.activation(y[3][:], y_acc[3][:], COPY, scale=discount[:])
         partner = {2: keep.tile([P, S], F32, name="partner"), 3: y[3]}
         nc.scalar.activation(partner[2][:], y_acc[2][:], COPY, scale=discount[:])
+        debt_late = {2: debt[:, 2, :], 3: y[2][:, S:]}
         for cols in halves:
-            nc.scalar.activation(seen[:, cols], y[3][:].indirect(cur_sb[:, entries(cols)]), COPY)
+            nc.scalar.activation(seen[:, cols], y[3][:].indirect(cur_sb[:, entries(cols)]), COPY, scale=1.0 / DISCOUNT)
+            nc.gpsimd.tensor_tensor(debt_late[3][:, cols], seen[:, cols], rw_sb[:, cols], ALU.subtract)
 
         low = {}
-        for t, number in zip((0, 1, 3, 2), (6, 7, 0, 1)):
+        for t, number in zip(range(PACK), (6, 7, 0, 1)):
             e_acc = bank(f"e{t}", number)
             product(e_acc[:], w2_q, t, slice(0, S))
             low[t] = keep.tile([P, S], F32, name=f"low{t}")
@@ -185,13 +187,17 @@ def tile_picked_redq_none_po_kernel(
                 nc.vector.tensor_tensor(low[t][:], e_acc[:], y[t][:, :S], ALU.min)
             else:
                 nc.vector.scalar_tensor_tensor(low[t][:], e_acc[:], DISCOUNT, partner[t][:], ALU.mult, ALU.min)
-        debt_late = {2: debt[:, 2, :], 3: y[3][:]}
-        nc.vector.scalar_tensor_tensor(debt_late[3], seen[:], 1.0 / DISCOUNT, rw_sb[:], ALU.mult, ALU.subtract)
 
-        ahead = keep.tile([P, 2, S], F32, name="ahead")
-        for cols in halves:
-            for t in EARLY:
-                nc.scalar.activation(ahead[:, t, cols], low[t][:].indirect(nx_sb[:, entries(cols)]), COPY)
+        shared = (EARLY, EARLY + LATE[:1])
+        ahead = [keep.tile([P, len(shared[h]), HALF], F32, name=f"ahead{h}") for h in range(2)]
+        for h, cols in enumerate(halves):
+            for t in shared[h]:
+                nc.scalar.activation(
+                    ahead[h][:, t, :],
+                    low[t][:].indirect(nx_sb[:, entries(cols)]),
+                    COPY,
+                    scale=DISCOUNT if t in EARLY else 1.0,
+                )
 
         out_rows = out_0.rearrange("(p t) j -> p t j", t=PACK)
         out_words = out_1[0].rearrange("p n t -> p (n t)").bitcast(I32)
@@ -202,13 +208,11 @@ def tile_picked_redq_none_po_kernel(
         def within(cols):
             return slice(cols.start % HALF, (cols.stop - 1) % HALF + 1)
 
-        def join_early(h):
-            nc.vector.scalar_tensor_tensor(
-                td[h][:, :2, :], ahead[:, :, halves[h]], DISCOUNT, debt[:, :2, halves[h]], ALU.mult, ALU.subtract
-            )
+        def join(h, planes):
+            nc.vector.tensor_tensor(td[h][:, planes, :], ahead[h][:, planes], debt[:, planes, halves[h]], ALU.subtract)
 
         def gather_late(cols):
-            for t in LATE:
+            for t in range(len(shared[cols.start // HALF]), PACK):
                 nc.vector.tensor_tensor(
                     td[cols.start // HALF][:, t, within(cols)],
                     low[t][:].indirect(nx_sb[:, entries(cols)]),
@@ -233,12 +237,13 @@ def tile_picked_redq_none_po_kernel(
 
         gather_late(halves[0])
         nc.sync.dma_start(out_rows[:, 2:, halves[0]], td[0][:, 2:])
-        join_early(0)
+        join(0, slice(0, 2))
         nc.sync.dma_start(out_rows[:, :2, halves[0]], td[0][:, :2])
         round_result(halves[0], nc.scalar.copy)
-        join_early(1)
+        join(1, slice(0, 2))
         nc.sync.dma_start(out_rows[:, :2, halves[1]], td[1][:, :2])
         gather_late(stages[1])
+        join(1, slice(2, 3))
         round_result(stages[1], nc.scalar.copy)
         last = stages[2]
         gather_late(last)

@@ -20,7 +20,7 @@ COPY = mybir.ActivationFunctionType.Copy
 
 DISCOUNT = 0.9
 W1_SPLIT = 80
-W2_SPLIT = 56
+W2_SPLIT = 64
 HALF = 256
 QUARTER = 128
 END_SPLIT = 96
@@ -108,6 +108,8 @@ def tile_picked_redq_none_po_kernel(
         for b, cols in enumerate(blocks):
             nc.tensor.transpose(rw_acc[:, cols], rw_col[:, b : b + 1].to_broadcast([P, P]), ident[:])
         nc.scalar.copy(rw_sb[:], rw_acc[:])
+        rw_scaled = keep.tile([P, HALF], F32, name="rw_scaled")
+        nc.scalar.activation(rw_scaled[:], rw_acc[:, halves[1]], COPY, scale=DISCOUNT)
 
         xq_w = keep.tile([P, S], U32, name="xq_w", align_bytes=64)
 
@@ -148,12 +150,26 @@ def tile_picked_redq_none_po_kernel(
         w2_bf = work[:, 2 * S :].bitcast(BF16)
         nc.vector.tensor_copy(dealt_out(w2_bf, slice(0, W2_SPLIT)), dealt_in(w2_left))
 
-        debt = work[:].rearrange("p (t s) -> p t s", t=PACK)
+        debt_pair = [
+            work[:].rearrange("p (t s) -> p t s", t=PACK)[:, :2, halves[0]],
+            work[:].rearrange("p (t s) -> p t s", t=2)[:, :, halves[1]],
+        ]
         y = {0: w1_flat}
-        y[1] = keep.tile([P, 2 * S], F32, name="y1")
-        nc.gpsimd.memset(y[1][:, S:], 0.0)
-        y[2] = placed.tile([P, 2 * S], F32, name="y2", offset=W2R_AT + 2 * LAP)
-        y[3] = placed.tile([P, S], F32, name="y3", offset=W2R_AT + 2 * LAP - ROW)
+        y[1] = keep.tile([P, S], F32, name="y1")
+        y[2] = placed.tile([P, 2 * S], F32, name="y2", offset=4 * ROW)
+        y[3] = placed.tile([P, S], F32, name="y3", offset=6 * ROW)
+        debt = {
+            (1, 0): debt_pair[0][:, 1, :],
+            (1, 1): debt_pair[1][:, 1, :],
+            (2, 0): y[2][:, S : S + HALF],
+            (2, 1): work[:, 3 * S : 3 * S + HALF],
+            (3, 0): y[2][:, S + HALF :],
+            (3, 1): rw_scaled[:],
+        }
+
+        def current(t, h):
+            return y[t][:].indirect(cur_sb[:, entries(halves[h])])
+
         for i, cols in enumerate(stages):
             piece = bank(f"y_first{i}", i, cols.stop - cols.start)
             product(piece[:], w1_q, 0, cols)
@@ -161,22 +177,19 @@ def tile_picked_redq_none_po_kernel(
         y_acc = {t: bank(f"y{t}", 2 + t) for t in (1, 2, 3)}
         for t in (1, 2, 3):
             product(y_acc[t][:], w1_q, t, slice(0, S))
-        nc.vector.tensor_tensor(debt[:, 0, :], y[0][:].indirect(cur_sb[:]), rw_sb[:], ALU.subtract)
+        nc.vector.tensor_tensor(work[:, :S], y[0][:].indirect(cur_sb[:]), rw_sb[:], ALU.subtract)
         nc.scalar.copy(y[1][:, :S], y_acc[1][:])
-        nc.vector.tensor_tensor(debt[:, 1, :], y[1][:].indirect(cur_sb[:]), rw_sb[:], ALU.subtract)
+        nc.vector.tensor_tensor(debt[1, 0], current(1, 0), rw_sb[:, halves[0]], ALU.subtract)
         nc.scalar.activation(dealt_out(w2_bf, slice(W2_SPLIT, P)), dealt_in(w2_right[:]), COPY)
         w2_q = quantize_weight(w2_bf, "w2")
-        nc.scalar.copy(y[2][:, :S], y_acc[2][:])
-        nc.vector.tensor_tensor(debt[:, 2, :], y[2][:].indirect(cur_sb[:]), rw_sb[:], ALU.subtract)
-
-        seen = keep.tile([P, S], F32, name="seen")
-        nc.scalar.activation(y[3][:], y_acc[3][:], COPY, scale=discount[:])
-        partner = {2: keep.tile([P, S], F32, name="partner"), 3: y[3]}
-        nc.scalar.activation(partner[2][:], y_acc[2][:], COPY, scale=discount[:])
-        debt_late = {2: debt[:, 2, :], 3: y[2][:, S:]}
-        for cols in halves:
-            nc.scalar.activation(seen[:, cols], y[3][:].indirect(cur_sb[:, entries(cols)]), COPY, scale=1.0 / DISCOUNT)
-            nc.gpsimd.tensor_tensor(debt_late[3][:, cols], seen[:, cols], rw_sb[:, cols], ALU.subtract)
+        nc.vector.tensor_tensor(debt[1, 1], current(1, 1), rw_sb[:, halves[1]], ALU.subtract)
+        for t in LATE:
+            nc.scalar.activation(y[t][:, :S], y_acc[t][:], COPY, scale=discount[:])
+        nc.vector.tensor_tensor(debt[2, 1], current(2, 1), rw_scaled[:], ALU.subtract)
+        for t, h in ((2, 0), (3, 0), (3, 1)):
+            seen = keep.tile([P, HALF], F32, name=f"seen{t}{h}")
+            nc.scalar.activation(seen[:], current(t, h), COPY, scale=1.0 / DISCOUNT)
+            nc.gpsimd.tensor_tensor(debt[t, h], seen[:], rw_sb[:, halves[h]], ALU.subtract)
 
         low = {}
         for t, number in zip(range(PACK), (6, 7, 0, 1)):
@@ -186,7 +199,7 @@ def tile_picked_redq_none_po_kernel(
             if t in EARLY:
                 nc.vector.tensor_tensor(low[t][:], e_acc[:], y[t][:, :S], ALU.min)
             else:
-                nc.vector.scalar_tensor_tensor(low[t][:], e_acc[:], DISCOUNT, partner[t][:], ALU.mult, ALU.min)
+                nc.vector.scalar_tensor_tensor(low[t][:], e_acc[:], DISCOUNT, y[t][:, :S], ALU.mult, ALU.min)
 
         shared = (EARLY, EARLY + LATE[:1])
         ahead = [keep.tile([P, len(shared[h]), HALF], F32, name=f"ahead{h}") for h in range(2)]
@@ -208,15 +221,15 @@ def tile_picked_redq_none_po_kernel(
         def within(cols):
             return slice(cols.start % HALF, (cols.stop - 1) % HALF + 1)
 
-        def join(h, planes):
-            nc.vector.tensor_tensor(td[h][:, planes, :], ahead[h][:, planes], debt[:, planes, halves[h]], ALU.subtract)
+        def join(h):
+            nc.vector.tensor_tensor(td[h][:, :2, :], ahead[h][:, :2], debt_pair[h], ALU.subtract)
 
         def gather_late(cols):
             for t in range(len(shared[cols.start // HALF]), PACK):
                 nc.vector.tensor_tensor(
                     td[cols.start // HALF][:, t, within(cols)],
                     low[t][:].indirect(nx_sb[:, entries(cols)]),
-                    debt_late[t][:, cols],
+                    debt[t, cols.start // HALF][:, within(cols)],
                     ALU.subtract,
                 )
 
@@ -237,13 +250,13 @@ def tile_picked_redq_none_po_kernel(
 
         gather_late(halves[0])
         nc.sync.dma_start(out_rows[:, 2:, halves[0]], td[0][:, 2:])
-        join(0, slice(0, 2))
+        join(0)
         nc.sync.dma_start(out_rows[:, :2, halves[0]], td[0][:, :2])
         round_result(halves[0], nc.scalar.copy)
-        join(1, slice(0, 2))
+        join(1)
         nc.sync.dma_start(out_rows[:, :2, halves[1]], td[1][:, :2])
         gather_late(stages[1])
-        join(1, slice(2, 3))
+        nc.vector.scalar_tensor_tensor(td[1][:, 2, :], debt[2, 1], -1.0 / DISCOUNT, ahead[1][:, 2], ALU.mult, ALU.add)
         round_result(stages[1], nc.scalar.copy)
         last = stages[2]
         gather_late(last)

@@ -23,7 +23,6 @@ W1_SPLIT = 80
 W2_SPLIT = 64
 HALF = 256
 QUARTER = 128
-END_SPLIT = 96
 EARLY = (0, 1)
 LATE = (2, 3)
 ROW = 4 * S
@@ -161,10 +160,10 @@ def tile_picked_redq_none_po_kernel(
         debt = {
             (1, 0): debt_pair[0][:, 1, :],
             (1, 1): debt_pair[1][:, 1, :],
-            (2, 0): y[2][:, S : S + HALF],
+            (2, 0): rw_scaled[:],
             (2, 1): work[:, 3 * S : 3 * S + HALF],
-            (3, 0): y[2][:, S + HALF :],
-            (3, 1): rw_scaled[:],
+            (3, 0): y[2][:, S : S + HALF],
+            (3, 1): y[2][:, S + HALF :],
         }
 
         def current(t, h):
@@ -174,11 +173,17 @@ def tile_picked_redq_none_po_kernel(
             piece = bank(f"y_first{i}", i, cols.stop - cols.start)
             product(piece[:], w1_q, 0, cols)
             nc.scalar.copy(y[0][:, cols], piece[:])
-        y_acc = {t: bank(f"y{t}", 2 + t) for t in (1, 2, 3)}
-        for t in (1, 2, 3):
+            if cols == halves[0]:
+                piece = bank("y_second0", 3, HALF)
+                product(piece[:], w1_q, 1, cols)
+                nc.scalar.copy(y[1][:, cols], piece[:])
+        second_rest = bank("y_second1", 6, HALF)
+        product(second_rest[:], w1_q, 1, halves[1])
+        y_acc = {t: bank(f"y{t}", 2 + t) for t in LATE}
+        for t in LATE:
             product(y_acc[t][:], w1_q, t, slice(0, S))
         nc.vector.tensor_tensor(work[:, :S], y[0][:].indirect(cur_sb[:]), rw_sb[:], ALU.subtract)
-        nc.scalar.copy(y[1][:, :S], y_acc[1][:])
+        nc.scalar.copy(y[1][:, halves[1]], second_rest[:])
         nc.vector.tensor_tensor(debt[1, 0], current(1, 0), rw_sb[:, halves[0]], ALU.subtract)
         nc.scalar.activation(dealt_out(w2_bf, slice(W2_SPLIT, P)), dealt_in(w2_right[:]), COPY)
         w2_q = quantize_weight(w2_bf, "w2")
@@ -186,13 +191,14 @@ def tile_picked_redq_none_po_kernel(
         for t in LATE:
             nc.scalar.activation(y[t][:, :S], y_acc[t][:], COPY, scale=discount[:])
         nc.vector.tensor_tensor(debt[2, 1], current(2, 1), rw_scaled[:], ALU.subtract)
+        seen = {t: keep.tile([P, S], F32, name=f"seen{t}") for t in LATE}
         for t, h in ((2, 0), (3, 0), (3, 1)):
-            seen = keep.tile([P, HALF], F32, name=f"seen{t}{h}")
-            nc.scalar.activation(seen[:], current(t, h), COPY, scale=1.0 / DISCOUNT)
-            nc.gpsimd.tensor_tensor(debt[t, h], seen[:], rw_sb[:, halves[h]], ALU.subtract)
+            nc.scalar.activation(seen[t][:, halves[h]], current(t, h), COPY, scale=1.0 / DISCOUNT)
+        nc.gpsimd.tensor_tensor(debt[2, 0], seen[2][:, halves[0]], rw_sb[:, halves[0]], ALU.subtract)
+        nc.gpsimd.tensor_tensor(y[2][:, S:], seen[3][:], rw_sb[:], ALU.subtract)
 
         low = {}
-        for t, number in zip(range(PACK), (6, 7, 0, 1)):
+        for t, number in zip(range(PACK), (7, 0, 1, 2)):
             e_acc = bank(f"e{t}", number)
             product(e_acc[:], w2_q, t, slice(0, S))
             low[t] = keep.tile([P, S], F32, name=f"low{t}")
@@ -263,9 +269,7 @@ def tile_picked_redq_none_po_kernel(
         nc.sync.dma_start(out_rows[:, 2:, halves[1]], td[1][:, 2:])
         quantize_result(stages[0])
         nc.sync.dma_start(out_words[:, halves[0]], o_codes[:, halves[0]])
-        cut = last.start + END_SPLIT
-        round_result(slice(last.start, cut), nc.vector.tensor_copy)
-        round_result(slice(cut, last.stop), nc.scalar.copy)
+        round_result(last, nc.vector.tensor_copy)
         quantize_result(stages[1])
         quantize_result(last)
         nc.sync.dma_start(out_words[:, halves[1]], o_codes[:, halves[1]])

@@ -108,7 +108,7 @@ def tile_picked_redq_none_po_kernel(
             nc.tensor.transpose(rw_acc[:, cols], rw_col[:, b : b + 1].to_broadcast([P, P]), ident[:])
         nc.scalar.copy(rw_sb[:], rw_acc[:])
         rw_scaled = keep.tile([P, HALF], F32, name="rw_scaled")
-        nc.scalar.activation(rw_scaled[:], rw_acc[:, halves[1]], COPY, scale=DISCOUNT)
+        nc.scalar.activation(rw_scaled[:], rw_acc[:, halves[1]], COPY, scale=discount[:])
 
         xq_w = keep.tile([P, S], U32, name="xq_w", align_bytes=64)
 
@@ -118,10 +118,15 @@ def tile_picked_redq_none_po_kernel(
         def dealt_in(raw):
             return raw.rearrange("p j (m t) -> p m j t", t=PACK)
 
-        def quantize_weight(grouped, name):
+        def quantize_weight(grouped, name, parts):
             codes = keep.tile([P, N], U32, name=f"{name}_codes", align_bytes=64)
             scales = keep.tile([P, N], U8, name=f"{name}_scales", align_bytes=64)
-            nc.vector.quantize_mx(out=codes[:].bitcast(FP8X4), scales=scales[:], in_=grouped)
+            for cols in parts:
+                nc.vector.quantize_mx(
+                    out=codes[:, cols].bitcast(FP8X4),
+                    scales=scales[:, cols],
+                    in_=grouped[:, PACK * cols.start : PACK * cols.stop],
+                )
             return codes, scales
 
         def product(acc, weight, t, cols):
@@ -142,7 +147,7 @@ def tile_picked_redq_none_po_kernel(
         w1_bf = keep.tile([P, PACK * N], BF16, name="w1_bf", align_bytes=64)
         nc.vector.tensor_copy(dealt_out(w1_bf[:], slice(0, W1_SPLIT)), dealt_in(w1_raw)[:, :W1_SPLIT])
         nc.scalar.activation(dealt_out(w1_bf[:], slice(W1_SPLIT, P)), dealt_in(w1_raw)[:, W1_SPLIT:], COPY)
-        w1_q = quantize_weight(w1_bf[:], "w1")
+        w1_q = quantize_weight(w1_bf[:], "w1", [slice(0, N)])
 
         for cols in stages:
             nc.vector.tensor_copy(xq_w[:, cols], xw[:].bitcast(U32).indirect(offs_sb[:, entries(cols)]))
@@ -151,17 +156,16 @@ def tile_picked_redq_none_po_kernel(
 
         debt_pair = [
             work[:].rearrange("p (t s) -> p t s", t=PACK)[:, :2, halves[0]],
-            work[:].rearrange("p (t s) -> p t s", t=2)[:, :, halves[1]],
+            work[:].rearrange("p (t s) -> p t s", t=PACK)[:, :2, halves[1]],
         ]
         y = {0: w1_flat}
-        y[1] = keep.tile([P, S], F32, name="y1")
-        y[2] = placed.tile([P, 2 * S], F32, name="y2", offset=4 * ROW)
-        y[3] = placed.tile([P, S], F32, name="y3", offset=6 * ROW)
+        for t in (1, 2):
+            y[t] = keep.tile([P, 2 * S], F32, name=f"y{t}")
+            nc.gpsimd.memset(y[t][:, S:], 0.0)
+        y[3] = placed.tile([P, 2 * S], F32, name="y3", offset=4 * ROW)
         debt = {
-            (1, 0): debt_pair[0][:, 1, :],
-            (1, 1): debt_pair[1][:, 1, :],
             (2, 0): rw_scaled[:],
-            (2, 1): work[:, 3 * S : 3 * S + HALF],
+            (2, 1): work[:, 2 * S : 2 * S + HALF],
             (3, 0): y[2][:, S : S + HALF],
             (3, 1): y[2][:, S + HALF :],
         }
@@ -184,16 +188,15 @@ def tile_picked_redq_none_po_kernel(
             product(y_acc[t][:], w1_q, t, slice(0, S))
         nc.vector.tensor_tensor(work[:, :S], y[0][:].indirect(cur_sb[:]), rw_sb[:], ALU.subtract)
         nc.scalar.copy(y[1][:, halves[1]], second_rest[:])
-        nc.vector.tensor_tensor(debt[1, 0], current(1, 0), rw_sb[:, halves[0]], ALU.subtract)
+        nc.vector.tensor_tensor(work[:, S : 2 * S], y[1][:].indirect(cur_sb[:]), rw_sb[:], ALU.subtract)
+        nc.scalar.activation(y[2][:, :S], y_acc[2][:], COPY, scale=DISCOUNT)
         nc.scalar.activation(dealt_out(w2_bf, slice(W2_SPLIT, P)), dealt_in(w2_right[:]), COPY)
-        w2_q = quantize_weight(w2_bf, "w2")
-        nc.vector.tensor_tensor(debt[1, 1], current(1, 1), rw_sb[:, halves[1]], ALU.subtract)
-        for t in LATE:
-            nc.scalar.activation(y[t][:, :S], y_acc[t][:], COPY, scale=discount[:])
+        w2_q = quantize_weight(w2_bf, "w2", [slice(0, P), slice(P, N)])
+        nc.scalar.activation(y[3][:, :S], y_acc[3][:], COPY, scale=DISCOUNT)
         nc.vector.tensor_tensor(debt[2, 1], current(2, 1), rw_scaled[:], ALU.subtract)
-        seen = {t: keep.tile([P, S], F32, name=f"seen{t}") for t in LATE}
-        for t, h in ((2, 0), (3, 0), (3, 1)):
-            nc.scalar.activation(seen[t][:, halves[h]], current(t, h), COPY, scale=1.0 / DISCOUNT)
+        seen = {2: placed.tile([P, HALF], F32, name="seen2", offset=6 * ROW), 3: keep.tile([P, S], F32, name="seen3")}
+        nc.scalar.activation(seen[2][:], current(2, 0), COPY, scale=1.0 / DISCOUNT)
+        nc.scalar.activation(seen[3][:], y[3][:].indirect(cur_sb[:]), COPY, scale=1.0 / DISCOUNT)
         nc.gpsimd.tensor_tensor(debt[2, 0], seen[2][:, halves[0]], rw_sb[:, halves[0]], ALU.subtract)
         nc.gpsimd.tensor_tensor(y[2][:, S:], seen[3][:], rw_sb[:], ALU.subtract)
 

@@ -23,6 +23,7 @@ W1_SPLIT = 80
 W2_SPLIT = 64
 HALF = 256
 QUARTER = 128
+END_SPLIT = 80
 EARLY = (0, 1)
 LATE = (2, 3)
 ROW = 4 * S
@@ -31,6 +32,7 @@ SCALE_ROW0 = 16
 LAP = 64
 XS_AT = 4 * ROW - LAP
 W2R_AT = XS_AT + T - LAP
+W1_AT = 7 * ROW
 
 
 def tile_picked_redq_none_po_kernel(
@@ -60,7 +62,7 @@ def tile_picked_redq_none_po_kernel(
         nc.vector.memset(xs[:SCALE_ROW0, :].bitcast(I32), 0)
         nc.vector.memset(xs[32:64, :].bitcast(I32), 0)
         nc.vector.memset(xs[64:, :].bitcast(I32), 0)
-        w1_flat = keep.tile([P, PACK * N], F32, name="w1_flat")
+        w1_flat = placed.tile([P, PACK * N], F32, name="w1_flat", offset=W1_AT)
         w1_raw = w1_flat[:].rearrange("p (j c) -> p j c", j=PACK)
         w1_rows = w1.rearrange("(p j) c -> p j c", j=PACK)
         nc.sync.dma_start(w1_raw[:, :1], w1_rows[:, :1])
@@ -107,8 +109,9 @@ def tile_picked_redq_none_po_kernel(
         for b, cols in enumerate(blocks):
             nc.tensor.transpose(rw_acc[:, cols], rw_col[:, b : b + 1].to_broadcast([P, P]), ident[:])
         nc.scalar.copy(rw_sb[:], rw_acc[:])
-        rw_scaled = keep.tile([P, HALF], F32, name="rw_scaled")
-        nc.scalar.activation(rw_scaled[:], rw_acc[:, halves[1]], COPY, scale=discount[:])
+        debt_late = keep.tile([P, HALF + S], F32, name="debt_late")
+        rw_scaled = debt_late[:, QUARTER : QUARTER + HALF]
+        nc.scalar.activation(rw_scaled, rw_acc[:, halves[1]], COPY, scale=discount[:])
 
         xq_w = keep.tile([P, S], U32, name="xq_w", align_bytes=64)
 
@@ -158,16 +161,14 @@ def tile_picked_redq_none_po_kernel(
             work[:].rearrange("p (t s) -> p t s", t=PACK)[:, :2, halves[0]],
             work[:].rearrange("p (t s) -> p t s", t=PACK)[:, :2, halves[1]],
         ]
-        y = {0: w1_flat}
-        for t in (1, 2):
-            y[t] = keep.tile([P, 2 * S], F32, name=f"y{t}")
-            nc.gpsimd.memset(y[t][:, S:], 0.0)
+        y = {t: placed.tile([P, 2 * S], F32, name=f"y{t}", offset=W1_AT + 2 * t * ROW) for t in EARLY}
+        y[2] = keep.tile([P, S], F32, name="y2")
         y[3] = placed.tile([P, 2 * S], F32, name="y3", offset=4 * ROW)
         debt = {
-            (2, 0): rw_scaled[:],
+            (2, 0): debt_late[:, :HALF],
             (2, 1): work[:, 2 * S : 2 * S + HALF],
-            (3, 0): y[2][:, S : S + HALF],
-            (3, 1): y[2][:, S + HALF :],
+            (3, 0): debt_late[:, HALF:S],
+            (3, 1): debt_late[:, S:],
         }
 
         def current(t, h):
@@ -193,12 +194,12 @@ def tile_picked_redq_none_po_kernel(
         nc.scalar.activation(dealt_out(w2_bf, slice(W2_SPLIT, P)), dealt_in(w2_right[:]), COPY)
         w2_q = quantize_weight(w2_bf, "w2", [slice(0, P), slice(P, N)])
         nc.scalar.activation(y[3][:, :S], y_acc[3][:], COPY, scale=DISCOUNT)
-        nc.vector.tensor_tensor(debt[2, 1], current(2, 1), rw_scaled[:], ALU.subtract)
+        nc.vector.tensor_tensor(debt[2, 1], current(2, 1), rw_scaled, ALU.subtract)
         seen = {2: placed.tile([P, HALF], F32, name="seen2", offset=6 * ROW), 3: keep.tile([P, S], F32, name="seen3")}
         nc.scalar.activation(seen[2][:], current(2, 0), COPY, scale=1.0 / DISCOUNT)
         nc.scalar.activation(seen[3][:], y[3][:].indirect(cur_sb[:]), COPY, scale=1.0 / DISCOUNT)
         nc.gpsimd.tensor_tensor(debt[2, 0], seen[2][:, halves[0]], rw_sb[:, halves[0]], ALU.subtract)
-        nc.gpsimd.tensor_tensor(y[2][:, S:], seen[3][:], rw_sb[:], ALU.subtract)
+        nc.gpsimd.tensor_tensor(debt_late[:, HALF:], seen[3][:], rw_sb[:], ALU.subtract)
 
         low = {}
         for t, number in zip(range(PACK), (7, 0, 1, 2)):
@@ -272,7 +273,9 @@ def tile_picked_redq_none_po_kernel(
         nc.sync.dma_start(out_rows[:, 2:, halves[1]], td[1][:, 2:])
         quantize_result(stages[0])
         nc.sync.dma_start(out_words[:, halves[0]], o_codes[:, halves[0]])
-        round_result(last, nc.vector.tensor_copy)
+        cut = last.start + END_SPLIT
+        round_result(slice(last.start, cut), nc.vector.tensor_copy)
+        round_result(slice(cut, last.stop), nc.scalar.copy)
         quantize_result(stages[1])
         quantize_result(last)
         nc.sync.dma_start(out_words[:, halves[1]], o_codes[:, halves[1]])

@@ -23,15 +23,17 @@ W1_SPLIT = 80
 W2_SPLIT = 64
 HALF = 256
 QUARTER = 128
-END_SPLIT = 80
-EARLY = (0, 1)
-LATE = (2, 3)
+END_SPLIT = 96
+PLAIN = (0, 1)
+SCALED = (2, 3)
 ROW = 4 * S
 SCALE_ROWS = K // 32
 SCALE_ROW0 = 16
 LAP = 64
 XS_AT = 4 * ROW - LAP
-W2R_AT = XS_AT + T - LAP
+W2_RIGHT_AT = XS_AT + T - LAP
+Y_FOURTH_AT = 4 * ROW
+SEEN_THIRD_AT = 6 * ROW
 W1_AT = 7 * ROW
 
 
@@ -88,15 +90,15 @@ def tile_picked_redq_none_po_kernel(
             )
         w2_rows = w2.rearrange("(p j) c -> p j c", j=PACK)
         w2_cut = PACK * W2_SPLIT
-        w2_right = placed.tile([P, PACK, N - w2_cut], F32, name="w2_right", offset=W2R_AT)
-        left_words = PACK * w2_cut
+        w2_right = placed.tile([P, PACK, N - w2_cut], F32, name="w2_right", offset=W2_RIGHT_AT)
         work = placed.tile([P, 4 * S], F32, name="work", offset=0, align_bytes=64)
-        w2_left = work[:, 2 * S - left_words : 2 * S].rearrange("p (j c) -> p j c", j=PACK)
+        w2_left = work[:, : PACK * w2_cut].rearrange("p (j c) -> p j c", j=PACK)
         ident = keep.tile([P, P], F32, name="ident")
         make_identity(nc, ident[:])
         nc.sync.dma_start(w2_left, w2_rows[:, :, :w2_cut])
         nc.sync.dma_start(w2_right[:], w2_rows[:, :, w2_cut:])
 
+        whole = slice(0, S)
         halves = [slice(h * HALF, (h + 1) * HALF) for h in range(S // HALF)]
         blocks = [slice(b * P, (b + 1) * P) for b in range(S // P)]
         stages = (halves[0], slice(HALF, HALF + QUARTER), slice(HALF + QUARTER, S))
@@ -109,8 +111,8 @@ def tile_picked_redq_none_po_kernel(
         for b, cols in enumerate(blocks):
             nc.tensor.transpose(rw_acc[:, cols], rw_col[:, b : b + 1].to_broadcast([P, P]), ident[:])
         nc.scalar.copy(rw_sb[:], rw_acc[:])
-        debt_late = keep.tile([P, HALF + S], F32, name="debt_late")
-        rw_scaled = debt_late[:, QUARTER : QUARTER + HALF]
+        side_debt = keep.tile([P, HALF + S], F32, name="side_debt")
+        rw_scaled = side_debt[:, QUARTER : QUARTER + HALF]
         nc.scalar.activation(rw_scaled, rw_acc[:, halves[1]], COPY, scale=discount[:])
 
         xq_w = keep.tile([P, S], U32, name="xq_w", align_bytes=64)
@@ -152,74 +154,75 @@ def tile_picked_redq_none_po_kernel(
         nc.scalar.activation(dealt_out(w1_bf[:], slice(W1_SPLIT, P)), dealt_in(w1_raw)[:, W1_SPLIT:], COPY)
         w1_q = quantize_weight(w1_bf[:], "w1", [slice(0, N)])
 
-        for cols in stages:
+        pieces = (slice(0, QUARTER), slice(QUARTER, QUARTER + HALF), slice(QUARTER + HALF, S))
+        for cols in pieces:
             nc.vector.tensor_copy(xq_w[:, cols], xw[:].bitcast(U32).indirect(offs_sb[:, entries(cols)]))
         w2_bf = work[:, 2 * S :].bitcast(BF16)
         nc.vector.tensor_copy(dealt_out(w2_bf, slice(0, W2_SPLIT)), dealt_in(w2_left))
 
-        debt_pair = [
-            work[:].rearrange("p (t s) -> p t s", t=PACK)[:, :2, halves[0]],
-            work[:].rearrange("p (t s) -> p t s", t=PACK)[:, :2, halves[1]],
-        ]
-        y = {t: placed.tile([P, 2 * S], F32, name=f"y{t}", offset=W1_AT + 2 * t * ROW) for t in EARLY}
+        y = {t: placed.tile([P, 2 * S], F32, name=f"y{t}", offset=W1_AT + 2 * t * ROW) for t in PLAIN}
         y[2] = keep.tile([P, S], F32, name="y2")
-        y[3] = placed.tile([P, 2 * S], F32, name="y3", offset=4 * ROW)
-        debt = {
-            (2, 0): debt_late[:, :HALF],
-            (2, 1): work[:, 2 * S : 2 * S + HALF],
-            (3, 0): debt_late[:, HALF:S],
-            (3, 1): debt_late[:, S:],
-        }
+        y[3] = placed.tile([P, 2 * S], F32, name="y3", offset=Y_FOURTH_AT)
+        plain_debt = work[:, : 2 * S].rearrange("p (t s) -> p t s", t=2)
+        scaled_debt = work[:, 2 * S : 2 * S + HALF]
+        debt_third = side_debt[:, :HALF]
+        debt_fourth = side_debt[:, HALF:]
 
-        def current(t, h):
-            return y[t][:].indirect(cur_sb[:, entries(halves[h])])
+        def current(t, cols):
+            return y[t][:].indirect(cur_sb[:, entries(cols)])
 
-        for i, cols in enumerate(stages):
+        for i, cols in enumerate(pieces):
             piece = bank(f"y_first{i}", i, cols.stop - cols.start)
             product(piece[:], w1_q, 0, cols)
             nc.scalar.copy(y[0][:, cols], piece[:])
-            if cols == halves[0]:
-                piece = bank("y_second0", 3, HALF)
-                product(piece[:], w1_q, 1, cols)
-                nc.scalar.copy(y[1][:, cols], piece[:])
-        second_rest = bank("y_second1", 6, HALF)
-        product(second_rest[:], w1_q, 1, halves[1])
-        y_acc = {t: bank(f"y{t}", 2 + t) for t in LATE}
-        for t in LATE:
-            product(y_acc[t][:], w1_q, t, slice(0, S))
-        nc.vector.tensor_tensor(work[:, :S], y[0][:].indirect(cur_sb[:]), rw_sb[:], ALU.subtract)
-        nc.scalar.copy(y[1][:, halves[1]], second_rest[:])
-        nc.vector.tensor_tensor(work[:, S : 2 * S], y[1][:].indirect(cur_sb[:]), rw_sb[:], ALU.subtract)
-        nc.scalar.activation(y[2][:, :S], y_acc[2][:], COPY, scale=DISCOUNT)
+            if i == 0:
+                for t, number in ((1, 3), (2, 7)):
+                    piece = bank(f"y_early{t}", number, QUARTER)
+                    product(piece[:], w1_q, t, cols)
+                    nc.scalar.activation(y[t][:, cols], piece[:], COPY, scale=1.0 if t in PLAIN else DISCOUNT)
+        second_rest = bank("y_second1", 6)
+        for cols in pieces[1:]:
+            product(second_rest[:, cols], w1_q, 1, cols)
+        y_acc = {t: bank(f"y{t}", number) for t, number in zip(SCALED, (4, 5))}
+        for cols in pieces[1:]:
+            product(y_acc[2][:, cols], w1_q, 2, cols)
+        product(y_acc[3][:], w1_q, 3, whole)
+        nc.vector.tensor_tensor(plain_debt[:, 0, :], current(0, whole), rw_sb[:], ALU.subtract)
+        nc.scalar.copy(y[1][:, QUARTER:S], second_rest[:, QUARTER:])
+        nc.vector.tensor_tensor(plain_debt[:, 1, :], current(1, whole), rw_sb[:], ALU.subtract)
+        nc.scalar.activation(y[2][:, QUARTER:], y_acc[2][:, QUARTER:], COPY, scale=DISCOUNT)
+
         nc.scalar.activation(dealt_out(w2_bf, slice(W2_SPLIT, P)), dealt_in(w2_right[:]), COPY)
         w2_q = quantize_weight(w2_bf, "w2", [slice(0, P), slice(P, N)])
         nc.scalar.activation(y[3][:, :S], y_acc[3][:], COPY, scale=DISCOUNT)
-        nc.vector.tensor_tensor(debt[2, 1], current(2, 1), rw_scaled, ALU.subtract)
-        seen = {2: placed.tile([P, HALF], F32, name="seen2", offset=6 * ROW), 3: keep.tile([P, S], F32, name="seen3")}
-        nc.scalar.activation(seen[2][:], current(2, 0), COPY, scale=1.0 / DISCOUNT)
-        nc.scalar.activation(seen[3][:], y[3][:].indirect(cur_sb[:]), COPY, scale=1.0 / DISCOUNT)
-        nc.gpsimd.tensor_tensor(debt[2, 0], seen[2][:, halves[0]], rw_sb[:, halves[0]], ALU.subtract)
-        nc.gpsimd.tensor_tensor(debt_late[:, HALF:], seen[3][:], rw_sb[:], ALU.subtract)
+        nc.vector.tensor_tensor(scaled_debt, current(2, halves[1]), rw_scaled, ALU.subtract)
+
+        seen_third = placed.tile([P, HALF], F32, name="seen_third", offset=SEEN_THIRD_AT)
+        seen_fourth = keep.tile([P, S], F32, name="seen_fourth")
+        nc.scalar.activation(seen_third[:], current(2, halves[0]), COPY, scale=1.0 / DISCOUNT)
+        nc.scalar.activation(seen_fourth[:], current(3, whole), COPY, scale=1.0 / DISCOUNT)
+        nc.gpsimd.tensor_tensor(debt_third, seen_third[:], rw_sb[:, halves[0]], ALU.subtract)
+        nc.gpsimd.tensor_tensor(debt_fourth, seen_fourth[:], rw_sb[:], ALU.subtract)
 
         low = {}
-        for t, number in zip(range(PACK), (7, 0, 1, 2)):
+        for t, number in zip(range(PACK), range(PACK)):
             e_acc = bank(f"e{t}", number)
-            product(e_acc[:], w2_q, t, slice(0, S))
+            product(e_acc[:], w2_q, t, whole)
             low[t] = keep.tile([P, S], F32, name=f"low{t}")
-            if t in EARLY:
+            if t in PLAIN:
                 nc.vector.tensor_tensor(low[t][:], e_acc[:], y[t][:, :S], ALU.min)
             else:
                 nc.vector.scalar_tensor_tensor(low[t][:], e_acc[:], DISCOUNT, y[t][:, :S], ALU.mult, ALU.min)
 
-        shared = (EARLY, EARLY + LATE[:1])
-        ahead = [keep.tile([P, len(shared[h]), HALF], F32, name=f"ahead{h}") for h in range(2)]
+        on_scalar = ((0, 1), (0, 1, 2))
+        ahead = [keep.tile([P, len(planes), HALF], F32, name=f"ahead{h}") for h, planes in enumerate(on_scalar)]
         for h, cols in enumerate(halves):
-            for t in shared[h]:
+            for t in on_scalar[h]:
                 nc.scalar.activation(
                     ahead[h][:, t, :],
                     low[t][:].indirect(nx_sb[:, entries(cols)]),
                     COPY,
-                    scale=DISCOUNT if t in EARLY else 1.0,
+                    scale=DISCOUNT if t in PLAIN else 1.0,
                 )
 
         out_rows = out_0.rearrange("(p t) j -> p t j", t=PACK)
@@ -228,25 +231,22 @@ def tile_picked_redq_none_po_kernel(
         td = [keep.tile([P, PACK, HALF], F32, name=f"td{h}") for h in range(2)]
         td_bf = keep.tile([P, S, PACK], BF16, name="td_bf", align_bytes=64)
 
-        def within(cols):
-            return slice(cols.start % HALF, (cols.stop - 1) % HALF + 1)
+        def result(planes, cols):
+            h = cols.start // HALF
+            return td[h][:, planes, cols.start - h * HALF : cols.stop - h * HALF]
 
-        def join(h):
-            nc.vector.tensor_tensor(td[h][:, :2, :], ahead[h][:, :2], debt_pair[h], ALU.subtract)
+        def join_plain(h):
+            nc.vector.tensor_tensor(td[h][:, :2, :], ahead[h][:, :2], plain_debt[:, :, halves[h]], ALU.subtract)
 
-        def gather_late(cols):
-            for t in range(len(shared[cols.start // HALF]), PACK):
-                nc.vector.tensor_tensor(
-                    td[cols.start // HALF][:, t, within(cols)],
-                    low[t][:].indirect(nx_sb[:, entries(cols)]),
-                    debt[t, cols.start // HALF][:, within(cols)],
-                    ALU.subtract,
-                )
+        def gather_next(t, cols, debt):
+            nc.vector.tensor_tensor(
+                result(t, cols), low[t][:].indirect(nx_sb[:, entries(cols)]), debt[:, cols], ALU.subtract
+            )
 
         def round_result(cols, copy):
             copy(
                 td_bf[:, cols, :].rearrange("p (c i) t -> p c t i", i=4),
-                td[cols.start // HALF][:, :, within(cols)].rearrange("p t (c i) -> p c t i", i=4),
+                result(slice(0, PACK), cols).rearrange("p t (c i) -> p c t i", i=4),
             )
 
         o_codes = keep.tile([P, S], I32, name="o_codes", align_bytes=64)
@@ -258,18 +258,19 @@ def tile_picked_redq_none_po_kernel(
                 in_=td_bf[:, cols].rearrange("p j t -> p (j t)"),
             )
 
-        gather_late(halves[0])
+        gather_next(2, halves[0], debt_third)
+        gather_next(3, halves[0], debt_fourth)
         nc.sync.dma_start(out_rows[:, 2:, halves[0]], td[0][:, 2:])
-        join(0)
+        join_plain(0)
         nc.sync.dma_start(out_rows[:, :2, halves[0]], td[0][:, :2])
         round_result(halves[0], nc.scalar.copy)
-        join(1)
+        join_plain(1)
         nc.sync.dma_start(out_rows[:, :2, halves[1]], td[1][:, :2])
-        gather_late(stages[1])
-        nc.vector.scalar_tensor_tensor(td[1][:, 2, :], debt[2, 1], -1.0 / DISCOUNT, ahead[1][:, 2], ALU.mult, ALU.add)
+        gather_next(3, stages[1], debt_fourth)
+        nc.vector.scalar_tensor_tensor(td[1][:, 2, :], scaled_debt, -1.0 / DISCOUNT, ahead[1][:, 2], ALU.mult, ALU.add)
         round_result(stages[1], nc.scalar.copy)
         last = stages[2]
-        gather_late(last)
+        gather_next(3, last, debt_fourth)
         nc.sync.dma_start(out_rows[:, 2:, halves[1]], td[1][:, 2:])
         quantize_result(stages[0])
         nc.sync.dma_start(out_words[:, halves[0]], o_codes[:, halves[0]])

@@ -20,21 +20,21 @@ COPY = mybir.ActivationFunctionType.Copy
 
 DISCOUNT = 0.9
 W1_SPLIT = 80
-W2_SPLIT = 64
 HALF = 256
 QUARTER = 128
 END_SPLIT = 96
 PLAIN = (0, 1)
-SCALED = (2, 3)
 ROW = 4 * S
 SCALE_ROWS = K // 32
 SCALE_ROW0 = 16
 LAP = 64
-XS_AT = 4 * ROW - LAP
-W2_RIGHT_AT = XS_AT + T - LAP
-Y_FOURTH_AT = 4 * ROW
-SEEN_THIRD_AT = 6 * ROW
-W1_AT = 7 * ROW
+WORK_ROWS = 5
+XS_AT = WORK_ROWS * ROW - LAP
+W2_LAST_AT = XS_AT + T - LAP
+Y_FOURTH_AT = W2_LAST_AT - LAP
+SEEN_THIRD_AT = Y_FOURTH_AT + ROW
+W1_AT = 8 * ROW
+DEBT_AT = 768
 
 
 def tile_picked_redq_none_po_kernel(
@@ -49,12 +49,16 @@ def tile_picked_redq_none_po_kernel(
         def bank(name, number, width=S):
             return psum.tile([P, width], F32, name=name, offset=number * ROW)
 
+        whole = slice(0, S)
+        halves = [slice(h * HALF, (h + 1) * HALF) for h in range(S // HALF)]
+        blocks = [slice(b * P, (b + 1) * P) for b in range(S // P)]
+        stages = (halves[0], slice(HALF, HALF + QUARTER), slice(HALF + QUARTER, S))
+
         offs_sb = keep.tile([P, S // 16], U16, name="offs_sb")
         cur_sb = keep.tile([P, S // 16], U16, name="cur_sb")
         nx_sb = keep.tile([P, S // 16], U16, name="nx_sb")
         xw = keep.tile([P, T], I32, name="xw", align_bytes=64)
         xs = placed.tile([P, T], U8, name="xs", offset=XS_AT, align_bytes=64)
-        rw_sb = keep.tile([P, S], F32, name="rw_sb")
 
         one = keep.tile([P, 1], F32, name="one")
         nc.gpsimd.memset(one[:], 1.0)
@@ -77,7 +81,6 @@ def tile_picked_redq_none_po_kernel(
         nc.gpsimd.memset(rw_quarters[96 : P - PACK, :], 0.0)
         nc.sync.dma_start(cur_sb[:], cur)
         nc.sync.dma_start(xw[:], x_words[0].rearrange("p n t -> p (n t)").bitcast(I32))
-        nc.sync.dma_start(nx_sb[:], nx)
 
         xq_s = keep.tile([P, S], U8, name="xq_s", align_bytes=64)
         nc.gpsimd.memset(xq_s[:].bitcast(I32), 0)
@@ -89,19 +92,20 @@ def tile_picked_redq_none_po_kernel(
                 picked_s[SCALE_ROW0 + 4 * q : SCALE_ROW0 + 4 * q + 4, :].bitcast(I32),
             )
         w2_rows = w2.rearrange("(p j) c -> p j c", j=PACK)
-        w2_cut = PACK * W2_SPLIT
-        w2_right = placed.tile([P, PACK, N - w2_cut], F32, name="w2_right", offset=W2_RIGHT_AT)
-        work = placed.tile([P, 4 * S], F32, name="work", offset=0, align_bytes=64)
-        w2_left = work[:, : PACK * w2_cut].rearrange("p (j c) -> p j c", j=PACK)
+        work = placed.tile([P, WORK_ROWS * S], F32, name="work", offset=0, align_bytes=64)
+        w2_first = work[:, : PACK * HALF].rearrange("p (j c) -> p j c", j=PACK)
+        w2_second = work[:, PACK * HALF : PACK * (HALF + QUARTER)].rearrange("p (j c) -> p j c", j=PACK)
+        w2_last = placed.tile([P, PACK, QUARTER], F32, name="w2_last", offset=W2_LAST_AT)
         ident = keep.tile([P, P], F32, name="ident")
         make_identity(nc, ident[:])
-        nc.sync.dma_start(w2_left, w2_rows[:, :, :w2_cut])
-        nc.sync.dma_start(w2_right[:], w2_rows[:, :, w2_cut:])
+        nc.sync.dma_start(w2_first, w2_rows[:, :, stages[0]])
+        nc.sync.dma_start(w2_second, w2_rows[:, :, stages[1]])
+        nc.sync.dma_start(w2_last[:], w2_rows[:, :, stages[2]])
 
-        whole = slice(0, S)
-        halves = [slice(h * HALF, (h + 1) * HALF) for h in range(S // HALF)]
-        blocks = [slice(b * P, (b + 1) * P) for b in range(S // P)]
-        stages = (halves[0], slice(HALF, HALF + QUARTER), slice(HALF + QUARTER, S))
+        y = {t: placed.tile([P, 2 * S], F32, name=f"y{t}", offset=W1_AT + 2 * t * ROW) for t in PLAIN}
+        y[2] = keep.tile([P, 2 * S], F32, name="y2")
+        y[3] = placed.tile([P, S], F32, name="y3", offset=Y_FOURTH_AT)
+        rw_sb = y[2][:, S:]
 
         rw_turned = bank("rw_turned", 6, P)
         nc.tensor.transpose(rw_turned[:], rw_quarters[:], ident[:])
@@ -110,10 +114,7 @@ def tile_picked_redq_none_po_kernel(
         rw_acc = bank("rw_acc", 7)
         for b, cols in enumerate(blocks):
             nc.tensor.transpose(rw_acc[:, cols], rw_col[:, b : b + 1].to_broadcast([P, P]), ident[:])
-        nc.scalar.copy(rw_sb[:], rw_acc[:])
-        side_debt = keep.tile([P, HALF + S], F32, name="side_debt")
-        rw_scaled = side_debt[:, QUARTER : QUARTER + HALF]
-        nc.scalar.activation(rw_scaled, rw_acc[:, halves[1]], COPY, scale=discount[:])
+        nc.scalar.copy(rw_sb, rw_acc[:])
 
         xq_w = keep.tile([P, S], U32, name="xq_w", align_bytes=64)
 
@@ -123,16 +124,21 @@ def tile_picked_redq_none_po_kernel(
         def dealt_in(raw):
             return raw.rearrange("p j (m t) -> p m j t", t=PACK)
 
-        def quantize_weight(grouped, name, parts):
+        def groups_of(cols):
+            return slice(cols.start // PACK, cols.stop // PACK)
+
+        def quantized(name):
             codes = keep.tile([P, N], U32, name=f"{name}_codes", align_bytes=64)
             scales = keep.tile([P, N], U8, name=f"{name}_scales", align_bytes=64)
-            for cols in parts:
-                nc.vector.quantize_mx(
-                    out=codes[:, cols].bitcast(FP8X4),
-                    scales=scales[:, cols],
-                    in_=grouped[:, PACK * cols.start : PACK * cols.stop],
-                )
             return codes, scales
+
+        def quantize_weight(weight, grouped, cols):
+            codes, scales = weight
+            nc.vector.quantize_mx(
+                out=codes[:, cols].bitcast(FP8X4),
+                scales=scales[:, cols],
+                in_=grouped[:, PACK * cols.start : PACK * cols.stop],
+            )
 
         def product(acc, weight, t, cols):
             codes, scales = weight
@@ -152,21 +158,18 @@ def tile_picked_redq_none_po_kernel(
         w1_bf = keep.tile([P, PACK * N], BF16, name="w1_bf", align_bytes=64)
         nc.vector.tensor_copy(dealt_out(w1_bf[:], slice(0, W1_SPLIT)), dealt_in(w1_raw)[:, :W1_SPLIT])
         nc.scalar.activation(dealt_out(w1_bf[:], slice(W1_SPLIT, P)), dealt_in(w1_raw)[:, W1_SPLIT:], COPY)
-        w1_q = quantize_weight(w1_bf[:], "w1", [slice(0, N)])
+        w1_q = quantized("w1")
+        quantize_weight(w1_q, w1_bf[:], whole)
 
         pieces = (slice(0, QUARTER), slice(QUARTER, QUARTER + HALF), slice(QUARTER + HALF, S))
         for cols in pieces:
             nc.vector.tensor_copy(xq_w[:, cols], xw[:].bitcast(U32).indirect(offs_sb[:, entries(cols)]))
-        w2_bf = work[:, 2 * S :].bitcast(BF16)
-        nc.vector.tensor_copy(dealt_out(w2_bf, slice(0, W2_SPLIT)), dealt_in(w2_left))
+        w2_bf = work[:, 3 * S :].bitcast(BF16)
+        nc.vector.tensor_copy(dealt_out(w2_bf, groups_of(stages[0])), dealt_in(w2_first))
+        nc.vector.tensor_copy(dealt_out(w2_bf, groups_of(stages[1])), dealt_in(w2_second))
 
-        y = {t: placed.tile([P, 2 * S], F32, name=f"y{t}", offset=W1_AT + 2 * t * ROW) for t in PLAIN}
-        y[2] = keep.tile([P, S], F32, name="y2")
-        y[3] = placed.tile([P, 2 * S], F32, name="y3", offset=Y_FOURTH_AT)
-        plain_debt = work[:, : 2 * S].rearrange("p (t s) -> p t s", t=2)
-        scaled_debt = work[:, 2 * S : 2 * S + HALF]
-        debt_third = side_debt[:, :HALF]
-        debt_fourth = side_debt[:, HALF:]
+        plain_debt = work[:, DEBT_AT : DEBT_AT + 2 * S].rearrange("p (t s) -> p t s", t=2)
+        debt_third = y[1][:, S:]
 
         def current(t, cols):
             return y[t][:].indirect(cur_sb[:, entries(cols)])
@@ -176,43 +179,54 @@ def tile_picked_redq_none_po_kernel(
             product(piece[:], w1_q, 0, cols)
             nc.scalar.copy(y[0][:, cols], piece[:])
             if i == 0:
-                for t, number in ((1, 3), (2, 7)):
-                    piece = bank(f"y_early{t}", number, QUARTER)
-                    product(piece[:], w1_q, t, cols)
-                    nc.scalar.activation(y[t][:, cols], piece[:], COPY, scale=1.0 if t in PLAIN else DISCOUNT)
-        second_rest = bank("y_second1", 6)
+                early_second = bank("y_early1", 3, QUARTER)
+                product(early_second[:], w1_q, 1, cols)
+                nc.scalar.copy(y[1][:, cols], early_second[:])
+                early_third = bank("y_early2", 4, QUARTER)
+                product(early_third[:], w1_q, 2, cols)
+                nc.scalar.activation(y[2][:, cols], early_third[:], COPY, scale=discount[:])
+        second_rest = bank("y_second", 6)
         for cols in pieces[1:]:
             product(second_rest[:, cols], w1_q, 1, cols)
-        y_acc = {t: bank(f"y{t}", number) for t, number in zip(SCALED, (4, 5))}
+        third_rest = bank("y_third", 5)
         for cols in pieces[1:]:
-            product(y_acc[2][:, cols], w1_q, 2, cols)
-        product(y_acc[3][:], w1_q, 3, whole)
-        nc.vector.tensor_tensor(plain_debt[:, 0, :], current(0, whole), rw_sb[:], ALU.subtract)
+            product(third_rest[:, cols], w1_q, 2, cols)
+        fourth = bank("y_fourth", 0)
+        product(fourth[:], w1_q, 3, whole)
+        nc.vector.tensor_tensor(plain_debt[:, 0, :], current(0, whole), rw_sb, ALU.subtract)
         nc.scalar.copy(y[1][:, QUARTER:S], second_rest[:, QUARTER:])
-        nc.vector.tensor_tensor(plain_debt[:, 1, :], current(1, whole), rw_sb[:], ALU.subtract)
-        nc.scalar.activation(y[2][:, QUARTER:], y_acc[2][:, QUARTER:], COPY, scale=DISCOUNT)
+        nc.vector.tensor_tensor(plain_debt[:, 1, halves[0]], current(1, halves[0]), rw_sb[:, halves[0]], ALU.subtract)
+        nc.scalar.activation(y[2][:, QUARTER:S], third_rest[:, QUARTER:], COPY, scale=DISCOUNT)
 
-        nc.scalar.activation(dealt_out(w2_bf, slice(W2_SPLIT, P)), dealt_in(w2_right[:]), COPY)
-        w2_q = quantize_weight(w2_bf, "w2", [slice(0, P), slice(P, N)])
-        nc.scalar.activation(y[3][:, :S], y_acc[3][:], COPY, scale=DISCOUNT)
-        nc.vector.tensor_tensor(scaled_debt, current(2, halves[1]), rw_scaled, ALU.subtract)
+        nc.scalar.activation(dealt_out(w2_bf, groups_of(stages[2])), dealt_in(w2_last[:]), COPY)
+        w2_q = quantized("w2")
+        quantize_weight(w2_q, w2_bf, slice(0, P))
+        quantize_weight(w2_q, w2_bf, slice(P, N))
+        nc.scalar.activation(y[3][:], fourth[:], COPY, scale=DISCOUNT)
+        nc.vector.tensor_tensor(plain_debt[:, 1, halves[1]], current(1, halves[1]), rw_sb[:, halves[1]], ALU.subtract)
+        nc.sync.dma_start(nx_sb[:], nx)
 
-        seen_third = placed.tile([P, HALF], F32, name="seen_third", offset=SEEN_THIRD_AT)
+        seen_third = placed.tile([P, S], F32, name="seen_third", offset=SEEN_THIRD_AT)
         seen_fourth = keep.tile([P, S], F32, name="seen_fourth")
-        nc.scalar.activation(seen_third[:], current(2, halves[0]), COPY, scale=1.0 / DISCOUNT)
-        nc.scalar.activation(seen_fourth[:], current(3, whole), COPY, scale=1.0 / DISCOUNT)
-        nc.gpsimd.tensor_tensor(debt_third, seen_third[:], rw_sb[:, halves[0]], ALU.subtract)
-        nc.gpsimd.tensor_tensor(debt_fourth, seen_fourth[:], rw_sb[:], ALU.subtract)
+        nc.scalar.activation(seen_third[:], current(2, whole), COPY, scale=1.0 / DISCOUNT)
+        for cols in halves:
+            nc.scalar.activation(seen_fourth[:, cols], current(3, cols), COPY, scale=1.0 / DISCOUNT)
+        debt_fourth = seen_third
+        nc.gpsimd.tensor_tensor(debt_third, seen_third[:], rw_sb, ALU.subtract)
+        nc.gpsimd.tensor_tensor(debt_fourth[:, halves[0]], seen_fourth[:, halves[0]], rw_sb[:, halves[0]], ALU.subtract)
 
         low = {}
-        for t, number in zip(range(PACK), range(PACK)):
-            e_acc = bank(f"e{t}", number)
+        for t in range(PACK):
+            e_acc = bank(f"e{t}", t + 1)
             product(e_acc[:], w2_q, t, whole)
             low[t] = keep.tile([P, S], F32, name=f"low{t}")
             if t in PLAIN:
                 nc.vector.tensor_tensor(low[t][:], e_acc[:], y[t][:, :S], ALU.min)
             else:
                 nc.vector.scalar_tensor_tensor(low[t][:], e_acc[:], DISCOUNT, y[t][:, :S], ALU.mult, ALU.min)
+        nc.vector.tensor_tensor(
+            debt_fourth[:, halves[1]], seen_fourth[:, halves[1]], rw_acc[:, halves[1]], ALU.subtract
+        )
 
         on_scalar = ((0, 1), (0, 1, 2))
         ahead = [keep.tile([P, len(planes), HALF], F32, name=f"ahead{h}") for h, planes in enumerate(on_scalar)]
@@ -260,14 +274,13 @@ def tile_picked_redq_none_po_kernel(
 
         gather_next(2, halves[0], debt_third)
         gather_next(3, halves[0], debt_fourth)
-        nc.sync.dma_start(out_rows[:, 2:, halves[0]], td[0][:, 2:])
         join_plain(0)
-        nc.sync.dma_start(out_rows[:, :2, halves[0]], td[0][:, :2])
+        nc.sync.dma_start(out_rows[:, :, halves[0]], td[0][:])
         round_result(halves[0], nc.scalar.copy)
         join_plain(1)
         nc.sync.dma_start(out_rows[:, :2, halves[1]], td[1][:, :2])
         gather_next(3, stages[1], debt_fourth)
-        nc.vector.scalar_tensor_tensor(td[1][:, 2, :], scaled_debt, -1.0 / DISCOUNT, ahead[1][:, 2], ALU.mult, ALU.add)
+        nc.vector.tensor_tensor(td[1][:, 2, :], ahead[1][:, 2], debt_third[:, halves[1]], ALU.subtract)
         round_result(stages[1], nc.scalar.copy)
         last = stages[2]
         gather_next(3, last, debt_fourth)

@@ -33,8 +33,9 @@ XS_AT = WORK_ROWS * ROW - LAP
 W2_LAST_AT = XS_AT + T - LAP
 Y_FOURTH_AT = W2_LAST_AT - LAP
 SEEN_THIRD_AT = Y_FOURTH_AT + ROW
-W1_AT = 8 * ROW
-DEBT_AT = 768
+W1_AT = 10 * ROW
+DEBT_AT = 512
+DEBT_STEP = 768
 
 
 def tile_picked_redq_none_po_kernel(
@@ -71,10 +72,9 @@ def tile_picked_redq_none_po_kernel(
         w1_flat = placed.tile([P, PACK * N], F32, name="w1_flat", offset=W1_AT)
         w1_raw = w1_flat[:].rearrange("p (j c) -> p j c", j=PACK)
         w1_rows = w1.rearrange("(p j) c -> p j c", j=PACK)
-        nc.sync.dma_start(w1_raw[:, :1], w1_rows[:, :1])
         nc.sync.dma_start(offs_sb[:], offs)
-        nc.sync.dma_start(xs[SCALE_ROW0 : SCALE_ROW0 + SCALE_ROWS, :].bitcast(I32), x_scales[0].bitcast(I32))
-        nc.sync.dma_start(w1_raw[:, 1:], w1_rows[:, 1:])
+        nc.scalar.dma_start(xs[SCALE_ROW0 : SCALE_ROW0 + SCALE_ROWS, :].bitcast(I32), x_scales[0].bitcast(I32))
+        nc.sync.dma_start(w1_raw, w1_rows)
         rw_quarters = keep.tile([P, P], F32, name="rw_quarters")
         nc.scalar.dma_start(rw_quarters[P - PACK :, :], rw[0].rearrange("(b c) -> b c", b=PACK))
         nc.gpsimd.memset(rw_quarters[:96, :], 0.0)
@@ -168,7 +168,7 @@ def tile_picked_redq_none_po_kernel(
         nc.vector.tensor_copy(dealt_out(w2_bf, groups_of(stages[0])), dealt_in(w2_first))
         nc.vector.tensor_copy(dealt_out(w2_bf, groups_of(stages[1])), dealt_in(w2_second))
 
-        plain_debt = work[:, DEBT_AT : DEBT_AT + 2 * S].rearrange("p (t s) -> p t s", t=2)
+        plain_debt = work[:, DEBT_AT : DEBT_AT + 2 * DEBT_STEP].rearrange("p (t s) -> p t s", t=2)[:, :, :S]
         debt_third = y[1][:, S:]
 
         def current(t, cols):
@@ -206,13 +206,14 @@ def tile_picked_redq_none_po_kernel(
         nc.vector.tensor_tensor(plain_debt[:, 1, halves[1]], current(1, halves[1]), rw_sb[:, halves[1]], ALU.subtract)
         nc.sync.dma_start(nx_sb[:], nx)
 
-        seen_third = placed.tile([P, S], F32, name="seen_third", offset=SEEN_THIRD_AT)
+        tail = placed.tile([P, 3 * HALF + S], F32, name="tail", offset=SEEN_THIRD_AT)
+        seen_third = tail[:, 3 * HALF :]
         seen_fourth = keep.tile([P, S], F32, name="seen_fourth")
-        nc.scalar.activation(seen_third[:], current(2, whole), COPY, scale=1.0 / DISCOUNT)
+        nc.scalar.activation(seen_third, current(2, whole), COPY, scale=1.0 / DISCOUNT)
         for cols in halves:
             nc.scalar.activation(seen_fourth[:, cols], current(3, cols), COPY, scale=1.0 / DISCOUNT)
         debt_fourth = seen_third
-        nc.gpsimd.tensor_tensor(debt_third, seen_third[:], rw_sb, ALU.subtract)
+        nc.gpsimd.tensor_tensor(debt_third, seen_third, rw_sb, ALU.subtract)
         nc.gpsimd.tensor_tensor(debt_fourth[:, halves[0]], seen_fourth[:, halves[0]], rw_sb[:, halves[0]], ALU.subtract)
 
         low = {}
@@ -229,11 +230,13 @@ def tile_picked_redq_none_po_kernel(
         )
 
         on_scalar = ((0, 1), (0, 1, 2))
-        ahead = [keep.tile([P, len(planes), HALF], F32, name=f"ahead{h}") for h, planes in enumerate(on_scalar)]
+        ahead_first = keep.tile([P, 2, HALF], F32, name="ahead_first")
+        ahead = [ahead_first[:], y[1][:, :S].rearrange("p (t c) -> p t c", t=2)]
+        ahead_third = keep.tile([P, HALF], F32, name="ahead_third")
         for h, cols in enumerate(halves):
             for t in on_scalar[h]:
                 nc.scalar.activation(
-                    ahead[h][:, t, :],
+                    ahead[h][:, t, :] if t in PLAIN else ahead_third[:],
                     low[t][:].indirect(nx_sb[:, entries(cols)]),
                     COPY,
                     scale=DISCOUNT if t in PLAIN else 1.0,
@@ -242,7 +245,8 @@ def tile_picked_redq_none_po_kernel(
         out_rows = out_0.rearrange("(p t) j -> p t j", t=PACK)
         out_words = out_1[0].rearrange("p n t -> p (n t)").bitcast(I32)
         o_scales = keep.tile([P, S], U8, name="o_scales", align_bytes=64)
-        td = [keep.tile([P, PACK, HALF], F32, name=f"td{h}") for h in range(2)]
+        td_first = keep.tile([P, PACK, HALF], F32, name="td_first")
+        td = [td_first[:], tail[:, : PACK * HALF].rearrange("p (t c) -> p t c", t=PACK)]
         td_bf = keep.tile([P, S, PACK], BF16, name="td_bf", align_bytes=64)
 
         def result(planes, cols):
@@ -250,7 +254,7 @@ def tile_picked_redq_none_po_kernel(
             return td[h][:, planes, cols.start - h * HALF : cols.stop - h * HALF]
 
         def join_plain(h):
-            nc.vector.tensor_tensor(td[h][:, :2, :], ahead[h][:, :2], plain_debt[:, :, halves[h]], ALU.subtract)
+            nc.vector.tensor_tensor(td[h][:, :2, :], ahead[h], plain_debt[:, :, halves[h]], ALU.subtract)
 
         def gather_next(t, cols, debt):
             nc.vector.tensor_tensor(
@@ -273,18 +277,19 @@ def tile_picked_redq_none_po_kernel(
             )
 
         gather_next(2, halves[0], debt_third)
-        gather_next(3, halves[0], debt_fourth)
         join_plain(0)
-        nc.sync.dma_start(out_rows[:, :, halves[0]], td[0][:])
+        nc.sync.dma_start(out_rows[:, :3, halves[0]], td[0][:, :3])
+        gather_next(3, halves[0], debt_fourth)
+        nc.sync.dma_start(out_rows[:, 3:, halves[0]], td[0][:, 3:])
         round_result(halves[0], nc.scalar.copy)
         join_plain(1)
-        nc.sync.dma_start(out_rows[:, :2, halves[1]], td[1][:, :2])
+        nc.vector.tensor_tensor(td[1][:, 2, :], ahead_third[:], debt_third[:, halves[1]], ALU.subtract)
+        nc.sync.dma_start(out_rows[:, :3, halves[1]], td[1][:, :3])
         gather_next(3, stages[1], debt_fourth)
-        nc.vector.tensor_tensor(td[1][:, 2, :], ahead[1][:, 2], debt_third[:, halves[1]], ALU.subtract)
         round_result(stages[1], nc.scalar.copy)
         last = stages[2]
         gather_next(3, last, debt_fourth)
-        nc.sync.dma_start(out_rows[:, 2:, halves[1]], td[1][:, 2:])
+        nc.sync.dma_start(out_rows[:, 3:, halves[1]], td[1][:, 3:])
         quantize_result(stages[0])
         nc.sync.dma_start(out_words[:, halves[0]], o_codes[:, halves[0]])
         cut = last.start + END_SPLIT

from contextlib import ExitStack

import concourse.mybir as mybir
from concourse.masks import make_identity

K, T, S, N = 512, 2048, 512, 512
P = 128
PACK = 4
FLOPS = 2 * 2 * K * N * S

F32 = mybir.dt.float32
BF16 = mybir.dt.bfloat16
I32 = mybir.dt.int32
U32 = mybir.dt.uint32
U16 = mybir.dt.uint16
U8 = mybir.dt.uint8
FP8X4 = mybir.dt.float8_e4m3fn_x4
ALU = mybir.AluOpType
COPY = mybir.ActivationFunctionType.Copy

DISCOUNT = 0.9
W1_SPLIT = 80
HALF = 256
QUARTER = 128
END_SPLIT = 96
PLAIN = (0, 1)
ROW = 4 * S
SCALE_ROWS = K // 32
SCALE_ROW0 = 16
LAP = 64
WORK_ROWS = 5
XS_AT = WORK_ROWS * ROW - LAP
W2_LAST_AT = XS_AT + T - LAP
Y_FOURTH_AT = W2_LAST_AT - LAP
SEEN_THIRD_AT = Y_FOURTH_AT + ROW
W1_AT = 10 * ROW
DEBT_AT = 512
DEBT_STEP = 768


def tile_picked_redq_none_po_kernel(
    tc, x_words, x_scales, w1, w2, rw, offs, nx, cur, out_0, out_1, out_2
):
    nc = tc.nc
    with ExitStack() as ctx:
        keep = ctx.enter_context(tc.tile_pool(name="keep", bufs=1))
        placed = ctx.enter_context(tc.tile_pool(name="placed", bufs=1))
        psum = ctx.enter_context(tc.psum_pool(name="psum", bufs=1))

        def bank(name, number, width=S):
            return psum.tile([P, width], F32, name=name, offset=number * ROW)

        whole = slice(0, S)
        halves = [slice(h * HALF, (h + 1) * HALF) for h in range(S // HALF)]
        blocks = [slice(b * P, (b + 1) * P) for b in range(S // P)]
        stages = (halves[0], slice(HALF, HALF + QUARTER), slice(HALF + QUARTER, S))

        offs_sb = keep.tile([P, S // 16], U16, name="offs_sb")
        cur_sb = keep.tile([P, S // 16], U16, name="cur_sb")
        nx_sb = keep.tile([P, S // 16], U16, name="nx_sb")
        xw = keep.tile([P, T], I32, name="xw", align_bytes=64)
        xs = placed.tile([P, T], U8, name="xs", offset=XS_AT, align_bytes=64)

        one = keep.tile([P, 1], F32, name="one")
        nc.gpsimd.memset(one[:], 1.0)
        discount = keep.tile([P, 1], F32, name="discount")
        nc.scalar.activation(discount[:], one[:], COPY, scale=DISCOUNT)

        nc.vector.memset(xs[:SCALE_ROW0, :].bitcast(I32), 0)
        nc.vector.memset(xs[32:64, :].bitcast(I32), 0)
        nc.vector.memset(xs[64:, :].bitcast(I32), 0)
        w1_flat = placed.tile([P, PACK * N], F32, name="w1_flat", offset=W1_AT)
        w1_raw = w1_flat[:].rearrange("p (j c) -> p j c", j=PACK)
        w1_rows = w1.rearrange("(p j) c -> p j c", j=PACK)
        nc.sync.dma_start(offs_sb[:], offs)
        nc.scalar.dma_start(xs[SCALE_ROW0 : SCALE_ROW0 + SCALE_ROWS, :].bitcast(I32), x_scales[0].bitcast(I32))
        nc.sync.dma_start(w1_raw, w1_rows)
        rw_quarters = keep.tile([P, P], F32, name="rw_quarters")
        nc.scalar.dma_start(rw_quarters[P - PACK :, :], rw[0].rearrange("(b c) -> b c", b=PACK))
        nc.gpsimd.memset(rw_quarters[:96, :], 0.0)
        nc.gpsimd.memset(rw_quarters[96 : P - PACK, :], 0.0)
        nc.sync.dma_start(cur_sb[:], cur)
        nc.sync.dma_start(xw[:], x_words[0].rearrange("p n t -> p (n t)").bitcast(I32))

        xq_s = keep.tile([P, S], U8, name="xq_s", align_bytes=64)
        nc.gpsimd.memset(xq_s[:].bitcast(I32), 0)
        picked_s = keep.tile([P, S], U8, name="picked_s", align_bytes=64)
        nc.vector.tensor_copy(picked_s[:], xs[:].indirect(offs_sb[:]))
        for q in range(4):
            nc.sync.dma_start(
                xq_s[32 * q : 32 * q + 4, :].bitcast(I32),
                picked_s[SCALE_ROW0 + 4 * q : SCALE_ROW0 + 4 * q + 4, :].bitcast(I32),
            )
        w2_rows = w2.rearrange("(p j) c -> p j c", j=PACK)
        work = placed.tile([P, WORK_ROWS * S], F32, name="work", offset=0, align_bytes=64)
        w2_first = work[:, : PACK * HALF].rearrange("p (j c) -> p j c", j=PACK)
        w2_second = work[:, PACK * HALF : PACK * (HALF + QUARTER)].rearrange("p (j c) -> p j c", j=PACK)
        w2_last = placed.tile([P, PACK, QUARTER], F32, name="w2_last", offset=W2_LAST_AT)
        ident = keep.tile([P, P], F32, name="ident")
        make_identity(nc, ident[:])
        nc.sync.dma_start(w2_first, w2_rows[:, :, stages[0]])
        nc.sync.dma_start(w2_second, w2_rows[:, :, stages[1]])
        nc.sync.dma_start(w2_last[:], w2_rows[:, :, stages[2]])

        y = {t: placed.tile([P, 2 * S], F32, name=f"y{t}", offset=W1_AT + 2 * t * ROW) for t in PLAIN}
        y[2] = keep.tile([P, 2 * S], F32, name="y2")
        y[3] = placed.tile([P, S], F32, name="y3", offset=Y_FOURTH_AT)
        rw_sb = y[2][:, S:]

        rw_turned = bank("rw_turned", 6, P)
        nc.tensor.transpose(rw_turned[:], rw_quarters[:], ident[:])
        rw_col = keep.tile([P, PACK], F32, name="rw_col")
        nc.scalar.copy(rw_col[:], rw_turned[:, P - PACK :])
        rw_acc = bank("rw_acc", 7)
        for b, cols in enumerate(blocks):
            nc.tensor.transpose(rw_acc[:, cols], rw_col[:, b : b + 1].to_broadcast([P, P]), ident[:])
        nc.scalar.copy(rw_sb, rw_acc[:])

        xq_w = keep.tile([P, S], U32, name="xq_w", align_bytes=64)

        def dealt_out(grouped, groups):
            return grouped.rearrange("p (t m j) -> p m j t", t=PACK, j=PACK)[:, groups]

        def dealt_in(raw):
            return raw.rearrange("p j (m t) -> p m j t", t=PACK)

        def groups_of(cols):
            return slice(cols.start // PACK, cols.stop // PACK)

        def quantized(name):
            codes = keep.tile([P, N], U32, name=f"{name}_codes", align_bytes=64)
            scales = keep.tile([P, N], U8, name=f"{name}_scales", align_bytes=64)
            return codes, scales

        def quantize_weight(weight, grouped, cols):
            codes, scales = weight
            nc.vector.quantize_mx(
                out=codes[:, cols].bitcast(FP8X4),
                scales=scales[:, cols],
                in_=grouped[:, PACK * cols.start : PACK * cols.stop],
            )

        def product(acc, weight, t, cols):
            codes, scales = weight
            nc.tensor.matmul_mx(
                out=acc,
                lhsT=codes[:, blocks[t]].bitcast(FP8X4),
                lhsT_scale=scales[:, blocks[t]],
                rhs=xq_w[:, cols].bitcast(FP8X4),
                rhs_scale=xq_s[:, cols],
                start=True,
                stop=True,
            )

        def entries(cols):
            return slice(cols.start // 16, cols.stop // 16)

        w1_bf = keep.tile([P, PACK * N], BF16, name="w1_bf", align_bytes=64)
        nc.vector.tensor_copy(dealt_out(w1_bf[:], slice(0, W1_SPLIT)), dealt_in(w1_raw)[:, :W1_SPLIT])
        nc.scalar.activation(dealt_out(w1_bf[:], slice(W1_SPLIT, P)), dealt_in(w1_raw)[:, W1_SPLIT:], COPY)
        w1_q = quantized("w1")
        quantize_weight(w1_q, w1_bf[:], whole)

        pieces = (slice(0, QUARTER), slice(QUARTER, QUARTER + HALF), slice(QUARTER + HALF, S))
        for cols in pieces:
            nc.vector.tensor_copy(xq_w[:, cols], xw[:].bitcast(U32).indirect(offs_sb[:, entries(cols)]))
        w2_bf = work[:, 3 * S :].bitcast(BF16)
        nc.vector.tensor_copy(dealt_out(w2_bf, groups_of(stages[0])), dealt_in(w2_first))
        nc.vector.tensor_copy(dealt_out(w2_bf, groups_of(stages[1])), dealt_in(w2_second))

        plain_debt = work[:, DEBT_AT : DEBT_AT + 2 * DEBT_STEP].rearrange("p (t s) -> p t s", t=2)[:, :, :S]
        debt_third = y[1][:, S:]

        def current(t, cols):
            return y[t][:].indirect(cur_sb[:, entries(cols)])

        for i, cols in enumerate(pieces):
            piece = bank(f"y_first{i}", i, cols.stop - cols.start)
            product(piece[:], w1_q, 0, cols)
            nc.scalar.copy(y[0][:, cols], piece[:])
            if i == 0:
                early_second = bank("y_early1", 3, QUARTER)
                product(early_second[:], w1_q, 1, cols)
                nc.scalar.copy(y[1][:, cols], early_second[:])
                early_third = bank("y_early2", 4, QUARTER)
                product(early_third[:], w1_q, 2, cols)
                nc.scalar.activation(y[2][:, cols], early_third[:], COPY, scale=discount[:])
        second_rest = bank("y_second", 6)
        for cols in pieces[1:]:
            product(second_rest[:, cols], w1_q, 1, cols)
        third_rest = bank("y_third", 5)
        for cols in pieces[1:]:
            product(third_rest[:, cols], w1_q, 2, cols)
        fourth = bank("y_fourth", 0)
        product(fourth[:], w1_q, 3, whole)
        nc.vector.tensor_tensor(plain_debt[:, 0, :], current(0, whole), rw_sb, ALU.subtract)
        nc.scalar.copy(y[1][:, QUARTER:S], second_rest[:, QUARTER:])
        nc.vector.tensor_tensor(plain_debt[:, 1, halves[0]], current(1, halves[0]), rw_sb[:, halves[0]], ALU.subtract)
        nc.scalar.activation(y[2][:, QUARTER:S], third_rest[:, QUARTER:], COPY, scale=DISCOUNT)

        nc.scalar.activation(dealt_out(w2_bf, groups_of(stages[2])), dealt_in(w2_last[:]), COPY)
        w2_q = quantized("w2")
        quantize_weight(w2_q, w2_bf, slice(0, P))
        quantize_weight(w2_q, w2_bf, slice(P, N))
        nc.scalar.activation(y[3][:], fourth[:], COPY, scale=DISCOUNT)
        nc.vector.tensor_tensor(plain_debt[:, 1, halves[1]], current(1, halves[1]), rw_sb[:, halves[1]], ALU.subtract)
        nc.sync.dma_start(nx_sb[:], nx)

        tail = placed.tile([P, 3 * HALF + S], F32, name="tail", offset=SEEN_THIRD_AT)
        seen_third = tail[:, 3 * HALF :]
        seen_fourth = keep.tile([P, S], F32, name="seen_fourth")
        nc.scalar.activation(seen_third, current(2, whole), COPY, scale=1.0 / DISCOUNT)
        for cols in halves:
            nc.scalar.activation(seen_fourth[:, cols], current(3, cols), COPY, scale=1.0 / DISCOUNT)
        debt_fourth = seen_third
        nc.gpsimd.tensor_tensor(debt_third, seen_third, rw_sb, ALU.subtract)
        nc.gpsimd.tensor_tensor(debt_fourth[:, halves[0]], seen_fourth[:, halves[0]], rw_sb[:, halves[0]], ALU.subtract)

        low = {}
        for t in range(PACK):
            e_acc = bank(f"e{t}", t + 1)
            product(e_acc[:], w2_q, t, whole)
            low[t] = keep.tile([P, S], F32, name=f"low{t}")
            if t in PLAIN:
                nc.vector.tensor_tensor(low[t][:], e_acc[:], y[t][:, :S], ALU.min)
            else:
                nc.vector.scalar_tensor_tensor(low[t][:], e_acc[:], DISCOUNT, y[t][:, :S], ALU.mult, ALU.min)
        nc.vector.tensor_tensor(
            debt_fourth[:, halves[1]], seen_fourth[:, halves[1]], rw_acc[:, halves[1]], ALU.subtract
        )

        on_scalar = ((0, 1), (0, 1, 2))
        ahead_first = keep.tile([P, 2, HALF], F32, name="ahead_first")
        ahead = [ahead_first[:], y[1][:, :S].rearrange("p (t c) -> p t c", t=2)]
        ahead_third = keep.tile([P, HALF], F32, name="ahead_third")
        for h, cols in enumerate(halves):
            for t in on_scalar[h]:
                nc.scalar.activation(
                    ahead[h][:, t, :] if t in PLAIN else ahead_third[:],
                    low[t][:].indirect(nx_sb[:, entries(cols)]),
                    COPY,
                    scale=DISCOUNT if t in PLAIN else 1.0,
                )

        out_rows = out_0.rearrange("(p t) j -> p t j", t=PACK)
        out_words = out_1[0].rearrange("p n t -> p (n t)").bitcast(I32)
        o_scales = keep.tile([P, S], U8, name="o_scales", align_bytes=64)
        td_first = keep.tile([P, PACK, HALF], F32, name="td_first")
        td = [td_first[:], tail[:, : PACK * HALF].rearrange("p (t c) -> p t c", t=PACK)]
        td_bf = keep.tile([P, S, PACK], BF16, name="td_bf", align_bytes=64)

        def result(planes, cols):
            h = cols.start // HALF
            return td[h][:, planes, cols.start - h * HALF : cols.stop - h * HALF]

        def join_plain(h):
            nc.vector.tensor_tensor(td[h][:, :2, :], ahead[h], plain_debt[:, :, halves[h]], ALU.subtract)

        def gather_next(t, cols, debt):
            nc.vector.tensor_tensor(
                result(t, cols), low[t][:].indirect(nx_sb[:, entries(cols)]), debt[:, cols], ALU.subtract
            )

        def round_result(cols, copy):
            copy(
                td_bf[:, cols, :].rearrange("p (c i) t -> p c t i", i=4),
                result(slice(0, PACK), cols).rearrange("p t (c i) -> p c t i", i=4),
            )

        o_codes = keep.tile([P, S], I32, name="o_codes", align_bytes=64)

        def quantize_result(cols):
            nc.vector.quantize_mx(
                out=o_codes[:, cols].bitcast(FP8X4),
                scales=o_scales[:, cols],
                in_=td_bf[:, cols].rearrange("p j t -> p (j t)"),
            )

        gather_next(2, halves[0], debt_third)
        join_plain(0)
        nc.sync.dma_start(out_rows[:, :3, halves[0]], td[0][:, :3])
        gather_next(3, halves[0], debt_fourth)
        nc.sync.dma_start(out_rows[:, 3:, halves[0]], td[0][:, 3:])
        round_result(halves[0], nc.scalar.copy)
        join_plain(1)
        nc.vector.tensor_tensor(td[1][:, 2, :], ahead_third[:], debt_third[:, halves[1]], ALU.subtract)
        nc.sync.dma_start(out_rows[:, :3, halves[1]], td[1][:, :3])
        gather_next(3, stages[1], debt_fourth)
        round_result(stages[1], nc.scalar.copy)
        last = stages[2]
        gather_next(3, last, debt_fourth)
        nc.sync.dma_start(out_rows[:, 3:, halves[1]], td[1][:, 3:])
        quantize_result(stages[0])
        nc.sync.dma_start(out_words[:, halves[0]], o_codes[:, halves[0]])
        cut = last.start + END_SPLIT
        round_result(slice(last.start, cut), nc.vector.tensor_copy)
        round_result(slice(cut, last.stop), nc.scalar.copy)
        quantize_result(stages[1])
        quantize_result(last)
        nc.sync.dma_start(out_words[:, halves[1]], o_codes[:, halves[1]])
        for q in range(4):
            queue = nc.scalar if q % 2 else nc.sync
            queue.dma_start(
                out_2[0, 4 * q : 4 * q + 4, :].bitcast(I32), o_scales[32 * q : 32 * q + 4, :].bitcast(I32)
            )
